import numpy as np, ml_dtypes
CORES = [36,164,52,180,100,228,116,244]
N = 8
BF = ml_dtypes.bfloat16
def gentries(a):
    return np.ascontiguousarray(a.reshape(8, 16, -1).transpose(0, 2, 1)).reshape(8, -1)
def gtable(e):
    e = np.asarray(e); return np.ascontiguousarray(e.reshape(8, -1, 16).transpose(0, 2, 1)).reshape(128, -1).astype(np.int32)
W, V, Q, L, B, RO = 1920, 512, 2, 256, 2, 5
def parts(rng):
    x = rng.integers(0, 16, (N, 8, 16, W)); s = rng.integers(0, 256, (N, 8, 16, W))
    p = rng.integers(0, W, (N, 8, 16, V)); u = rng.integers(0, V, (N, 8, 16, V))
    share = rng.choice(np.array([0.0006, 0.0025, 0.008, 0.025]), (N, 8, 1, 1))
    m = np.where(rng.random((N, 8, 16, V)) < share, rng.integers(8, 16, (N, 8, 16, V)), rng.integers(0, 8, (N, 8, 16, V)))
    h = np.ascontiguousarray(np.argsort(rng.random((N, 8, V)), axis=-1)[..., :B * L])
    c = rng.integers(132, 157, (N, 8, 1)) + rng.integers(0, 8, (N, 8, 16)); t = rng.integers(45, 111, (N, 8, 16, RO))
    return x, s, p, u, m, h, c, t
def pack(x, s, p, u, m, h, c, t):
    def w(a): return np.ascontiguousarray(a.reshape(N, 128, -1))
    return {"xf": w(x).astype(np.float32).astype(BF), "stp": w(s).astype(np.float32).astype(BF), "pl": w(p).astype(np.int32), "su": w(u).astype(np.int32),
            "mk": w(m).astype(np.float32).astype(BF), "hp": np.stack([gtable(a) for a in h]), "cp": w(c).astype(np.int32), "th": w(t).astype(np.int32)}
def setup_inputs(rng):
    return pack(*parts(rng))
def uneven(rng, n, k, e):
    return np.minimum((n * rng.random((N, 8, 16, k)) ** np.exp2(e)).astype(np.int64), n - 1)
def setup_inputs_spread(rng):
    x, s, p, u, m, h, c, t = parts(rng)
    x = uneven(rng, 16, W, rng.integers(-2, 3, (N, 8, 1, W))); s = uneven(rng, 256, W, rng.integers(-2, 3, (N, 8, 1, W)))
    p = uneven(rng, W, V, rng.integers(-2, 3, (N, 8, 1, 1))); u = uneven(rng, V, V, rng.integers(-2, 3, (N, 8, 1, 1)))
    m = np.where(rng.random((N, 8, 16, V)) < rng.choice(np.array([0.0, 0.0, 0.0, 0.0, 0.01, 0.05]), (N, 8, 1, V)), rng.integers(0, 16, (N, 8, 16, V)), 0)
    c = rng.integers(0, 241, (N, 8, 16)); t = rng.integers(1, 241, (N, 8, 16, RO))
    c[:, 1::2] = rng.integers(100, 241, (N, 4, 16)); t[:, 1::2] = rng.integers(100, 241, (N, 4, 16, RO))
    return pack(x, s, p, u, m, h, c, t)
def binary(rng, n):
    k = rng.integers(0, 3, (N, 8, 1, n)); return np.where(k == 2, rng.integers(0, 2, (N, 8, 16, n)), k)
def setup_inputs_ends(rng):
    x, s, p, u, m, h, c, t = parts(rng)
    x = 15 * binary(rng, W); s = 255 * binary(rng, W)
    x[..., 0] = 0; x[..., 1] = 15; x[..., 2] = 15; x[..., W - 1] = 15; x[:, 1:6:2, :, 0] = 15 * rng.integers(0, 2, (N, 3, 16))
    s[..., W - 1] = 255 * rng.integers(0, 2, (N, 8, 16)); s[..., 0] = 255 * rng.integers(0, 2, (N, 8, 16))
    k = rng.integers(0, 10, (N, 8, 1, V)); z = rng.random((N, 8, 16, V))
    p = np.where(k < 2, 0, np.where(k < 4, W - 1, np.where(z < 0.35, 0, np.where(z < 0.7, W - 1, p))))
    p[..., 0] = 0; p[..., V - Q:] = W - 1
    k = rng.integers(0, 10, (N, 8, 1, V)); z = rng.random((N, 8, 16, V))
    u = np.where(k < 4, 0, np.where(k < 6, V - 1, np.where(z < 0.25, 0, np.where(z < 0.5, V - 1, u))))
    m = 15 * ((rng.random((N, 8, 1, V)) < 0.03) | (rng.random((N, 8, 16, V)) < 0.004)).astype(np.int64)
    m[..., 0] = 0; m[..., V - 1] = 15 * rng.integers(0, 2, (N, 8, 16)); m[N - 1, 7, :, V - 1] = 15
    e = np.stack([np.arange(V // 2), V - 1 - np.arange(V // 2)], axis=1).reshape(-1)[:B * L]
    h[:, (0, 2, 6)] = e; h[:, (1, 3, 7)] = e[::-1]
    k = np.stack([rng.permutation(np.array([0, 0, 0, 1, 1, 2, 2, 2])) for r in range(N)])[:, :, None]
    c = 240 * np.where(k == 2, rng.integers(0, 2, (N, 8, 16)), k); c[N - 1, 7] = 0
    t = np.where(rng.random((N, 8, 16, RO)) < 0.25, 1, 240)
    return pack(x, s, p, u, m, h, c, t)
def setup_inputs_corners(rng):
    x, s, p, u, m, h, c, t = parts(rng)
    near = rng.random((N, 8, 16, V)) < 0.25; p = np.where(near, W - 1 - rng.integers(0, 256, (N, 8, 16, V)), p)
    a = W - np.arange(W - 255, W); s[..., W - 255:] = np.minimum(a + rng.integers(-1, 2, (N, 8, 16, 255)), 255)
    x[:, ::2] = 7 + (np.arange(W) & 1)
    odd = (rng.random((N, 4, 16, V)) < rng.random((N, 4, 1, V))).astype(np.int64); p[:, ::2] = (p[:, ::2] >> 1) * 2 + odd
    c[:, ::2] = 112 + rng.integers(4, 13, (N, 4, 16)); t[:, ::2] = rng.integers(7, 9, (N, 4, 16, RO)) * rng.integers(6, 17, (N, 4, 16, RO)) + rng.integers(0, 2, (N, 4, 16, RO))
    m = rng.choice(np.array([0, 3, 4, 7, 8, 11, 12, 15]), (N, 8, 16, V), p=np.array([0.3, 0.15, 0.15, 0.308, 0.04, 0.05, 0.001, 0.001]))
    v = np.arange(V)
    for r in range(N):
        o = rng.permutation(8)
        m[r, o[0]] = 15; m[r, o[1]] = 0
        m[r, o[2]] = np.where(rng.random((16, V)) < 0.002, rng.integers(11, 13, (16, V)), 7)
        o = rng.permutation(8)
        u[r, o[0]] = v; u[r, o[1]] = (v + V - 1) % V; u[r, o[2]] = rng.choice(np.array([0, V - 1]), (16, V)); u[r, o[3]] = (v + 1) % V
        p[r, o[4]] = p[r, o[4], :1]
    return pack(x, s, p, u, m, h, c, t)
def setup_inputs_crowd(rng):
    x, s, p, u, m, h, c, t = parts(rng)
    for r in range(N):
        o = rng.permutation(8)
        for i in range(6):
            g = o[i]; lone = Q * int(rng.choice(np.array([0, L // 2, L - 1]))) + np.arange(Q)
            w = rng.permutation(np.setdiff1d(np.arange(V), lone)); hot = w[:16]
            m[r, g] = 0
            if i < 4: c[r, g] = 240
            if i in (0, 1, 3): m[r, g, np.arange(16), hot] = 15
            if i < 2: u[r, g] = hot[:, None]
            if i == 1: u[r, g][:, lone] = lone
            if i == 2: u[r, g] = V - 1
            if i == 3: u[r, g] = w[16]; u[r, g][:, lone] = hot[:, None]
            if i >= 4:
                p[r, g] = W - 1; x[r, g, :, W - 1] = 15; x[r, g, :, 0] = 0
                c[r, g] = rng.integers(229, 237, 16); t[r, g] = rng.integers(1, 121, (16, RO)); u[r, g] = V - 1
            if i == 5: p[r, g][:, lone] = 0; u[r, g] = np.arange(V)
    return pack(x, s, p, u, m, h, c, t)
def setup_inputs_tides(rng):
    x, s, p, u, m, h, c, t = parts(rng); x = np.minimum(x, 14); q = rng.permutation(N); a, b, e = int(q[0]), int(q[1]), int(q[2]); v = np.arange(V)
    for g in range(8):
        o = rng.permutation(16)[:RO]
        m[:, g, o] = m[:, g, o] & 7; t[:, g, o] = 240
        for r in (a, e):
            m[r, g] = m[r, g] & 7; u[r, g] = Q * rng.integers(0, L, (16, V)) + v % Q
        x[a, g] = np.maximum(x[a, g], 1); c[a, g, ::2] = rng.integers(0, 9, 8); t[a, g, o, np.arange(RO)] = rng.integers(1, 9, RO)
        k = rng.integers(0, 12, (16, V)); k[o] = k[o] & 7; m[b, g] = k
        c[b, g] = 240; t[b, g] = rng.integers(1, 241, (16, RO))
        c[e, g] = rng.integers(116, 141, 16); t[e, g] = 240
        even = np.arange(0, RO, 2); t[e, g, o[even], even] = rng.integers(24, 57, len(even))
    return pack(x, s, p, u, m, h, c, t)
def check_inputs(d):
    bad = []
    for k, lo, hi in (("xf", 0, 15), ("stp", 0, 255), ("pl", 0, W - 1), ("su", 0, V - 1), ("mk", 0, 15), ("hp", 0, V - 1), ("cp", 0, 240), ("th", 1, 240)):
        v = np.asarray(d[k]).astype(np.float64)
        if not np.all((v >= lo) & (v <= hi)): bad.append("range of " + k)
        elif not np.all(v == np.floor(v)): bad.append("whole numbers in " + k)
    e = np.sort(np.stack([gentries(a) for a in d["hp"]]), axis=-1)
    if np.any(e[..., 1:] == e[..., :-1]): bad.append("repeats in hp")
    return bad
def pick(a, ix):
    return np.stack([np.stack([np.take(a[r, g], ix[r, g], axis=1) for g in range(8)]) for r in range(N)])
def reference(xf, stp, pl, su, mk, hp, cp, th):
    x = xf.astype(np.float32).astype(np.int32).reshape(N, 8, 16, W); s = stp.astype(np.float32).astype(np.int32).reshape(N, 8, 16, W)
    p = pl.astype(np.int32).reshape(N, 8, 16, V); nx = su.astype(np.int32).reshape(N, 8, 16, V); m = mk.astype(np.float32).astype(np.int32).reshape(N, 8, 16, V)
    h = np.stack([gentries(a) for a in hp]).astype(np.int32).reshape(N, 8, B, L); cap = cp.astype(np.int32).reshape(N, 8, 16, 1); theta = th.astype(np.int32).reshape(N, 8, 16, RO)
    wt = (2 * np.arange(16, dtype=np.int32) + 1).reshape(1, 1, 16, 1); A = np.zeros((N, 8, 1, 1), np.int32)
    for t in range(RO):
        lanes = slice(t % Q, V, Q)
        old = m[..., lanes].copy(); at = p[..., lanes].copy()
        climb = np.max(pick(m, nx[..., lanes].reshape(N, 8, 16 * L)).reshape(N, 8, 16, 16, L), axis=3)
        new = np.maximum(old, climb - 4)
        ix = at.reshape(N, 8, 16 * L)
        xk = pick(x, ix).reshape(N, 8, 16, 16, L)
        S = np.add.reduce(xk, axis=3)
        over = S > cap + (A & 7)
        load = np.add.reduce(np.where(over[:, :, :, None, :], xk, 0), axis=2)
        new = np.where(load >= theta[..., t:t + 1], 15, new)
        opened = np.any((new >= 8) & (old < 8), axis=2)
        u = np.add.reduce(wt * S, axis=2)
        move = np.where(new >= 8, np.maximum(u & 15, 1)[:, :, None, :], 0)
        sk = pick(s, ix).reshape(N, 8, 16, 16, L)
        child = at + np.take_along_axis(sk, move[:, :, None], axis=2)[:, :, 0]
        child = np.where(child >= W, child - W, child)
        c = np.take_along_axis(h, ((u >> 4) & (B - 1))[:, :, None], axis=2)[:, :, 0]
        A = np.add.reduce(opened.astype(np.int32), axis=2).reshape(N, 8, 1, 1)
        m[..., lanes] = new
        back = np.zeros((N, 8, 16, L), np.int32)
        for r in range(N):
            d = (r + 1 + t % (N - 1)) % N
            for g in range(8):
                i = np.flatnonzero(opened[r, g]); cc = c[r, g, i]
                back[r, g][:, i] = m[d, g][:, cc]
                p[d, g][:, cc] = child[r, g][:, i]; m[d, g][:, cc] = 0
        now = m[..., lanes]
        m[..., lanes] = np.where(opened[:, :, None, :], np.maximum(now, back - 4), now)
    return {"ypl": p.reshape(N, 128, V).astype(np.float32), "ymk": m.reshape(N, 128, V).astype(np.float32).astype(BF)}

@@ -1,0 +1,562 @@
+import math
+import numpy as np
+from concourse.mybir import AluOpType as A, ActivationFunctionType as F
+
+W, V, L, RO = 1920, 512, 256, 5
+F32, BF, F16, I32, U16 = "float32", "bfloat16", "float16", "int32", "uint16"
+
+
+def _s(n, d):
+    return ("sbuf", [128, n], d)
+
+
+SCRATCH = {
+    "xw": _s(W, BF), "sw": _s(W, BF), "pli": _s(V, I32), "sui": _s(V, I32), "mki": _s(V, BF),
+    "hpi": _s(32, I32), "cpi": _s(8, I32), "thi": _s(8, I32),
+    "io5": _s(V, F32), "io16": _s(480, F16), "iob": _s(128, F32), "pcol": _s(8, I32), "ci": _s(8, I32), "cf": _s(16, F32),
+    "wi": _s(128, BF), "wim": _s(128, BF), "wbp": _s(128, BF), "wbn": _s(128, BF), "wu": _s(128, BF), "whi": _s(128, BF),
+    "wold": _s(128, BF), "bsum": _s(144, BF), "b0": _s(144, BF), "bd": _s(144, BF), "b0f": _s(144, F32),
+    "capf": _s(8, F32), "thf": _s(8, F32), "thr": _s(8, F32), "ai": _s(8, I32), "af": _s(8, F32), "acc": _s(8, F32),
+    "glist": _s(16, U16), "hpu": _s(32, U16), "invl": _s(32, U16), "invi": _s(64, I32), "lanel": _s(32, U16),
+    "suu": _s(V, U16), "offn": _s(L, U16), "offa": _s(L, U16), "inv": _s(V, F32), "dt": _s(W, F32), "wk": _s(L, F32),
+    "sg": _s(288, F32), "so": _s(L, F16), "s1": _s(L, F16), "s2": _s(L, F16), "lv": _s(V, BF),
+    "tw": _s(544, F32), "xg": _s(4096, BF), "mg": _s(4096, BF), "zg": _s(4096, F16), "yy": _s(4096, BF),
+    "ox": _s(V, BF), "yp": _s(2048, F16), "vi": _s(L, I32), "va": _s(L, I32), "bpair": _s(144, BF), "ones": _s(L, BF),
+    "wc": _s(128, BF), "wi256": _s(128, BF), "wm2k": _s(128, BF), "wneg": _s(128, BF),
+    "sb": _s(L, BF), "ov": _s(V, BF), "ow": _s(V, BF), "ui": _s(L, I32), "jj": _s(L, I32), "bi": _s(L, I32), "oh": _s(L, BF), "bfl": _s(L, BF),
+    "hot": _s(L, BF), "n1": _s(L, BF), "hi": _s(L, BF), "hio": _s(L, BF),
+    "tt": _s(L, F32), "ch": _s(L, F32), "ms": _s(V, F16), "sgn": _s(V, BF), "kb": _s(V, BF), "ks": _s(V, BF),
+    "sel": _s(V, BF), "bm": _s(V, BF), "bmx": _s(L, BF),
+    "lm": _s(RO * V, F16), "lb": _s(RO * V, BF), "lk": _s(RO * V, BF),
+    "da": _s(1536, BF), "db": _s(768, BF), "la": _s(1536, F32), "ls": _s(768, F32), "d1": _s(768, BF),
+    "d2": _s(768, BF), "om": _s(V, BF), "op": _s(V, F32), "fe": _s(V, F16),
+}
+for _k in range(8):
+    SCRATCH["ps%d" % _k] = ("psum", [128, 512], F32)
+
+LOADS = ["hp", "pl", "xf", "mk", "su", "cp", "th", "stp"]
+SEMAPHORES = (["cv", "cs", "cp_", "cg", "sb_", "sn", "so", "sk", "o1", "o2"] + ["l" + n for n in LOADS]
+              + ["a%s%d" % (k, t) for k in "bnok" for t in range(RO)])
+
+E15 = 2.0 ** 97
+DOWN = 2.0 ** -52
+LN2 = math.log(2.0)
+XS = [("s", 0, 64), ("v", 160, 96), ("s", 64, 64), ("s", 128, 32)]
+XS0 = [("s", 0, 64), ("s", 64, 64), ("v", 192, 64), ("s", 128, 64)]
+NP = 0
+U = 2.0 ** -11
+TILE_BANKS = [2, 3, 1]
+TE, OVE, SBE = "sss", "v", "v"
+TAB = [6, 7, 6, 7]
+MN = 8
+MS0, MS = "ssssssss", "vsssssss"
+YS0, YS = "vvvvssss", "vsssssss"
+LOAD_ORDER = [("s", "hpi", "hp", 2.1), ("y", "mki", "mk", 2.8), ("y", "pli", "pl", 4.0), ("y", "xw", "xf", 6.3),
+              ("y", "sui", "su", 7.6), ("y", "sw", "stp", 9.9), ("s", "cpi", "cp", 2.8), ("s", "thi", "th", 2.8)]
+FIX, CYC, PE, LAT, SLACK, G = 0.06, 0.00083, 0.00042, 0.08, 0.1, 1.56
+T_SMALL, T_BIG = 2.8, 3.6
+SEED, TRIES, CACHE = 1, 4000, {}
+SHIFTS = {}
+COST = {"sg": 512, "offn": 256, "tw": 272, "offa": 256 * G, "sb": 256, "ov": 128, "ui": 256, "jj": 256, "bi": 256, "oh": 256,
+        "bfl": 256, "hot": 256, "n1": 256, "lv": 256, "hi": 128, "tt": 256, "ch": 256, "ms": 256 * G, "bm": 512 * G, "s1": 256,
+        "s2": 256, "so": 512, "bmx": 256, "yy": 512, "mg": 4096 * G / MN, "hio": 256, "sgn": 256, "ks": 512 * G, "ow": 128, "ox": 128, "yp": 512, "vi": 256, "va": 256,
+        "wneg": 128, "sov": 256, "shi": 256, "ssel": 512 * G, "vbm": 512, "ones": 128, "wi256": 128, "wm2k": 128,
+        "sel": 512, "dt": 480, "wk": 256, "zg": 256 * G, "inv": 1900, "io16": 480, "io5": 1200, "iob": 400, "suu": 256,
+        "wi": 128, "wim": 128, "wbp": 128, "wbn": 128, "wu": 128, "whi": 128, "wold": 128, "da": 128, "db": 128, "la": 256, "lt": 2000,
+        "lbb": 256, "ls": 512, "dd": 256, "de": 128, "om": 256, "op": 256, "fe": 256, "enc": 2200}
+
+
+def rank_program(g, core, T, topo):
+    rank = T.rank_of(core)
+    if rank is None:
+        return
+    N = len(T.cores)
+    Q = {"v": g.vector, "s": g.scalar, "p": g.tensor, "g": g, "y": g.sync}
+    SEM = {"v": "cv", "s": "cs", "p": "cp_", "g": "cg"}
+    cnt = {}
+    known = {q: {} for q in Q}
+    writer, readers = {}, {}
+
+    def wait(q, tok):
+        sem, n, clock = tok
+        if q == "p" and sem == "cp_":
+            return
+        if known[q].get(sem, 0) >= n:
+            return
+        assert n <= cnt.get(sem, n)
+        Q[q].wait_ge(T.sem[sem], n)
+        known[q][sem] = n
+        for s2, n2 in clock.items():
+            if known[q].get(s2, 0) < n2:
+                known[q][s2] = n2
+
+    rnd, seen, kinds = [0], {}, []
+    ops = []
+
+    def record(q, kind, what, r, w, busy, done):
+        deps = set(writer[k] for k in r if k in writer)
+        for k in w:
+            if k in writer:
+                deps.add(writer[k])
+            deps.update(readers.get(k, []))
+        me = len(ops)
+        c = "%s%s%s" % ("z" if rnd[0] == 0 else "", q, w[0].rstrip("0123456789") if w else "")
+        seen[(rnd[0], c)] = seen.get((rnd[0], c), -1) + 1
+        kinds.append("%s%d" % (c, seen[(rnd[0], c)]))
+        ops.append((q, kind, what, busy, done, sorted(deps)))
+        for k in r:
+            readers.setdefault(k, []).append(me)
+        for k in w:
+            writer[k] = me
+            readers[k] = []
+        return me
+
+    def schedule():
+        n = len(ops)
+        after = [[] for _ in range(n)]
+        for i, o in enumerate(ops):
+            for d in o[5]:
+                after[d].append(i)
+
+        def gap(d, i):
+            both = ops[d][0] == ops[i][0] and (ops[d][0] == "p" or ops[d][1] == ops[i][1] == "dma")
+            return ops[d][3] if both else ops[d][4]
+
+        level = [0.0] * n
+        for i in range(n - 1, -1, -1):
+            level[i] = max([gap(i, j) + level[j] for j in after[i]] + [ops[i][4]])
+        edges = [[(j, gap(i, j)) for j in after[i]] for i in range(n)]
+
+        def place(prio):
+            left = [len(o[5]) for o in ops]
+            est, start = [0.0] * n, [0.0] * n
+            ready = [i for i in range(n) if left[i] == 0]
+            busy = {q: [] for q in Q}
+            while ready:
+                i = max(ready, key=lambda k: prio[k])
+                ready.remove(i)
+                q, s, d = ops[i][0], est[i], ops[i][3]
+                if q is not None:
+                    iv = busy[q]
+                    k = len(iv)
+                    while k > 0 and iv[k - 1][1] > s:
+                        k -= 1
+                    while k < len(iv) and iv[k][0] < s + d - 1e-9:
+                        s = max(s, iv[k][1])
+                        k += 1
+                    iv.insert(k, (s, s + d))
+                start[i] = s
+                for j, e in edges[i]:
+                    if est[j] < s + e:
+                        est[j] = s + e
+                    left[j] -= 1
+                    if left[j] == 0:
+                        ready.append(j)
+            return max(start[i] + ops[i][4] for i in range(n)), start
+
+        if "seq" not in CACHE:
+            rng = np.random.default_rng(SEED)
+            names = sorted(set(kinds))
+            members = [[i for i in range(n) if kinds[i] == c] for c in names]
+            prio = [level[i] + SHIFTS.get(kinds[i], 0.0) for i in range(n)]
+            best, start = place(prio)
+            now, moved = best, dict(SHIFTS)
+            for it in range(TRIES):
+                trial, step = list(prio), {}
+                for c in rng.integers(0, len(names), int(rng.integers(1, 5))):
+                    d = round(float(rng.normal(0.0, 2.0)), 1)
+                    step[names[int(c)]] = step.get(names[int(c)], 0.0) + d
+                    for i in members[int(c)]:
+                        trial[i] += d
+                t2, s2 = place(trial)
+                if t2 <= now + 0.3 * (1.0 - it / TRIES) * float(rng.random()):
+                    now, prio = t2, trial
+                    for c, d in step.items():
+                        moved[c] = round(moved.get(c, 0.0) + d, 1)
+                    if t2 < best:
+                        best, start = t2, s2
+                        CACHE["shifts"] = dict(moved)
+            CACHE["seq"] = sorted(range(n), key=lambda i: (start[i], i))
+            CACHE["time"] = best
+        return CACHE["seq"], after
+
+    def emit():
+        seq, after = schedule()
+        tok = {}
+        for i in seq:
+            q, kind, what, busy, done, deps = ops[i]
+            if kind == "arrival":
+                tok[i] = what + ({},)
+                continue
+            best = {}
+            for d in deps:
+                tk = None if kind == ops[d][1] == "dma" else tok[d]
+                if tk is not None and (tk[0] not in best or best[tk[0]][1] < tk[1]):
+                    best[tk[0]] = tk
+            for tk in best.values():
+                wait(q, tk)
+            if kind == "op":
+                ins = what()
+                if q == "p" and all(ops[j][0] == "p" for j in after[i]):
+                    tok[i] = None
+                    continue
+                sem, n = SEM[q], 1
+                ins.then_inc(T.sem[sem], 1)
+            elif kind == "dma":
+                sem, n = what[2], 16
+                Q[q].dma_start(what[0], what[1]).then_inc(T.sem[sem], 16)
+            else:
+                sem, n = what[1], what[2]
+                what[0]()
+            cnt[sem] = cnt.get(sem, 0) + n
+            tok[i] = (sem, cnt[sem], dict(known[q]))
+
+    def op(q, call, r, w, cost=None):
+        if cost is None:
+            cost = FIX + CYC * COST.get(q + w[0].rstrip("0123456789"), COST.get(w[0], COST.get(w[0].rstrip("0123456789"), 64)))
+        record(q, "op", call, r, w, cost, cost + LAT)
+
+    def dma(q, out, in_, sem, r, w, done=2.5):
+        record(q, "dma", (out, in_, sem), r, w, 0.1, done)
+
+    def ts(out, in0, s1, s2, o0, o1, r, w):
+        if o1 is None:
+            op("v", lambda: g.vector.tensor_scalar(out, in0, s1, None, o0), r, w)
+        else:
+            op("v", lambda: g.vector.tensor_scalar(out, in0, s1, s2, o0, o1), r, w)
+
+    def tt(out, in0, in1, o, r, w):
+        op("v", lambda: g.vector.tensor_tensor(out, in0, in1, o), r, w)
+
+    def cpy(out, in_, r, w):
+        op("v", lambda: g.vector.tensor_copy(out, in_), r, w)
+
+    def fill(ap, c, w):
+        op("v", lambda: g.vector.memset(ap, c), [], w)
+
+    def act(out, in_, f, r, w, bias=0.0, scale=1.0, acc=None):
+        op("s", lambda: g.scalar.activation(out, in_, f, bias=bias, scale=scale, accum_out=acc), r, w)
+
+    def mm(out, lhsT, rhs, start, stop, r, w, n=L):
+        op("p", lambda: g.tensor.matmul(out, lhsT, rhs, start, stop), r, w, PE * n)
+
+    def mms(out, pairs, r, w, n):
+        def call():
+            return [g.tensor.matmul(out, a, b, k == 0, k == len(pairs) - 1) for k, (a, b) in enumerate(pairs)][-1]
+        op("p", call, r, w, PE * n * len(pairs))
+
+    def send(shift, out, in_, arr, loc, r, key, done):
+        dst, src = T.cores[(rank + shift) % N], T.cores[(rank - shift) % N]
+        rid, pid = topo.addr(dst, core)
+        record("g", "send", (lambda: g.remote_dma(out, in_, T.sem[arr], T.sem[loc], pid, rid, topo.mask(core, dst)), loc,
+                             len(topo.engines(core, dst))), r, ["sent" + key], 0.3, done)
+        record(None, "arrival", (arr, len(topo.engines(src, core))), ["sent" + key], [key], 0.0, LAT)
+
+    ps = [T["ps%d" % k] for k in range(8)]
+    cf, ci = T.cf, T.ci
+    sgl = T.sg[:, 16:272]
+
+    for qq, name, src, done in LOAD_ORDER:
+        wide = {"cpi": 1, "thi": 5}.get(name)
+        dma(qq, T[name][:, 0:wide] if wide else T[name][:], T[src][:], "l" + src, [], [name, "load" + qq], done)
+
+    op("g", lambda: g.iota(T.pcol[:, 0:1], [[0, 1]], 0, 1), [], ["pcol"])
+    op("g", lambda: g.iota(T.io5[:], [[1, V]], 0, 0, allow_small_or_imprecise_dtypes=True), [], ["io5"])
+    op("g", lambda: g.iota(T.iob[:], [[1, 8], [0, 16]], 0, 0, allow_small_or_imprecise_dtypes=True), [], ["iob"])
+    fill(T.b0f[:], 0.0, ["b0f"])
+    fill(T.b0[:], 0.0, ["b0"])
+    fill(T.bd[:], 0.0, ["bd"])
+    fill(T.sg[:, 0:16], 1.0, ["pada"])
+    fill(T.sg[:, 272:288], 1.0, ["padb"])
+    g8 = T.io5[:, 0:8]
+    ts(ci[:, 0:1], T.pcol[:, 0:1], 15, None, A.bitwise_and, None, ["pcol"], ["ci0"])
+    ts(ci[:, 1:2], T.pcol[:, 0:1], 4, None, A.logical_shift_right, None, ["pcol"], ["ci1"])
+    cpy(cf[:, 0:1], T.pcol[:, 0:1], ["pcol"], ["cf0"])
+    cpy(cf[:, 1:3], ci[:, 0:2], ["ci0", "ci1"], ["cf1"])
+    tt(ci[:, 2:3], ci[:, 0:1], ci[:, 1:2], A.add, ["ci0", "ci1"], ["ci2"])
+    ts(cf[:, 3:4], cf[:, 1:2], 0.0, None, A.is_equal, None, ["cf1"], ["cf3"])
+    ts(ci[:, 3:4], ci[:, 2:3], 1, None, A.bitwise_and, None, ["ci2"], ["ci3"])
+    ts(cf[:, 6:7], cf[:, 1:2], 2.0, 1.0, A.mult, A.add, ["cf1"], ["cf6"])
+    ts(T.b0f[:, 15:143:16], g8, cf[:, 2:3], cf[:, 3:4], A.is_equal, A.mult, ["io5", "cf1", "cf3"], ["b0f"])
+    ts(T.wi[:], T.io5[:, 0:128], cf[:, 0:1], None, A.is_equal, None, ["io5", "cf0"], ["wi"])
+    ts(cf[:, 4:5], cf[:, 3:4], 99.0, 1.0, A.mult, A.add, ["cf3"], ["cf4"])
+    ts(cf[:, 7:8], cf[:, 3:4], -1.0, 0.5, A.mult, A.add, ["cf3"], ["cf7"])
+    ts(cf[:, 8:9], ci[:, 3:4], 17.0, cf[:, 1:2], A.mult, A.add, ["ci3", "cf1"], ["cf8"])
+    cpy(T.hpu[:], T.hpi[:], ["hpi"], ["hpu"])
+    ts(cf[:, 9:10], cf[:, 8:9], 16.0, None, A.mult, None, ["cf8"], ["cf9"])
+    fill(T.inv[:], 0.0, ["inv"])
+    op("v", lambda: g.vector.tensor_copy(T.inv[:, 0:V].indirect(T.hpu[:, 0:32]), T.io5[:]), ["hpu", "io5"], ["inv"])
+    for q in range(2):
+        mms(ps[1][:, 16 * q:16 * q + 16], [(T.b0f[:, 15 - rho:143 - rho], T.inv[:, 2 * rho + q:V:32]) for rho in range(16)],
+            ["b0f", "inv"], ["B1"], 256)
+    cpy(T.offn[:], T.pli[:, 0:V:2], ["pli"], ["offn"])
+    ts(sgl, T.pli[:, 0:V:2], 1.0, U, A.add, A.mult, ["pli"], ["sg"])
+    act(T.lv[:], T.mki[:], F.Exp, ["mki"], ["enc", "lv0", "lv1"], bias=-98.0 * LN2, scale=13.0 * LN2)
+    ts(T.glist[:], T.io5[:, 0:16], cf[:, 9:10], None, A.add, None, ["io5", "cf9"], ["glist"])
+    cpy(T.io16[:], T.io5[:, 0:480], ["io5"], ["io16"])
+    for name, c in (("wim", DOWN), ("wneg", -1.0), ("wbp", 16384.0), ("wbn", -16384.0)):
+        act(T[name][:], T.wi[:], F.Identity, ["wi"], [name], scale=c)
+    tt(cf[:, 5:6], cf[:, 1:2], cf[:, 4:5], A.max, ["cf1", "cf4"], ["cf5"])
+    ts(T.wu[:], T.iob[:], cf[:, 2:3], cf[:, 6:7], A.is_equal, A.mult, ["iob", "cf1", "cf6"], ["wu"])
+
+    def agent_lists():
+        op("v", lambda: g.vector.transpose(T.tw[:, 0:256], sgl), ["sg"], ["tw1"])
+        op("v", lambda: g.vector.transpose(T.tw[:, 256:544], T.sg[:, 0:288]), ["sg", "pada", "padb"], ["tw2"])
+
+    def agent_lists2():
+        ts(T.offa[:], T.tw[:, 0:544].indirect(T.glist[:, 0:16]), 1.0 / U, -1.0, A.mult, A.add, ["tw1", "tw2", "glist"], ["offa"])
+
+    def xgather(k, spec):
+        e, a, n = spec
+        o, w = T.xg[:, 16 * a:16 * (a + n)], T.xw[:, 0:W].indirect(T.offn[:, a:a + n])
+        gather(e, o, w, ["xw", "offn"], ["xg%d" % k], 16 * n)
+
+    def gather(e, o, w, r, wr, n):
+        if e == "s":
+            op("s", lambda: g.scalar.activation(o, w, F.Identity), r, wr, FIX + CYC * G * n)
+        else:
+            op("v", lambda: g.vector.tensor_copy(o, w), r, wr, FIX + CYC * G * n)
+
+    def s_mm(k, spec):
+        e, a0, n = spec
+        mms(ps[0][:, a0:a0 + n], [(T.wi[:], T.xg[:, 16 * a0 + a:16 * (a0 + n):16]) for a in range(16)], ["wi", "xg%d" % k], ["B0"],
+            max(n, 64))
+
+    def climb(q, engines):
+        n = L // MN
+        for k in range(MN):
+            o = L * q + n * k
+            gather(engines[k], T.mg[:, 16 * n * k:16 * n * (k + 1)], T.lv[:, 0:V].indirect(T.suu[:, o:o + n]),
+                   ["lv0", "lv1", "suu%d" % q], ["mg%d" % k], 16 * n)
+        for k in range(4):
+            mms(ps[5][:, 64 * k:64 * k + 64], [(T.wim[:], T.mg[:, 1024 * k + a:1024 * k + 1024:16]) for a in range(16)],
+                ["wim"] + ["mg%d" % j for j in range(k * MN // 4, (k + 1) * MN // 4)], ["B5"], 64)
+
+    def masked(engines, nx):
+        xk = ["xg%d" % k for k in range(nx)]
+        nb = 0
+        for i in range(NP // 2):
+            b = TILE_BANKS[nb % len(TILE_BANKS)]
+            nb += 1
+            for e in range(2):
+                a = 2 * i + 8 * e
+                mms(ps[b][:, L * e:L * e + L], [(T.wm2k[:], T.ones[:]), (T.wi[:], T.xg[:, a:4096:16]), (T.wi256[:], T.xg[:, a + 1:4096:16])],
+                    ["wm2k", "ones", "wi", "wi256"] + xk, ["B%d" % b], L)
+            tt(T.yp[:, V * i:V * i + V], ps[b][:], T.ox[:], A.mult, ["B%d" % b, "ox0", "ox1"], ["yp%d" % i])
+        steps = []
+        if NP:
+            steps.append((T.wc[:], T.ox[:, 0:L], ["wc", "ox0"]))
+        for i in range(NP // 2):
+            for e in range(2):
+                a = 2 * i + 8 * e
+                steps.append((T.bpair[:, 14 - a:142 - a], T.yp[:, V * i + L * e:V * i + L * e + L], ["bpair", "yp%d" % i]))
+        for j in range(NP, 8):
+            y = T.yy[:, V * j:V * j + V]
+            if engines[j] == "s":
+                b = TILE_BANKS[nb % len(TILE_BANKS)]
+                nb += 1
+                mm(ps[b][:], T.wi[:], T.xg[:, j:4096:8], True, False, ["wi"] + xk, ["B%d" % b], V)
+                mm(ps[b][:], T.wneg[:], T.ov[:], False, True, ["wneg", "ov0", "ov1"], ["B%d" % b], V)
+                act(y, ps[b][:], F.Relu, ["B%d" % b], ["yy%d" % j])
+            else:
+                tt(y, T.xg[:, j:4096:8], T.ow[:], A.mult, xk + ["ow0", "ow1"], ["yy%d" % j])
+            for e in range(2):
+                a = j + 8 * e
+                steps.append((T.bsum[:, 15 - a:143 - a], T.yy[:, V * j + e:V * j + V:2], ["bsum", "yy%d" % j]))
+        for k, (w, y, r) in enumerate(steps):
+            mm(ps[4][:, 0:L], w, y, k == 0, k == len(steps) - 1, r, ["B4"])
+
+    def sgather(a):
+        tt(T.zg[:, 256 * a:256 * a + 256], T.dt[:, 0:W].indirect(T.offa[:, 16 * a:16 * a + 16]), T.oh[:], A.mult,
+           ["dt0", "dt1", "dt2", "dt3", "offa", "oh"], ["zg%d" % a])
+
+    def d_mm(a):
+        z = T.zg[:, 256 * a:256 * a + 256]
+        mm(ps[6][:, 0:L], T.b0[:, 15 - a:143 - a], z, a == 0, a == 15, ["b0", "zg%d" % a], ["B6"])
+        mm(ps[7][:, 0:L], T.bd[:, 15 - a:143 - a], z, a == 0, a == 15, ["bd", "zg%d" % a], ["B7"])
+
+    def children(par, part, t, shift):
+        tt(T.ms[:, L * part:L * part + L], T.ch[:, 0:L].indirect(T.lanel[:, 16 * par:16 * par + 16]), T.ks[:, L * par:L * par + L],
+           A.subtract, ["ch", "lanel", "ks"], ["ms%d" % part])
+        o = V * t + L * part
+        send(shift, T.lm[:, o:o + L], T.ms[:, L * part:L * part + L], "a%s%d" % ("no"[part], t),
+             ("sn", "so")[part], ["ms%d" % part], "lm%d%d" % (t, part), T_SMALL)
+
+    def decode(k, src, key):
+        c, c2 = slice(L * k, L * k + L), slice(V * k, V * k + V)
+        ts(T.da[:, V * k:V * k + L], src, 1.0, 2.0 ** -49, A.max, A.mult, [key], ["da%d" % k])
+        ts(T.db[:, c], src, 1.0, 2.0 ** -98, A.min, A.max, [key], ["db%d" % k])
+        act(T.la[:, V * k:V * k + L], T.da[:, V * k:V * k + L], F.Ln, ["da%d" % k], ["lt" if k == 0 else "la%d" % k, "ln"])
+        act(T.la[:, V * k + L:V * k + V], T.db[:, c], F.Ln, ["db%d" % k], ["lbb%d" % k, "ln"], scale=2.0 ** 49)
+        tt(T.ls[:, c], T.la[:, V * k:V * k + L], T.la[:, V * k + L:V * k + V], A.add,
+           ["lt" if k == 0 else "la%d" % k, "lbb%d" % k], ["ls%d" % k])
+        ts(T.d1[:, c], T.ls[:, c], 1.0 / (13.0 * LN2), 160.0 + 92.0 / 13.0, A.mult, A.add, ["ls%d" % k], ["dd%d" % k])
+        ts(T.d2[:, c], T.d1[:, c], -160.0, None, A.add, None, ["dd%d" % k], ["de%d" % k])
+
+    def keep(t, par):
+        return T.lk[:, V * t + L * par:V * t + L * par + L]
+
+    def lm(t, part):
+        return T.lm[:, V * t + L * part:V * t + L * part + L]
+
+    for t in range(RO):
+        q = t % 2
+        lanes = T.lv[:, q:V:2]
+        other = T.lv[:, 1 - q:V:2]
+        lq, lo = "lv%d" % q, "lv%d" % (1 - q)
+        shift = 1 + t % (N - 1)
+        xs = XS0 if t == 0 else XS
+        ys = YS0 if t == 0 else YS
+        rnd[0] = t
+        if t > 0:
+            tt(sgl, T.s2[:], lm(t - 1, 0), A.max, ["s2", "lm%d0" % (t - 1)], ["sg"])
+            ts(T.offn[:], sgl, 1.0 / U, -1.0, A.mult, A.add, ["sg"], ["offn"])
+        for k, spec in enumerate(xs):
+            if spec[0] == "s":
+                xgather(k, spec)
+        agent_lists()
+        if t == 0:
+            cpy(T.thr[:, 0:1], T.cpi[:, 0:1], ["cpi"], ["thr"])
+            for k in range(4):
+                b = TAB[k]
+                mm(ps[b][:, 0:480], T.wi[:], T.sw[:, 480 * k:480 * k + 480], True, False, ["wi", "sw"], ["B%d" % b], 480)
+                mm(ps[b][:, 0:480], T.wi[:], T.io16[:], False, True, ["wi", "io16"], ["B%d" % b], 480)
+                if k == 3:
+                    ts(T.dt[:, 1440:W], ps[b][:, 0:480], 1441.0, U, A.add, A.mult, ["B%d" % b], ["dt3"])
+                elif TE[k] == "v":
+                    ts(T.dt[:, 480 * k:480 * k + 480], ps[b][:, 0:480], 480.0 * k + 1.0, U, A.add, A.mult, ["B%d" % b], ["dt%d" % k])
+                else:
+                    act(T.dt[:, 480 * k:480 * k + 480], ps[b][:, 0:480], F.Identity, ["B%d" % b], ["dt%d" % k],
+                        bias=(480.0 * k + 1.0) * U, scale=U)
+        agent_lists2()
+        if t == 0:
+            if NP < 8:
+                fill(T.bsum[:], 0.0, ["bsum"])
+                ts(T.bsum[:, 15:143:16], g8, cf[:, 2:3], 256.0, A.is_equal, A.mult, ["io5", "cf1"], ["bsum"])
+            if NP:
+                fill(T.bpair[:], 0.0, ["bpair"])
+                fill(T.ones[:], 1.0, ["ones"])
+                ts(T.bpair[:, 14:142:16], g8, cf[:, 2:3], 256.0, A.is_equal, A.mult, ["io5", "cf1"], ["bpair"])
+                ts(T.bpair[:, 15:143:16], g8, cf[:, 2:3], None, A.is_equal, None, ["io5", "cf1"], ["bpair"])
+                ts(T.wc[:, 0:128:2], T.iob[:, 0:128:2], cf[:, 2:3], 524288.0, A.is_equal, A.mult, ["iob", "cf1"], ["wc"])
+                ts(T.wc[:, 1:128:2], T.iob[:, 1:128:2], cf[:, 2:3], 2048.0, A.is_equal, A.mult, ["iob", "cf1"], ["wc"])
+                for a in range(NP, 8):
+                    fill(T.wc[:, a:128:8], 0.0, ["wc"])
+                for name, c in (("wi256", 256.0), ("wm2k", -2048.0)):
+                    act(T[name][:], T.wi[:], F.Identity, ["wi"], [name], scale=c)
+            ts(T.b0[:, 15:143:16], g8, cf[:, 2:3], 0.5, A.is_equal, A.mult, ["io5", "cf1"], ["b0"])
+            ts(T.bd[:, 15:143:16], g8, cf[:, 2:3], cf[:, 7:8], A.is_equal, A.mult, ["io5", "cf1", "cf7"], ["bd"])
+            cpy(T.invl[:], ps[1][:, 0:32], ["B1"], ["invl"])
+            cpy(T.invi[:, 0:32], ps[1][:, 0:32], ["B1"], ["invi0"])
+            ts(T.thf[:, 0:5], T.thi[:, 0:5], 256.0, None, A.mult, None, ["thi"], ["thf"])
+            ts(T.invi[:, 32:64], T.invi[:, 0:32], 255, None, A.bitwise_and, None, ["invi0"], ["invi1"])
+            ts(T.whi[:], T.iob[:], cf[:, 2:3], -4096.0, A.is_equal, A.mult, ["iob", "cf1"], ["whi"])
+            ts(T.wold[:], T.iob[:], cf[:, 2:3], 4096.0, A.is_equal, A.mult, ["iob", "cf1"], ["wold"])
+            cpy(T.lanel[:], T.invi[:, 32:64], ["invi1"], ["lanel"])
+        for k, spec in enumerate(xs):
+            if spec[0] == "v":
+                xgather(k, spec)
+        if t == 0:
+            cpy(T.suu[:, 0:L], T.sui[:, 0:V:2], ["sui"], ["suu0"])
+            ts(T.wk[:], T.dt[:, 1664:W], 1920.5 * U, -1920.0 * U, A.is_gt, A.mult, ["dt3"], ["wk"])
+            tt(T.dt[:, 1664:W], T.dt[:, 1664:W], T.wk[:], A.add, ["dt3", "wk"], ["dt3"])
+            climb(0, MS0)
+        for k, spec in enumerate(xs):
+            s_mm(k, spec)
+        if SBE == "s" and t > 0:
+            act(T.sb[:], ps[0][:, 0:L], F.Identity, ["B0"], ["sb"])
+        else:
+            cpy(T.sb[:], ps[0][:, 0:L], ["B0"], ["sb"])
+        mm(ps[0][:, L:V], T.wu[:], T.sb[:], True, True, ["wu", "sb"], ["B0"])
+        for e in range(2):
+            if NP:
+                ts(T.ox[:, L * e:L * e + L], T.sb[:], T.thr[:, 0:1], None, A.is_gt, None, ["sb", "thr"], ["ox%d" % e])
+            if "s" in ys[NP:]:
+                if OVE == "s" and t > 0:
+                    act(T.ov[:, e:V:2], T.sb[:], F.Relu, ["sb", "ths"], ["ov%d" % e], bias=T.thr[:, 1:2], scale=-16.0)
+                else:
+                    ts(T.ov[:, e:V:2], T.sb[:], T.thr[:, 0:1], 16.0, A.is_le, A.mult, ["sb", "thr"], ["ov%d" % e])
+            if "v" in ys[NP:]:
+                ts(T.ow[:, e:V:2], T.sb[:], T.thr[:, 0:1], None, A.is_gt, None, ["sb", "thr"], ["ow%d" % e])
+        cpy(T.ui[:], ps[0][:, L:V], ["B0"], ["ui"])
+        act(T.hio[:], lanes, F.Sign, [lq], ["hio"], bias=-16.0)
+        ts(T.jj[:], T.ui[:], 15, None, A.bitwise_and, None, ["ui"], ["jj"])
+        ts(T.bi[:], T.ui[:], 16, None, A.bitwise_and, None, ["ui"], ["bi"])
+        ts(T.oh[:], T.jj[:], cf[:, 4:5], cf[:, 5:6], A.max, A.is_equal, ["jj", "cf4", "cf5"], ["oh"])
+        cpy(T.bfl[:], T.bi[:], ["bi"], ["bfl"])
+        masked(ys, len(xs))
+        for a in range(16):
+            sgather(a)
+            d_mm(a)
+        tt(T.n1[:], ps[5][:, 0:L], lanes, A.max, ["B5", lq], ["n1"])
+        if NP:
+            cpy(T.vi[:], ps[4][:, 0:L], ["B4"], ["vi"])
+            ts(T.va[:], T.vi[:], 0xFF00, None, A.bitwise_and, None, ["vi"], ["va"])
+            ts(T.hot[:], T.va[:], T.thf[:, t:t + 1], E15, A.is_ge, A.mult, ["va", "thf"], ["hot"])
+        else:
+            ts(T.hot[:], ps[4][:, 0:L], T.thf[:, t:t + 1], E15, A.is_ge, A.mult, ["B4", "thf"], ["hot"])
+        tt(lanes, T.hot[:], T.n1[:], A.max, ["hot", "n1"], [lq])
+        send(-shift, T.lb[:, V * t:V * t + V], T.lv[:], "ab%d" % t, "sb_", ["lv0", "lv1"], "lb%d" % t, T_BIG)
+        act(T.hi[:], lanes, F.Sign, [lq], ["hi"], bias=-16.0)
+        for b in range(2):
+            o = ps[b][:, L:V]
+            mm(o, (T.wbp, T.wbn)[b][:], T.bfl[:], True, False, ["wbp", "wbn", "bfl"], ["B%d" % b])
+            mm(o, T.wold[:], T.hio[:], False, False, ["wold", "hio"], ["B%d" % b])
+            mm(o, T.whi[:], T.hi[:], False, True, ["whi", "hi"], ["B%d" % b])
+            act(T.sgn[:, L * b:L * b + L], o, F.Sign, ["B%d" % b], ["sgn%d" % b, "acc%d" % b],
+                bias=(-4096.0, -266240.0)[b], scale=-1.0, acc=T.acc[:, b:b + 1])
+        act(T.ks[:], T.sgn[:, 0:V].indirect(T.invl[:, 0:32]), F.Relu, ["sgn0", "sgn1", "invl"], ["ks"], scale=-1.0)
+        send(shift, T.lk[:, V * t:V * t + V], T.ks[:], "ak%d" % t, "sk", ["ks"], "lk%d" % t, T_BIG)
+        tt(T.tt[:], ps[7][:, 0:L], T.hi[:], A.mult, ["B7", "hi"], ["tt"])
+        tt(T.ch[:], ps[6][:, 0:L], T.tt[:], A.add, ["B6", "tt"], ["ch"])
+        children(1 - q, 0, t, shift)
+        kk = "lk%d" % t
+        if t == RO - 1:
+            children(q, 1, t, shift)
+            decode(0, other, lo)
+            decode(1, lanes, lq)
+        act(T.sel[:], T.lb[:, V * t:V * t + V].indirect(T.hpu[:, 0:32]), F.Identity, ["lb%d" % t, "hpu"], ["sel"], scale=DOWN)
+        tt(T.bm[:], T.sel[:], T.sgn[:], A.mult, ["sel", "sgn0", "sgn1"], ["bm"])
+        if t == 0:
+            cpy(T.suu[:, L:V], T.sui[:, 1:V:2], ["sui"], ["suu1"])
+            ts(T.s1[:], T.pli[:, 1:V:2], 1.0, U, A.add, A.mult, ["pli"], ["s1"])
+        else:
+            tt(T.s1[:], T.so[:], lm(t - 1, 1), A.max, ["so", "lm%d1" % (t - 1)], ["s1"])
+        tt(T.bmx[:], T.bm[:, 0:L], T.bm[:, L:V], A.max, ["bm"], ["bmx"])
+        if t < RO - 1:
+            tt(lanes, lanes, keep(t, q), A.mult, [lq, kk], [lq])
+            tt(other, other, keep(t, 1 - q), A.mult, [lo, kk], [lo])
+            tt(lanes, lanes, T.bmx[:], A.max, [lq, "bmx"], [lq])
+            climb(1 - q, MS)
+        tt(T.s2[:], T.s1[:], keep(t, 1 - q), A.mult, ["s1", kk], ["s2"])
+        if t < RO - 1:
+            children(q, 1, t, shift)
+            af = T.af
+            act(af[:, 0:1], T.acc[:, 0:1], F.Identity, ["acc0", "acc1"], ["af0"], bias=T.acc[:, 1:2])
+            act(af[:, 1:2], af[:, 0:1], F.Identity, ["af0"], ["af1"], bias=31.5625, scale=0.0625)
+            if t == 0:
+                ts(T.capf[:, 0:1], T.cpi[:, 0:1], 256.0, None, A.add, None, ["cpi"], ["capf"])
+            act(af[:, 4:5], af[:, 0:1], F.Identity, ["af0", "capf"], ["af4"], bias=T.capf[:, 0:1], scale=0.5)
+            act(af[:, 2:3], af[:, 1:2], F.Identity, ["af1"], ["af2"], bias=12582912.0)
+            act(af[:, 3:4], af[:, 2:3], F.Identity, ["af2"], ["af3"], bias=-12582912.0)
+            act(T.thr[:, 0:1], af[:, 3:4], F.Identity, ["af3", "af4"], ["thr"], bias=af[:, 4:5], scale=-8.0)
+            if OVE == "s":
+                act(T.thr[:, 1:2], T.thr[:, 0:1], F.Identity, ["thr"], ["ths"], bias=16.0, scale=16.0)
+        tt(T.so[:], sgl, keep(t, q), A.mult, ["sg", kk], ["so"])
+
+    t, q = RO - 1, (RO - 1) % 2
+    rnd[0] = RO
+    kk = "lk%d" % t
+    decode(2, T.bmx[:], "bmx")
+    tt(T.fe[:, 0:L], T.s2[:], lm(t, 0), A.max, ["s2", "lm%d0" % t], ["fe0"])
+    ts(T.op[:, 1 - q:V:2], T.fe[:, 0:L], 1.0 / U, -1.0, A.mult, A.add, ["fe0"], ["op0"])
+    tt(T.fe[:, L:V], T.so[:], lm(t, 1), A.max, ["so", "lm%d1" % t], ["fe1"])
+    ts(T.op[:, q:V:2], T.fe[:, L:V], 1.0 / U, -1.0, A.mult, A.add, ["fe1"], ["op1"])
+    dma("y", T.ypl[:], T.op[:], "o1", ["op0", "op1"], [], 3.3)
+    tt(T.n1[:], T.d2[:, L:V], keep(t, q), A.mult, ["de1", kk], ["n1"])
+    tt(T.om[:, 1 - q:V:2], T.d2[:, 0:L], keep(t, 1 - q), A.mult, ["de0", kk], ["om1"])
+    tt(T.om[:, q:V:2], T.n1[:], T.d2[:, V:768], A.max, ["n1", "de2"], ["om0"])
+    dma("s", T.ymk[:], T.om[:], "o2", ["om0", "om1"], [])
+    emit()
+    for sem in ("sb_", "sn", "so", "sk", "cg", "cp_", "cs", "cv", "o1", "o2"):
+        g.wait_ge(T.sem[sem], cnt[sem])

@@ -1,8 +1,9 @@
 import math
-import numpy as np
 from concourse.mybir import AluOpType as A, ActivationFunctionType as F
 
 W, V, L, RO = 1920, 512, 256, 5
+WX = W + 255 * (RO - 1)
+PAD = 32
 F32, BF, F16, I32, U16 = "float32", "bfloat16", "float16", "int32", "uint16"
 
 
@@ -11,59 +12,45 @@ def _s(n, d):
 
 
 SCRATCH = {
-    "xw": _s(W, BF), "sw": _s(W, BF), "pli": _s(V, I32), "sui": _s(V, I32), "mki": _s(V, BF),
+    "xw": _s(WX, BF), "sw": _s(WX, BF), "pli": _s(V, I32), "sui": _s(V, I32), "mki": _s(V, BF),
     "hpi": _s(32, I32), "cpi": _s(8, I32), "thi": _s(8, I32),
-    "io5": _s(V, F32), "io16": _s(480, F16), "iob": _s(128, F32), "pcol": _s(8, I32), "ci": _s(8, I32), "cf": _s(16, F32),
-    "wi": _s(128, BF), "wim": _s(128, BF), "wbp": _s(128, BF), "wbn": _s(128, BF), "wu": _s(128, BF), "whi": _s(128, BF),
-    "wold": _s(128, BF), "bsum": _s(144, BF), "b0": _s(144, BF), "bd": _s(144, BF), "b0f": _s(144, F32),
-    "capf": _s(8, F32), "thf": _s(8, F32), "thr": _s(8, F32), "ai": _s(8, I32), "af": _s(8, F32), "acc": _s(8, F32),
-    "glist": _s(16, U16), "hpu": _s(32, U16), "invl": _s(32, U16), "invi": _s(64, I32), "lanel": _s(32, U16),
-    "suu": _s(V, U16), "offn": _s(L, U16), "offa": _s(L, U16), "inv": _s(V, F32), "dt": _s(W, F32), "wk": _s(L, F32),
-    "sg": _s(288, F32), "so": _s(L, F16), "s1": _s(L, F16), "s2": _s(L, F16), "lv": _s(V, BF),
-    "tw": _s(544, F32), "xg": _s(4096, BF), "mg": _s(4096, BF), "zg": _s(4096, F16), "yy": _s(4096, BF),
-    "ox": _s(V, BF), "yp": _s(2048, F16), "vi": _s(L, I32), "va": _s(L, I32), "bpair": _s(144, BF), "ones": _s(L, BF),
-    "wc": _s(128, BF), "wi256": _s(128, BF), "wm2k": _s(128, BF), "wneg": _s(128, BF),
-    "sb": _s(L, BF), "ov": _s(V, BF), "ow": _s(V, BF), "ui": _s(L, I32), "jj": _s(L, I32), "bi": _s(L, I32), "oh": _s(L, BF), "bfl": _s(L, BF),
-    "hot": _s(L, BF), "n1": _s(L, BF), "hi": _s(L, BF), "hio": _s(L, BF),
-    "tt": _s(L, F32), "ch": _s(L, F32), "ms": _s(V, F16), "sgn": _s(V, BF), "kb": _s(V, BF), "ks": _s(V, BF),
-    "sel": _s(V, BF), "bm": _s(V, BF), "bmx": _s(L, BF),
-    "lm": _s(RO * V, F16), "lb": _s(RO * V, BF), "lk": _s(RO * V, BF),
-    "da": _s(1536, BF), "db": _s(768, BF), "la": _s(1536, F32), "ls": _s(768, F32), "d1": _s(768, BF),
-    "d2": _s(768, BF), "om": _s(V, BF), "op": _s(V, F32), "fe": _s(V, F16),
+    "io1": _s(128, F32), "iob": _s(128, F32), "ioh": _s(128, F32), "iow": _s(128, F32), "pcol": _s(8, I32), "ci": _s(8, I32),
+    "cf": _s(24, F32), "wi": _s(128, BF), "wif": _s(128, F32), "wim": _s(128, BF), "w128": _s(128, BF), "w256": _s(128, BF),
+    "w512": _s(128, BF), "wneg": _s(128, BF), "w16": _s(128, BF), "w127": _s(128, BF), "wtop": _s(128, BF), "wwrap": _s(128, BF),
+    "wlog": _s(128, F16), "wu": _s(128, BF), "wa": _s(128, F32), "wh": _s(128, BF), "wh0": _s(128, BF), "wh1": _s(128, BF),
+    "wja": _s(128, BF), "wjb": _s(128, BF), "wxa": _s(128, BF), "wxb": _s(128, BF), "e8": _s(8, BF), "bm": _s(720, BF),
+    "capf": _s(8, BF), "ths": _s(8, F32), "thr": _s(8, F32), "f8": _s(8, BF),
+    "acc": _s(8, F32), "h0": _s(16, F16), "dh": _s(16, F32),
+    "glist": _s(16, U16), "suu": _s(V, U16), "offa": _s(L, U16), "idx": _s(RO * 16, U16),
+    "pw": _s(PAD + 2 * V, F32), "lv": _s(2 * V, BF), "enc": _s(V, F32),
+    "tw": _s(544, F32), "xl": _s(2048, BF), "xp": _s(2048, F16), "mg": _s(4096, BF), "zg": _s(4096, BF), "zu": _s(4096, BF),
+    "yy": _s(2048, F16), "sb": _s(L, BF), "ox": _s(L, BF), "h16": _s(L, F16), "oh": _s(V, BF), "hb": _s(L, BF), "hot": _s(L, BF),
+    "hi": _s(L, BF), "hio": _s(L, BF), "ri": _s(16, I32), "bt": _s(16, BF), "bd": _s(16, F16), "ind": _s(16, BF),
+    "tt": _s(V, F16), "ch": _s(L, F16), "ck": _s(L, F16), "cw": _s(L, F16), "sel": _s(L, BF),
+    "lm": _s(RO * L, F16), "lb": _s(RO * 2 * V, BF), "li": _s(RO * 16, U16),
+    "da": _s(2 * V, BF), "la": _s(2 * V, F16), "om": _s(V, BF), "sg": _s(V, BF), "op": _s(2 * V, F32),
 }
 for _k in range(8):
     SCRATCH["ps%d" % _k] = ("psum", [128, 512], F32)
 
-LOADS = ["hp", "pl", "xf", "mk", "su", "cp", "th", "stp"]
-SEMAPHORES = (["cv", "cs", "cp_", "cg", "sb_", "sn", "so", "sk", "o1", "o2"] + ["l" + n for n in LOADS]
-              + ["a%s%d" % (k, t) for k in "bnok" for t in range(RO)])
+LOADS = ["hp", "pl", "xf", "mk", "su0", "su1", "cp", "th", "stp", "xe", "se"]
+SEMAPHORES = (["cv", "cs", "cp_", "cg", "sb_", "sm", "si", "o1", "o2"] + ["l" + n for n in LOADS]
+              + ["a%s%d" % (k, t) for k in "bim" for t in range(RO)])
 
-E15 = 2.0 ** 97
-DOWN = 2.0 ** -52
 LN2 = math.log(2.0)
-XS = [("s", 0, 64), ("v", 160, 96), ("s", 64, 64), ("s", 128, 32)]
-XS0 = [("s", 0, 64), ("s", 64, 64), ("v", 192, 64), ("s", 128, 64)]
-NP = 0
-U = 2.0 ** -11
-TILE_BANKS = [2, 3, 1]
-TE, OVE, SBE = "sss", "v", "v"
-TAB = [6, 7, 6, 7]
-MN = 8
-MS0, MS = "ssssssss", "vsssssss"
-YS0, YS = "vvvvssss", "vsssssss"
-LOAD_ORDER = [("s", "hpi", "hp", 2.1), ("y", "mki", "mk", 2.8), ("y", "pli", "pl", 4.0), ("y", "xw", "xf", 6.3),
-              ("y", "sui", "su", 7.6), ("y", "sw", "stp", 9.9), ("s", "cpi", "cp", 2.8), ("s", "thi", "th", 2.8)]
-FIX, CYC, PE, LAT, SLACK, G = 0.06, 0.00083, 0.00042, 0.08, 0.1, 1.56
-T_SMALL, T_BIG = 2.8, 3.6
-SEED, TRIES, CACHE = 1, 4000, {}
-SHIFTS = {}
-COST = {"sg": 512, "offn": 256, "tw": 272, "offa": 256 * G, "sb": 256, "ov": 128, "ui": 256, "jj": 256, "bi": 256, "oh": 256,
-        "bfl": 256, "hot": 256, "n1": 256, "lv": 256, "hi": 128, "tt": 256, "ch": 256, "ms": 256 * G, "bm": 512 * G, "s1": 256,
-        "s2": 256, "so": 512, "bmx": 256, "yy": 512, "mg": 4096 * G / MN, "hio": 256, "sgn": 256, "ks": 512 * G, "ow": 128, "ox": 128, "yp": 512, "vi": 256, "va": 256,
-        "wneg": 128, "sov": 256, "shi": 256, "ssel": 512 * G, "vbm": 512, "ones": 128, "wi256": 128, "wm2k": 128,
-        "sel": 512, "dt": 480, "wk": 256, "zg": 256 * G, "inv": 1900, "io16": 480, "io5": 1200, "iob": 400, "suu": 256,
-        "wi": 128, "wim": 128, "wbp": 128, "wbn": 128, "wu": 128, "whi": 128, "wold": 128, "da": 128, "db": 128, "la": 256, "lt": 2000,
-        "lbb": 256, "ls": 512, "dd": 256, "de": 128, "om": 256, "op": 256, "fe": 256, "enc": 2200}
+DOWN = 2.0 ** -64
+HIGH = 4.0
+ROUND = 1.5 * 2.0 ** 23
+APART = 3
+CLIMB0, CLIMB = "svsvsvsv", "vsvsssss"
+TILES = "vvss"
+TILE_BANKS, PICK_BANKS, NB = [1, 2, 1, 6], [6, 4], 7
+STEPS = "vvvvvsss"
+WHO = {"sb": "v", "h16": "v", "lv": "s", "hio": "v", "tt": "sv"}
+ORDER = ("sa sc n0 tr q1< c4< al0 al1 hi3 lo0 q2< lo1 Sl0 hi0 Sh3 lo2 Sl1 hi1 Sh0 t0 lo3 hi2 Sh1 Sl2 va z5 Sl3 Sh2 t1 sb z6 t3 sd "
+         "ox u o0 h16 o3 y0 o1 y3 q3< y1 t2 o2 m16 y2 F0 oh P0 vc z7 P1 P3 z2 P2 F2 hb F3 vb z1 F1 Fh w5 hot z0 top r5 uT w6 hi bit "
+         "lv n1 z3 sendb w7 ind r6 hx1 k5 r7 Y0 Y1 A k0 idx z4 k3 sendi k6 hx0 k2 k7 k1 k4 tt0 wr0 tt1 f8 j0 j1 wr1 ch sel zero "
+         "sendm wr2 max old c0 c7 da1 db1 c2 c6 da2 c1 hio put c3 q0 thr c5 db2 out dc1 dc2").split()
 
 
 def rank_program(g, core, T, topo):
@@ -76,121 +63,62 @@ def rank_program(g, core, T, topo):
     cnt = {}
     known = {q: {} for q in Q}
     writer, readers = {}, {}
+    ops = []
+    now = [(-1, 0), -1]
+
+    def step(name):
+        now[0] = (now[1] + 1, ORDER.index(name + "<")) if name + "<" in ORDER else (now[1], ORDER.index(name))
+
+    def in_order(name, ks):
+        return sorted(ks, key=lambda k: ORDER.index(name + str(k)))
 
     def wait(q, tok):
         sem, n, clock = tok
-        if q == "p" and sem == "cp_":
+        if (q == "p" and sem == "cp_") or known[q].get(sem, 0) >= n:
             return
-        if known[q].get(sem, 0) >= n:
-            return
-        assert n <= cnt.get(sem, n)
         Q[q].wait_ge(T.sem[sem], n)
         known[q][sem] = n
         for s2, n2 in clock.items():
             if known[q].get(s2, 0) < n2:
                 known[q][s2] = n2
 
-    rnd, seen, kinds = [0], {}, []
-    ops = []
-
-    def record(q, kind, what, r, w, busy, done):
+    def record(q, kind, what, r, w):
+        w = w + [k for k in r if k[0] == "B"]
         deps = set(writer[k] for k in r if k in writer)
         for k in w:
             if k in writer:
                 deps.add(writer[k])
             deps.update(readers.get(k, []))
         me = len(ops)
-        c = "%s%s%s" % ("z" if rnd[0] == 0 else "", q, w[0].rstrip("0123456789") if w else "")
-        seen[(rnd[0], c)] = seen.get((rnd[0], c), -1) + 1
-        kinds.append("%s%d" % (c, seen[(rnd[0], c)]))
-        ops.append((q, kind, what, busy, done, sorted(deps)))
+        ops.append((q, kind, what, now[0], sorted(deps)))
         for k in r:
             readers.setdefault(k, []).append(me)
         for k in w:
             writer[k] = me
             readers[k] = []
-        return me
-
-    def schedule():
-        n = len(ops)
-        after = [[] for _ in range(n)]
-        for i, o in enumerate(ops):
-            for d in o[5]:
-                after[d].append(i)
-
-        def gap(d, i):
-            both = ops[d][0] == ops[i][0] and (ops[d][0] == "p" or ops[d][1] == ops[i][1] == "dma")
-            return ops[d][3] if both else ops[d][4]
-
-        level = [0.0] * n
-        for i in range(n - 1, -1, -1):
-            level[i] = max([gap(i, j) + level[j] for j in after[i]] + [ops[i][4]])
-        edges = [[(j, gap(i, j)) for j in after[i]] for i in range(n)]
-
-        def place(prio):
-            left = [len(o[5]) for o in ops]
-            est, start = [0.0] * n, [0.0] * n
-            ready = [i for i in range(n) if left[i] == 0]
-            busy = {q: [] for q in Q}
-            while ready:
-                i = max(ready, key=lambda k: prio[k])
-                ready.remove(i)
-                q, s, d = ops[i][0], est[i], ops[i][3]
-                if q is not None:
-                    iv = busy[q]
-                    k = len(iv)
-                    while k > 0 and iv[k - 1][1] > s:
-                        k -= 1
-                    while k < len(iv) and iv[k][0] < s + d - 1e-9:
-                        s = max(s, iv[k][1])
-                        k += 1
-                    iv.insert(k, (s, s + d))
-                start[i] = s
-                for j, e in edges[i]:
-                    if est[j] < s + e:
-                        est[j] = s + e
-                    left[j] -= 1
-                    if left[j] == 0:
-                        ready.append(j)
-            return max(start[i] + ops[i][4] for i in range(n)), start
-
-        if "seq" not in CACHE:
-            rng = np.random.default_rng(SEED)
-            names = sorted(set(kinds))
-            members = [[i for i in range(n) if kinds[i] == c] for c in names]
-            prio = [level[i] + SHIFTS.get(kinds[i], 0.0) for i in range(n)]
-            best, start = place(prio)
-            now, moved = best, dict(SHIFTS)
-            for it in range(TRIES):
-                trial, step = list(prio), {}
-                for c in rng.integers(0, len(names), int(rng.integers(1, 5))):
-                    d = round(float(rng.normal(0.0, 2.0)), 1)
-                    step[names[int(c)]] = step.get(names[int(c)], 0.0) + d
-                    for i in members[int(c)]:
-                        trial[i] += d
-                t2, s2 = place(trial)
-                if t2 <= now + 0.3 * (1.0 - it / TRIES) * float(rng.random()):
-                    now, prio = t2, trial
-                    for c, d in step.items():
-                        moved[c] = round(moved.get(c, 0.0) + d, 1)
-                    if t2 < best:
-                        best, start = t2, s2
-                        CACHE["shifts"] = dict(moved)
-            CACHE["seq"] = sorted(range(n), key=lambda i: (start[i], i))
-            CACHE["time"] = best
-        return CACHE["seq"], after
 
     def emit():
-        seq, after = schedule()
+        after = [[] for _ in ops]
+        for i, o in enumerate(ops):
+            for d in o[4]:
+                after[d].append(i)
+        left = [len(o[4]) for o in ops]
+        ready = [i for i in range(len(ops)) if left[i] == 0]
         tok = {}
-        for i in seq:
-            q, kind, what, busy, done, deps = ops[i]
+        while ready:
+            i = min(ready, key=lambda k: (ops[k][3], k))
+            ready.remove(i)
+            for j in after[i]:
+                left[j] -= 1
+                if left[j] == 0:
+                    ready.append(j)
+            q, kind, what, _, deps = ops[i]
             if kind == "arrival":
                 tok[i] = what + ({},)
                 continue
             best = {}
             for d in deps:
-                tk = None if kind == ops[d][1] == "dma" else tok[d]
+                tk = tok[d]
                 if tk is not None and (tk[0] not in best or best[tk[0]][1] < tk[1]):
                     best[tk[0]] = tk
             for tk in best.values():
@@ -211,13 +139,11 @@ def rank_program(g, core, T, topo):
             cnt[sem] = cnt.get(sem, 0) + n
             tok[i] = (sem, cnt[sem], dict(known[q]))
 
-    def op(q, call, r, w, cost=None):
-        if cost is None:
-            cost = FIX + CYC * COST.get(q + w[0].rstrip("0123456789"), COST.get(w[0], COST.get(w[0].rstrip("0123456789"), 64)))
-        record(q, "op", call, r, w, cost, cost + LAT)
+    def op(q, call, r, w):
+        record(q, "op", call, r, w)
 
-    def dma(q, out, in_, sem, r, w, done=2.5):
-        record(q, "dma", (out, in_, sem), r, w, 0.1, done)
+    def dma(q, out, in_, sem, r, w):
+        record(q, "dma", (out, in_, sem), r, w)
 
     def ts(out, in0, s1, s2, o0, o1, r, w):
         if o1 is None:
@@ -237,326 +163,345 @@ def rank_program(g, core, T, topo):
     def act(out, in_, f, r, w, bias=0.0, scale=1.0, acc=None):
         op("s", lambda: g.scalar.activation(out, in_, f, bias=bias, scale=scale, accum_out=acc), r, w)
 
-    def mm(out, lhsT, rhs, start, stop, r, w, n=L):
-        op("p", lambda: g.tensor.matmul(out, lhsT, rhs, start, stop), r, w, PE * n)
+    def move(e, out, in_, r, w):
+        if e == "s":
+            act(out, in_, F.Identity, r, w)
+        else:
+            cpy(out, in_, r, w)
 
-    def mms(out, pairs, r, w, n):
+    def relu(e, out, in_, bias, r, w):
+        if e == "s":
+            act(out, in_, F.Relu, r, w, bias=bias)
+        else:
+            ts(out, in_, bias, 0.0, A.add, A.max, r, w)
+
+    def iota(out, pattern, w):
+        op("g", lambda: g.iota(out, pattern, 0, 0, allow_small_or_imprecise_dtypes=True), [], w)
+
+    def mms(bank, c, pairs, r, start=True, stop=True):
+        out = ps[bank][:, c]
+
         def call():
-            return [g.tensor.matmul(out, a, b, k == 0, k == len(pairs) - 1) for k, (a, b) in enumerate(pairs)][-1]
-        op("p", call, r, w, PE * n * len(pairs))
+            return [g.tensor.matmul(out, a, b, start and k == 0, stop and k == len(pairs) - 1) for k, (a, b) in enumerate(pairs)][-1]
+        op("p", call, r, ["B%d" % bank])
 
-    def send(shift, out, in_, arr, loc, r, key, done):
+    def send(shift, out, in_, arr, loc, r, key):
         dst, src = T.cores[(rank + shift) % N], T.cores[(rank - shift) % N]
         rid, pid = topo.addr(dst, core)
         record("g", "send", (lambda: g.remote_dma(out, in_, T.sem[arr], T.sem[loc], pid, rid, topo.mask(core, dst)), loc,
-                             len(topo.engines(core, dst))), r, ["sent" + key], 0.3, done)
-        record(None, "arrival", (arr, len(topo.engines(src, core))), ["sent" + key], [key], 0.0, LAT)
+                             len(topo.engines(core, dst))), r, ["sent" + key])
+        record(None, "arrival", (arr, len(topo.engines(src, core))), ["sent" + key], [key])
 
     ps = [T["ps%d" % k] for k in range(8)]
     cf, ci = T.cf, T.ci
-    sgl = T.sg[:, 16:272]
+    LO, UP, ALL, TINY = slice(0, L), slice(L, V), slice(0, V), slice(0, 16)
 
-    for qq, name, src, done in LOAD_ORDER:
-        wide = {"cpi": 1, "thi": 5}.get(name)
-        dma(qq, T[name][:, 0:wide] if wide else T[name][:], T[src][:], "l" + src, [], [name, "load" + qq], done)
+    def into_row(m, a):
+        return T.bm[:, 144 * m + 15 - a:144 * m + 143 - a]
+
+    for qq, out, in_, name in (
+            ("y", T.mki[:], T.mk[:], "mk"), ("y", T.sui[:, LO], T.su[:, LO], "su0"), ("y", T.sui[:, UP], T.su[:, UP], "su1"),
+            ("y", T.pli[:], T.pl[:], "pl"), ("y", T.xw[:, 0:W], T.xf[:], "xf"), ("y", T.cpi[:, 0:1], T.cp[:], "cp"),
+            ("y", T.thi[:, 0:5], T.th[:], "th"), ("y", T.hpi[:], T.hp[:], "hp"), ("y", T.sw[:, 0:W], T.stp[:], "stp"),
+            ("y", T.xw[:, W:WX], T.xf[:, 0:WX - W], "xe"), ("y", T.sw[:, W:WX], T.stp[:, 0:WX - W], "se")):
+        dma(qq, out, in_, "l" + name, [], [name])
 
     op("g", lambda: g.iota(T.pcol[:, 0:1], [[0, 1]], 0, 1), [], ["pcol"])
-    op("g", lambda: g.iota(T.io5[:], [[1, V]], 0, 0, allow_small_or_imprecise_dtypes=True), [], ["io5"])
-    op("g", lambda: g.iota(T.iob[:], [[1, 8], [0, 16]], 0, 0, allow_small_or_imprecise_dtypes=True), [], ["iob"])
-    fill(T.b0f[:], 0.0, ["b0f"])
-    fill(T.b0[:], 0.0, ["b0"])
-    fill(T.bd[:], 0.0, ["bd"])
-    fill(T.sg[:, 0:16], 1.0, ["pada"])
-    fill(T.sg[:, 272:288], 1.0, ["padb"])
-    g8 = T.io5[:, 0:8]
+    iota(T.io1[:], [[1, 128]], ["io1"])
+    iota(T.iob[:], [[1, 8], [0, 16]], ["iob"])
+    iota(T.ioh[:], [[16, 8], [0, 2], [1, 8]], ["ioh"])
+    iota(T.iow[:], [[0, 8], [1, 2], [0, 8]], ["iow"])
+    for t in range(RO):
+        iota(T.lb[:, 2 * V * t + V:2 * V * (t + 1)], [[0, V]], ["lz%d" % t])
+    zeros = T.lb[:, V:V + L]
+    fill(T.bm[:], 0.0, ["bm0", "bm1", "bm2", "bm3", "bm4"])
+    fill(T.pw[:, 0:PAD], 0.0, ["pada"])
+    fill(T.pw[:, PAD + V:2 * PAD + V], 0.0, ["padb"])
+    g8 = T.io1[:, 0:8]
+    cpy(cf[:, 0:1], T.pcol[:, 0:1], ["pcol"], ["cf0"])
     ts(ci[:, 0:1], T.pcol[:, 0:1], 15, None, A.bitwise_and, None, ["pcol"], ["ci0"])
     ts(ci[:, 1:2], T.pcol[:, 0:1], 4, None, A.logical_shift_right, None, ["pcol"], ["ci1"])
-    cpy(cf[:, 0:1], T.pcol[:, 0:1], ["pcol"], ["cf0"])
-    cpy(cf[:, 1:3], ci[:, 0:2], ["ci0", "ci1"], ["cf1"])
-    tt(ci[:, 2:3], ci[:, 0:1], ci[:, 1:2], A.add, ["ci0", "ci1"], ["ci2"])
-    ts(cf[:, 3:4], cf[:, 1:2], 0.0, None, A.is_equal, None, ["cf1"], ["cf3"])
-    ts(ci[:, 3:4], ci[:, 2:3], 1, None, A.bitwise_and, None, ["ci2"], ["ci3"])
-    ts(cf[:, 6:7], cf[:, 1:2], 2.0, 1.0, A.mult, A.add, ["cf1"], ["cf6"])
-    ts(T.b0f[:, 15:143:16], g8, cf[:, 2:3], cf[:, 3:4], A.is_equal, A.mult, ["io5", "cf1", "cf3"], ["b0f"])
-    ts(T.wi[:], T.io5[:, 0:128], cf[:, 0:1], None, A.is_equal, None, ["io5", "cf0"], ["wi"])
-    ts(cf[:, 4:5], cf[:, 3:4], 99.0, 1.0, A.mult, A.add, ["cf3"], ["cf4"])
-    ts(cf[:, 7:8], cf[:, 3:4], -1.0, 0.5, A.mult, A.add, ["cf3"], ["cf7"])
-    ts(cf[:, 8:9], ci[:, 3:4], 17.0, cf[:, 1:2], A.mult, A.add, ["ci3", "cf1"], ["cf8"])
-    cpy(T.hpu[:], T.hpi[:], ["hpi"], ["hpu"])
-    ts(cf[:, 9:10], cf[:, 8:9], 16.0, None, A.mult, None, ["cf8"], ["cf9"])
-    fill(T.inv[:], 0.0, ["inv"])
-    op("v", lambda: g.vector.tensor_copy(T.inv[:, 0:V].indirect(T.hpu[:, 0:32]), T.io5[:]), ["hpu", "io5"], ["inv"])
-    for q in range(2):
-        mms(ps[1][:, 16 * q:16 * q + 16], [(T.b0f[:, 15 - rho:143 - rho], T.inv[:, 2 * rho + q:V:32]) for rho in range(16)],
-            ["b0f", "inv"], ["B1"], 256)
-    cpy(T.offn[:], T.pli[:, 0:V:2], ["pli"], ["offn"])
-    ts(sgl, T.pli[:, 0:V:2], 1.0, U, A.add, A.mult, ["pli"], ["sg"])
-    act(T.lv[:], T.mki[:], F.Exp, ["mki"], ["enc", "lv0", "lv1"], bias=-98.0 * LN2, scale=13.0 * LN2)
-    ts(T.glist[:], T.io5[:, 0:16], cf[:, 9:10], None, A.add, None, ["io5", "cf9"], ["glist"])
-    cpy(T.io16[:], T.io5[:, 0:480], ["io5"], ["io16"])
-    for name, c in (("wim", DOWN), ("wneg", -1.0), ("wbp", 16384.0), ("wbn", -16384.0)):
-        act(T[name][:], T.wi[:], F.Identity, ["wi"], [name], scale=c)
-    tt(cf[:, 5:6], cf[:, 1:2], cf[:, 4:5], A.max, ["cf1", "cf4"], ["cf5"])
-    ts(T.wu[:], T.iob[:], cf[:, 2:3], cf[:, 6:7], A.is_equal, A.mult, ["iob", "cf1", "cf6"], ["wu"])
+    ts(T.wi[:], T.io1[:], cf[:, 0:1], None, A.is_equal, None, ["io1", "cf0"], ["wi"])
+    ts(ci[:, 2:3], T.pcol[:, 0:1], 119, None, A.bitwise_and, None, ["pcol"], ["ci2"])
+    tt(ci[:, 3:4], ci[:, 0:1], ci[:, 1:2], A.add, ["ci0", "ci1"], ["ci3"])
+    ts(ci[:, 5:6], ci[:, 0:1], 2.0, 9.0, A.mult, A.add, ["ci0"], ["ci5"])
+    cpy(cf[:, 1:4], ci[:, 0:3], ["ci0", "ci1", "ci2"], ["cf1"])
+    ts(ci[:, 4:5], ci[:, 3:4], 1, None, A.bitwise_and, None, ["ci3"], ["ci4"])
+    ts(ci[:, 6:7], ci[:, 5:6], 15, None, A.bitwise_and, None, ["ci5"], ["ci6"])
 
-    def agent_lists():
-        op("v", lambda: g.vector.transpose(T.tw[:, 0:256], sgl), ["sg"], ["tw1"])
-        op("v", lambda: g.vector.transpose(T.tw[:, 256:544], T.sg[:, 0:288]), ["sg", "pada", "padb"], ["tw2"])
+    def scaled(names):
+        for name, c in names:
+            act(T[name][:], T.wi[:], F.Identity, ["wi"], [name], scale=c)
 
-    def agent_lists2():
-        ts(T.offa[:], T.tw[:, 0:544].indirect(T.glist[:, 0:16]), 1.0 / U, -1.0, A.mult, A.add, ["tw1", "tw2", "glist"], ["offa"])
+    scaled([("wim", DOWN), ("w256", 256.0)])
+    act(cf[:, 11:12], cf[:, 1:2], F.Sigmoid, ["cf1"], ["cf11"], bias=7.5 * 256, scale=-256.0)
+    ts(cf[:, 4:5], cf[:, 1:2], 0.0, None, A.is_equal, None, ["cf1"], ["cf4"])
+    ts(cf[:, 9:10], ci[:, 4:5], 17.0, cf[:, 1:2], A.mult, A.add, ["ci4", "cf1"], ["cf9"])
+    ts(cf[:, 13:14], ci[:, 6:7], -8.0, None, A.add, None, ["ci6"], ["cf13"])
+    ts(cf[:, 5:6], cf[:, 4:5], 99.0, 1.0 - 24576.0, A.mult, A.add, ["cf4"], ["cf5"])
+    ts(cf[:, 10:11], cf[:, 9:10], 16.0, None, A.mult, None, ["cf9"], ["cf10"])
+    ts(cf[:, 7:8], cf[:, 1:2], 1.0 / 16, 1.0 / 32, A.mult, A.add, ["cf1"], ["cf7"])
+    ts(cf[:, 8:9], cf[:, 1:2], 1.0, None, A.min, None, ["cf1"], ["cf8"])
+    ts(cf[:, 12:13], cf[:, 1:2], 8.0, None, A.is_ge, None, ["cf1"], ["cf12"])
+    ts(T.glist[:], T.io1[:, 0:16], cf[:, 10:11], None, A.add, None, ["io1", "cf10"], ["glist"])
+    ts(cf[:, 6:7], cf[:, 1:2], -24576.0, cf[:, 5:6], A.add, A.max, ["cf1", "cf5"], ["cf6"])
+    ts(cf[:, 14:15], cf[:, 12:13], -65536.0 * 129 - 256.0 * 258, 65536.0 * 129 + 128, A.mult, A.add, ["cf12"], ["cf14"])
+    ts(T.e8[:], g8, cf[:, 2:3], None, A.is_equal, None, ["io1", "cf1"], ["e8"])
+    ts(T.wu[:], T.iob[:], cf[:, 2:3], cf[:, 13:14], A.is_equal, A.mult, ["iob", "cf1", "cf13"], ["wu"])
+    ts(T.wh0[:], T.ioh[:], cf[:, 3:4], None, A.is_equal, None, ["ioh", "cf1"], ["wh0"])
+    ts(T.wh1[:], T.iow[:], 0.5 + 1.0 / 256, -0.5, A.mult, A.add, ["iow"], ["wh1"])
+    ts(T.wa[:], T.iob[:], cf[:, 2:3], -1.0, A.is_equal, A.mult, ["iob", "cf1"], ["wa"])
+    tt(T.wjb[:], T.wh0[:], T.iow[:], A.mult, ["wh0", "iow"], ["wjb"])
+    tt(T.wh[:], T.wh0[:], T.wh1[:], A.mult, ["wh0", "wh1"], ["wh"])
+    ts(T.wxa[:], T.wh0[:], 128.0, None, A.mult, None, ["wh0"], ["wxa"])
+    tt(T.wja[:], T.wh0[:], T.wjb[:], A.subtract, ["wh0", "wjb"], ["wja"])
+    tt(T.wh1[:], T.w256[:], T.wxa[:], A.subtract, ["w256", "wxa"], ["wh1", "wx"])
+    SPREAD = ((0, 15, 0.5, "cf1"), (2, 15, cf[:, 7:8], "cf7"), (3, 15, cf[:, 11:12], "cf11"), (3, 23, cf[:, 12:13], "cf12"),
+              (1, 15, cf[:, 8:9], "cf8"), (1, 23, cf[:, 4:5], "cf4"), (4, 15, cf[:, 8:9], "cf8"), (4, 7, cf[:, 4:5], "cf4"))
 
-    def xgather(k, spec):
-        e, a, n = spec
-        o, w = T.xg[:, 16 * a:16 * (a + n)], T.xw[:, 0:W].indirect(T.offn[:, a:a + n])
-        gather(e, o, w, ["xw", "offn"], ["xg%d" % k], 16 * n)
-
-    def gather(e, o, w, r, wr, n):
-        if e == "s":
-            op("s", lambda: g.scalar.activation(o, w, F.Identity), r, wr, FIX + CYC * G * n)
-        else:
-            op("v", lambda: g.vector.tensor_copy(o, w), r, wr, FIX + CYC * G * n)
-
-    def s_mm(k, spec):
-        e, a0, n = spec
-        mms(ps[0][:, a0:a0 + n], [(T.wi[:], T.xg[:, 16 * a0 + a:16 * (a0 + n):16]) for a in range(16)], ["wi", "xg%d" % k], ["B0"],
-            max(n, 64))
+    act(T.enc[:], T.mki[:], F.Sigmoid, ["mk"], ["enc"], bias=-125.0 * LN2, scale=8.0 * LN2)
+    act(T.lv[:, ALL], T.enc[:], F.Square, ["enc"], ["lv0", "lv1"], scale=2.0 ** 63)
+    for h in range(2):
+        cpy(T.suu[:, 128 * h:128 * h + 128], T.sui[:, L * h:L * h + L:2], ["su%d" % h], ["suu0%d" % h])
 
     def climb(q, engines):
-        n = L // MN
-        for k in range(MN):
-            o = L * q + n * k
-            gather(engines[k], T.mg[:, 16 * n * k:16 * n * (k + 1)], T.lv[:, 0:V].indirect(T.suu[:, o:o + n]),
-                   ["lv0", "lv1", "suu%d" % q], ["mg%d" % k], 16 * n)
-        for k in range(4):
-            mms(ps[5][:, 64 * k:64 * k + 64], [(T.wim[:], T.mg[:, 1024 * k + a:1024 * k + 1024:16]) for a in range(16)],
-                ["wim"] + ["mg%d" % j for j in range(k * MN // 4, (k + 1) * MN // 4)], ["B5"], 64)
-
-    def masked(engines, nx):
-        xk = ["xg%d" % k for k in range(nx)]
-        nb = 0
-        for i in range(NP // 2):
-            b = TILE_BANKS[nb % len(TILE_BANKS)]
-            nb += 1
-            for e in range(2):
-                a = 2 * i + 8 * e
-                mms(ps[b][:, L * e:L * e + L], [(T.wm2k[:], T.ones[:]), (T.wi[:], T.xg[:, a:4096:16]), (T.wi256[:], T.xg[:, a + 1:4096:16])],
-                    ["wm2k", "ones", "wi", "wi256"] + xk, ["B%d" % b], L)
-            tt(T.yp[:, V * i:V * i + V], ps[b][:], T.ox[:], A.mult, ["B%d" % b, "ox0", "ox1"], ["yp%d" % i])
-        steps = []
-        if NP:
-            steps.append((T.wc[:], T.ox[:, 0:L], ["wc", "ox0"]))
-        for i in range(NP // 2):
-            for e in range(2):
-                a = 2 * i + 8 * e
-                steps.append((T.bpair[:, 14 - a:142 - a], T.yp[:, V * i + L * e:V * i + L * e + L], ["bpair", "yp%d" % i]))
-        for j in range(NP, 8):
-            y = T.yy[:, V * j:V * j + V]
-            if engines[j] == "s":
-                b = TILE_BANKS[nb % len(TILE_BANKS)]
-                nb += 1
-                mm(ps[b][:], T.wi[:], T.xg[:, j:4096:8], True, False, ["wi"] + xk, ["B%d" % b], V)
-                mm(ps[b][:], T.wneg[:], T.ov[:], False, True, ["wneg", "ov0", "ov1"], ["B%d" % b], V)
-                act(y, ps[b][:], F.Relu, ["B%d" % b], ["yy%d" % j])
-            else:
-                tt(y, T.xg[:, j:4096:8], T.ow[:], A.mult, xk + ["ow0", "ow1"], ["yy%d" % j])
-            for e in range(2):
-                a = j + 8 * e
-                steps.append((T.bsum[:, 15 - a:143 - a], T.yy[:, V * j + e:V * j + V:2], ["bsum", "yy%d" % j]))
-        for k, (w, y, r) in enumerate(steps):
-            mm(ps[4][:, 0:L], w, y, k == 0, k == len(steps) - 1, r, ["B4"])
-
-    def sgather(a):
-        tt(T.zg[:, 256 * a:256 * a + 256], T.dt[:, 0:W].indirect(T.offa[:, 16 * a:16 * a + 16]), T.oh[:], A.mult,
-           ["dt0", "dt1", "dt2", "dt3", "offa", "oh"], ["zg%d" % a])
-
-    def d_mm(a):
-        z = T.zg[:, 256 * a:256 * a + 256]
-        mm(ps[6][:, 0:L], T.b0[:, 15 - a:143 - a], z, a == 0, a == 15, ["b0", "zg%d" % a], ["B6"])
-        mm(ps[7][:, 0:L], T.bd[:, 15 - a:143 - a], z, a == 0, a == 15, ["bd", "zg%d" % a], ["B7"])
-
-    def children(par, part, t, shift):
-        tt(T.ms[:, L * part:L * part + L], T.ch[:, 0:L].indirect(T.lanel[:, 16 * par:16 * par + 16]), T.ks[:, L * par:L * par + L],
-           A.subtract, ["ch", "lanel", "ks"], ["ms%d" % part])
-        o = V * t + L * part
-        send(shift, T.lm[:, o:o + L], T.ms[:, L * part:L * part + L], "a%s%d" % ("no"[part], t),
-             ("sn", "so")[part], ["ms%d" % part], "lm%d%d" % (t, part), T_SMALL)
-
-    def decode(k, src, key):
-        c, c2 = slice(L * k, L * k + L), slice(V * k, V * k + V)
-        ts(T.da[:, V * k:V * k + L], src, 1.0, 2.0 ** -49, A.max, A.mult, [key], ["da%d" % k])
-        ts(T.db[:, c], src, 1.0, 2.0 ** -98, A.min, A.max, [key], ["db%d" % k])
-        act(T.la[:, V * k:V * k + L], T.da[:, V * k:V * k + L], F.Ln, ["da%d" % k], ["lt" if k == 0 else "la%d" % k, "ln"])
-        act(T.la[:, V * k + L:V * k + V], T.db[:, c], F.Ln, ["db%d" % k], ["lbb%d" % k, "ln"], scale=2.0 ** 49)
-        tt(T.ls[:, c], T.la[:, V * k:V * k + L], T.la[:, V * k + L:V * k + V], A.add,
-           ["lt" if k == 0 else "la%d" % k, "lbb%d" % k], ["ls%d" % k])
-        ts(T.d1[:, c], T.ls[:, c], 1.0 / (13.0 * LN2), 160.0 + 92.0 / 13.0, A.mult, A.add, ["ls%d" % k], ["dd%d" % k])
-        ts(T.d2[:, c], T.d1[:, c], -160.0, None, A.add, None, ["dd%d" % k], ["de%d" % k])
-
-    def keep(t, par):
-        return T.lk[:, V * t + L * par:V * t + L * par + L]
-
-    def lm(t, part):
-        return T.lm[:, V * t + L * part:V * t + L * part + L]
-
-    for t in range(RO):
-        q = t % 2
+        n = L // len(engines)
         lanes = T.lv[:, q:V:2]
-        other = T.lv[:, 1 - q:V:2]
-        lq, lo = "lv%d" % q, "lv%d" % (1 - q)
-        shift = 1 + t % (N - 1)
-        xs = XS0 if t == 0 else XS
-        ys = YS0 if t == 0 else YS
-        rnd[0] = t
-        if t > 0:
-            tt(sgl, T.s2[:], lm(t - 1, 0), A.max, ["s2", "lm%d0" % (t - 1)], ["sg"])
-            ts(T.offn[:], sgl, 1.0 / U, -1.0, A.mult, A.add, ["sg"], ["offn"])
-        for k, spec in enumerate(xs):
-            if spec[0] == "s":
-                xgather(k, spec)
-        agent_lists()
-        if t == 0:
-            cpy(T.thr[:, 0:1], T.cpi[:, 0:1], ["cpi"], ["thr"])
-            for k in range(4):
-                b = TAB[k]
-                mm(ps[b][:, 0:480], T.wi[:], T.sw[:, 480 * k:480 * k + 480], True, False, ["wi", "sw"], ["B%d" % b], 480)
-                mm(ps[b][:, 0:480], T.wi[:], T.io16[:], False, True, ["wi", "io16"], ["B%d" % b], 480)
-                if k == 3:
-                    ts(T.dt[:, 1440:W], ps[b][:, 0:480], 1441.0, U, A.add, A.mult, ["B%d" % b], ["dt3"])
-                elif TE[k] == "v":
-                    ts(T.dt[:, 480 * k:480 * k + 480], ps[b][:, 0:480], 480.0 * k + 1.0, U, A.add, A.mult, ["B%d" % b], ["dt%d" % k])
-                else:
-                    act(T.dt[:, 480 * k:480 * k + 480], ps[b][:, 0:480], F.Identity, ["B%d" % b], ["dt%d" % k],
-                        bias=(480.0 * k + 1.0) * U, scale=U)
-        agent_lists2()
-        if t == 0:
-            if NP < 8:
-                fill(T.bsum[:], 0.0, ["bsum"])
-                ts(T.bsum[:, 15:143:16], g8, cf[:, 2:3], 256.0, A.is_equal, A.mult, ["io5", "cf1"], ["bsum"])
-            if NP:
-                fill(T.bpair[:], 0.0, ["bpair"])
-                fill(T.ones[:], 1.0, ["ones"])
-                ts(T.bpair[:, 14:142:16], g8, cf[:, 2:3], 256.0, A.is_equal, A.mult, ["io5", "cf1"], ["bpair"])
-                ts(T.bpair[:, 15:143:16], g8, cf[:, 2:3], None, A.is_equal, None, ["io5", "cf1"], ["bpair"])
-                ts(T.wc[:, 0:128:2], T.iob[:, 0:128:2], cf[:, 2:3], 524288.0, A.is_equal, A.mult, ["iob", "cf1"], ["wc"])
-                ts(T.wc[:, 1:128:2], T.iob[:, 1:128:2], cf[:, 2:3], 2048.0, A.is_equal, A.mult, ["iob", "cf1"], ["wc"])
-                for a in range(NP, 8):
-                    fill(T.wc[:, a:128:8], 0.0, ["wc"])
-                for name, c in (("wi256", 256.0), ("wm2k", -2048.0)):
-                    act(T[name][:], T.wi[:], F.Identity, ["wi"], [name], scale=c)
-            ts(T.b0[:, 15:143:16], g8, cf[:, 2:3], 0.5, A.is_equal, A.mult, ["io5", "cf1"], ["b0"])
-            ts(T.bd[:, 15:143:16], g8, cf[:, 2:3], cf[:, 7:8], A.is_equal, A.mult, ["io5", "cf1", "cf7"], ["bd"])
-            cpy(T.invl[:], ps[1][:, 0:32], ["B1"], ["invl"])
-            cpy(T.invi[:, 0:32], ps[1][:, 0:32], ["B1"], ["invi0"])
-            ts(T.thf[:, 0:5], T.thi[:, 0:5], 256.0, None, A.mult, None, ["thi"], ["thf"])
-            ts(T.invi[:, 32:64], T.invi[:, 0:32], 255, None, A.bitwise_and, None, ["invi0"], ["invi1"])
-            ts(T.whi[:], T.iob[:], cf[:, 2:3], -4096.0, A.is_equal, A.mult, ["iob", "cf1"], ["whi"])
-            ts(T.wold[:], T.iob[:], cf[:, 2:3], 4096.0, A.is_equal, A.mult, ["iob", "cf1"], ["wold"])
-            cpy(T.lanel[:], T.invi[:, 32:64], ["invi1"], ["lanel"])
-        for k, spec in enumerate(xs):
-            if spec[0] == "v":
-                xgather(k, spec)
-        if t == 0:
-            cpy(T.suu[:, 0:L], T.sui[:, 0:V:2], ["sui"], ["suu0"])
-            ts(T.wk[:], T.dt[:, 1664:W], 1920.5 * U, -1920.0 * U, A.is_gt, A.mult, ["dt3"], ["wk"])
-            tt(T.dt[:, 1664:W], T.dt[:, 1664:W], T.wk[:], A.add, ["dt3", "wk"], ["dt3"])
-            climb(0, MS0)
-        for k, spec in enumerate(xs):
-            s_mm(k, spec)
-        if SBE == "s" and t > 0:
-            act(T.sb[:], ps[0][:, 0:L], F.Identity, ["B0"], ["sb"])
+        step("hio")
+        if WHO["hio"] == "v":
+            ts(T.hio[:], lanes, HIGH, 2.0, A.is_lt, A.mult, ["lv%d" % q], ["hio"])
         else:
-            cpy(T.sb[:], ps[0][:, 0:L], ["B0"], ["sb"])
-        mm(ps[0][:, L:V], T.wu[:], T.sb[:], True, True, ["wu", "sb"], ["B0"])
-        for e in range(2):
-            if NP:
-                ts(T.ox[:, L * e:L * e + L], T.sb[:], T.thr[:, 0:1], None, A.is_gt, None, ["sb", "thr"], ["ox%d" % e])
-            if "s" in ys[NP:]:
-                if OVE == "s" and t > 0:
-                    act(T.ov[:, e:V:2], T.sb[:], F.Relu, ["sb", "ths"], ["ov%d" % e], bias=T.thr[:, 1:2], scale=-16.0)
-                else:
-                    ts(T.ov[:, e:V:2], T.sb[:], T.thr[:, 0:1], 16.0, A.is_le, A.mult, ["sb", "thr"], ["ov%d" % e])
-            if "v" in ys[NP:]:
-                ts(T.ow[:, e:V:2], T.sb[:], T.thr[:, 0:1], None, A.is_gt, None, ["sb", "thr"], ["ow%d" % e])
-        cpy(T.ui[:], ps[0][:, L:V], ["B0"], ["ui"])
-        act(T.hio[:], lanes, F.Sign, [lq], ["hio"], bias=-16.0)
-        ts(T.jj[:], T.ui[:], 15, None, A.bitwise_and, None, ["ui"], ["jj"])
-        ts(T.bi[:], T.ui[:], 16, None, A.bitwise_and, None, ["ui"], ["bi"])
-        ts(T.oh[:], T.jj[:], cf[:, 4:5], cf[:, 5:6], A.max, A.is_equal, ["jj", "cf4", "cf5"], ["oh"])
-        cpy(T.bfl[:], T.bi[:], ["bi"], ["bfl"])
-        masked(ys, len(xs))
-        for a in range(16):
-            sgather(a)
-            d_mm(a)
-        tt(T.n1[:], ps[5][:, 0:L], lanes, A.max, ["B5", lq], ["n1"])
-        if NP:
-            cpy(T.vi[:], ps[4][:, 0:L], ["B4"], ["vi"])
-            ts(T.va[:], T.vi[:], 0xFF00, None, A.bitwise_and, None, ["vi"], ["va"])
-            ts(T.hot[:], T.va[:], T.thf[:, t:t + 1], E15, A.is_ge, A.mult, ["va", "thf"], ["hot"])
-        else:
-            ts(T.hot[:], ps[4][:, 0:L], T.thf[:, t:t + 1], E15, A.is_ge, A.mult, ["B4", "thf"], ["hot"])
-        tt(lanes, T.hot[:], T.n1[:], A.max, ["hot", "n1"], [lq])
-        send(-shift, T.lb[:, V * t:V * t + V], T.lv[:], "ab%d" % t, "sb_", ["lv0", "lv1"], "lb%d" % t, T_BIG)
-        act(T.hi[:], lanes, F.Sign, [lq], ["hi"], bias=-16.0)
-        for b in range(2):
-            o = ps[b][:, L:V]
-            mm(o, (T.wbp, T.wbn)[b][:], T.bfl[:], True, False, ["wbp", "wbn", "bfl"], ["B%d" % b])
-            mm(o, T.wold[:], T.hio[:], False, False, ["wold", "hio"], ["B%d" % b])
-            mm(o, T.whi[:], T.hi[:], False, True, ["whi", "hi"], ["B%d" % b])
-            act(T.sgn[:, L * b:L * b + L], o, F.Sign, ["B%d" % b], ["sgn%d" % b, "acc%d" % b],
-                bias=(-4096.0, -266240.0)[b], scale=-1.0, acc=T.acc[:, b:b + 1])
-        act(T.ks[:], T.sgn[:, 0:V].indirect(T.invl[:, 0:32]), F.Relu, ["sgn0", "sgn1", "invl"], ["ks"], scale=-1.0)
-        send(shift, T.lk[:, V * t:V * t + V], T.ks[:], "ak%d" % t, "sk", ["ks"], "lk%d" % t, T_BIG)
-        tt(T.tt[:], ps[7][:, 0:L], T.hi[:], A.mult, ["B7", "hi"], ["tt"])
-        tt(T.ch[:], ps[6][:, 0:L], T.tt[:], A.add, ["B6", "tt"], ["ch"])
-        children(1 - q, 0, t, shift)
-        kk = "lk%d" % t
-        if t == RO - 1:
-            children(q, 1, t, shift)
-            decode(0, other, lo)
-            decode(1, lanes, lq)
-        act(T.sel[:], T.lb[:, V * t:V * t + V].indirect(T.hpu[:, 0:32]), F.Identity, ["lb%d" % t, "hpu"], ["sel"], scale=DOWN)
-        tt(T.bm[:], T.sel[:], T.sgn[:], A.mult, ["sel", "sgn0", "sgn1"], ["bm"])
-        if t == 0:
-            cpy(T.suu[:, L:V], T.sui[:, 1:V:2], ["sui"], ["suu1"])
-            ts(T.s1[:], T.pli[:, 1:V:2], 1.0, U, A.add, A.mult, ["pli"], ["s1"])
-        else:
-            tt(T.s1[:], T.so[:], lm(t - 1, 1), A.max, ["so", "lm%d1" % (t - 1)], ["s1"])
-        tt(T.bmx[:], T.bm[:, 0:L], T.bm[:, L:V], A.max, ["bm"], ["bmx"])
-        if t < RO - 1:
-            tt(lanes, lanes, keep(t, q), A.mult, [lq, kk], [lq])
-            tt(other, other, keep(t, 1 - q), A.mult, [lo, kk], [lo])
-            tt(lanes, lanes, T.bmx[:], A.max, [lq, "bmx"], [lq])
-            climb(1 - q, MS)
-        tt(T.s2[:], T.s1[:], keep(t, 1 - q), A.mult, ["s1", kk], ["s2"])
-        if t < RO - 1:
-            children(q, 1, t, shift)
-            af = T.af
-            act(af[:, 0:1], T.acc[:, 0:1], F.Identity, ["acc0", "acc1"], ["af0"], bias=T.acc[:, 1:2])
-            act(af[:, 1:2], af[:, 0:1], F.Identity, ["af0"], ["af1"], bias=31.5625, scale=0.0625)
-            if t == 0:
-                ts(T.capf[:, 0:1], T.cpi[:, 0:1], 256.0, None, A.add, None, ["cpi"], ["capf"])
-            act(af[:, 4:5], af[:, 0:1], F.Identity, ["af0", "capf"], ["af4"], bias=T.capf[:, 0:1], scale=0.5)
-            act(af[:, 2:3], af[:, 1:2], F.Identity, ["af1"], ["af2"], bias=12582912.0)
-            act(af[:, 3:4], af[:, 2:3], F.Identity, ["af2"], ["af3"], bias=-12582912.0)
-            act(T.thr[:, 0:1], af[:, 3:4], F.Identity, ["af3", "af4"], ["thr"], bias=af[:, 4:5], scale=-8.0)
-            if OVE == "s":
-                act(T.thr[:, 1:2], T.thr[:, 0:1], F.Identity, ["thr"], ["ths"], bias=16.0, scale=16.0)
-        tt(T.so[:], sgl, keep(t, q), A.mult, ["sg", kk], ["so"])
+            act(T.hio[:], lanes, F.Sign, ["lv%d" % q], ["hio"], bias=HIGH, scale=-1.0)
+        step("old")
+        mms(5, LO, [(T.wi[:], lanes)], ["wi", "lv%d" % q], True, False)
+        for k, e in enumerate(engines):
+            o = L * q + n * k
+            step("c%d" % k)
+            move(e, T.mg[:, 16 * n * k:16 * n * (k + 1)], T.lv[:, ALL].indirect(T.suu[:, o:o + n]),
+                 ["lv0", "lv1", "suu%d%d" % (q, n * k // 128)], ["mg%d" % k])
+        per = len(engines) // 4
+        for k in range(4):
+            step("q%d" % k)
+            mms(5, slice(64 * k, 64 * k + 64), [(T.wim[:], T.mg[:, 1024 * k + a:1024 * k + 1024:16]) for a in range(16)],
+                ["wim"] + ["mg%d" % j for j in range(k * per, (k + 1) * per)], False, False)
 
-    t, q = RO - 1, (RO - 1) % 2
-    rnd[0] = RO
-    kk = "lk%d" % t
-    decode(2, T.bmx[:], "bmx")
-    tt(T.fe[:, 0:L], T.s2[:], lm(t, 0), A.max, ["s2", "lm%d0" % t], ["fe0"])
-    ts(T.op[:, 1 - q:V:2], T.fe[:, 0:L], 1.0 / U, -1.0, A.mult, A.add, ["fe0"], ["op0"])
-    tt(T.fe[:, L:V], T.so[:], lm(t, 1), A.max, ["so", "lm%d1" % t], ["fe1"])
-    ts(T.op[:, q:V:2], T.fe[:, L:V], 1.0 / U, -1.0, A.mult, A.add, ["fe1"], ["op1"])
-    dma("y", T.ypl[:], T.op[:], "o1", ["op0", "op1"], [], 3.3)
-    tt(T.n1[:], T.d2[:, L:V], keep(t, q), A.mult, ["de1", kk], ["n1"])
-    tt(T.om[:, 1 - q:V:2], T.d2[:, 0:L], keep(t, 1 - q), A.mult, ["de0", kk], ["om1"])
-    tt(T.om[:, q:V:2], T.n1[:], T.d2[:, V:768], A.max, ["n1", "de2"], ["om0"])
-    dma("s", T.ymk[:], T.om[:], "o2", ["om0", "om1"], [])
+    def decode(k, bank):
+        a, b = slice(V * k, V * k + L), slice(V * k + L, V * k + V)
+        src, key = T.lv[:, k:V:2], "lv%d" % k
+        step("da%d" % bank)
+        ts(T.da[:, a], src, 2.0 ** -124, 2.0 ** -4, A.max, A.min, [key], ["da%d" % k])
+        ts(T.da[:, b], src, 2.0 ** -4, None, A.max, None, [key], ["db%d" % k])
+        step("db%d" % bank)
+        act(T.la[:, a], T.da[:, a], F.Ln, ["da%d" % k], ["la%d" % k], scale=2.0 ** 64.25)
+        act(T.la[:, b], T.da[:, b], F.Ln, ["db%d" % k], ["lc%d" % k], scale=2.0 ** -55.5)
+        mms(bank, LO, [(T.wlog[:], T.la[:, a]), (T.wlog[:], T.la[:, b])], ["wlog", "la%d" % k, "lc%d" % k])
+        step("dc%d" % bank)
+        ts(T.om[:, k:V:2], ps[bank][:, LO], ROUND + 7.0, -ROUND, A.add, A.add, ["B%d" % bank], ["om%d" % k])
+
+    climb(0, CLIMB0)
+    step("put")
+    ts(T.pw[:, PAD:PAD + V], T.pli[:], -float(W), None, A.add, None, ["pl"], ["pw"])
+    for t in range(RO):
+        now[1] = t
+        q, last = t % 2, t == RO - 1
+        shift = 1 + t % (N - 1)
+        wide = W + 255 * t
+        tables = ["xf", "xe"] if t else ["xf"]
+        places = T.pw[:, PAD + q:PAD + V:2]
+        sk = ["lv0", "lv1"]
+        lanes = T.lv[:, q:V:2]
+        idx, got = T.idx[:, 16 * t:16 * t + 16], T.li[:, 16 * t:16 * t + 16]
+
+        step("tr")
+        op("v", lambda p=places: g.vector.transpose(T.tw[:, 0:256], p), ["pw"], ["tw1"])
+        op("v", lambda p=T.pw[:, q:q + 576:2]: g.vector.transpose(T.tw[:, 256:544], p), ["pw", "pada", "padb"], ["tw2"])
+        for h in range(2):
+            step("al%d" % h)
+            ts(T.offa[:, 128 * h:128 * h + 128], T.tw[:, 0:544].indirect(T.glist[:, 8 * h:8 * h + 8]), float(W), None, A.add, None,
+               ["tw1", "tw2", "glist"], ["offa%d" % h])
+        if t == 0:
+            step("va")
+            ts(T.thr[:, 0:1], T.cpi[:, 0:1], -1288.0, None, A.add, None, ["cp"], ["thr"])
+            step("vb")
+            ts(T.ths[:, 0:5], T.thi[:, 0:5], -256.0, cf[:, 14:15], A.mult, A.add, ["th", "cf14"], ["ths"])
+            cpy(T.h0[:], T.hpi[:, 0:16], ["hp"], ["h0"])
+            tt(T.dh[:], T.hpi[:, 16:32], T.hpi[:, 0:16], A.subtract, ["hp"], ["dh"])
+            step("vc")
+            cpy(T.capf[:, 0:1], T.cpi[:, 0:1], ["cp"], ["capf"])
+            cpy(T.suu[:, UP], T.sui[:, 1:V:2], ["su0", "su1"], ["suu10", "suu11"])
+            step("sa")
+            scaled([("w127", 127.0), ("w128", 128.0)])
+            step("sc")
+            scaled([("w16", 16.0), ("wneg", -1.0)])
+            for m, o, c, key in SPREAD[:4]:
+                act(T.bm[:, 144 * m + o:144 * m + o + 113:16], T.e8[:], F.Identity, ["e8", key], ["bm%d" % m], scale=c)
+            act(T.wtop[:], T.wi[:], F.Square, ["wi"], ["wtop"], scale=2.0 ** 58)
+            step("sd")
+            scaled([("w512", 512.0)])
+            for m, o, c, key in SPREAD[4:]:
+                act(T.bm[:, 144 * m + o:144 * m + o + 113:16], T.e8[:], F.Identity, ["e8", key], ["bm%d" % m], scale=c)
+            for w, c, key in ((T.wxa, cf[:, 11:12], "cf11"), (T.wxb, cf[:, 12:13], "cf12")):
+                act(w[:], T.wh1[:], F.Identity, ["wx", key], ["wxa", "wxb"], scale=c)
+        for k in range(4):
+            c = slice(V * k, V * k + V)
+            step("lo%d" % k)
+            act(T.xl[:, c], T.xw[:, 0:wide].indirect(T.offa[:, 32 * k:32 * k + 32]), F.Identity, tables + ["offa0"], ["xl%d" % k],
+                scale=1.0 / 128)
+            step("hi%d" % k)
+            win = T.xw[:, 0:wide].indirect(T.offa[:, 128 + 32 * k:160 + 32 * k])
+            if k == APART:
+                cpy(T.xp[:, c], win, tables + ["offa1"], ["xp%d" % k])
+            else:
+                tt(T.xp[:, c], win, T.xl[:, c], A.add, tables + ["offa1", "xl%d" % k], ["xp%d" % k])
+        parts = sorted([h + str(k) for h in ("Sl", "Sh") for k in range(4)], key=ORDER.index)
+        for name in parts:
+            step(name)
+            k = int(name[2])
+            w, x, key = (T.wi, T.xp, "xp") if name[1] == "h" else (T.w128 if k == APART else T.w127, T.xl, "xl")
+            mms(0, LO, [(w[:], x[:, L * a:L * a + L]) for a in (2 * k, 2 * k + 1)], ["wi", "w127", "w128", key + str(k)],
+                name == parts[0], name == parts[-1])
+        step("sb")
+        move(WHO["sb"], T.sb[:], ps[0][:, LO], ["B0"], ["sb"])
+        step("ox")
+        ts(T.ox[:], T.sb[:], -1288.0, T.thr[:, 0:1], A.add, A.is_gt, ["sb", "thr"], ["ox"])
+        step("u")
+        mms(0, UP, [(T.wu[:], T.sb[:])], ["wu", "sb"])
+        step("h16")
+        if WHO["h16"] == "s":
+            act(T.h16[:], ps[0][:, UP], F.Identity, ["B0"], ["h16"], bias=24576.0 - 7.5)
+        else:
+            ts(T.h16[:], ps[0][:, UP], 24576.0 - 7.5, None, A.add, None, ["B0"], ["h16"])
+        step("m16")
+        mms(0, LO, [(T.wu[:], T.sb[:]), (T.wneg[:], T.h16[:])], ["wu", "sb", "wneg", "h16"])
+        step("oh")
+        ts(T.oh[:, LO], ps[0][:, LO], cf[:, 5:6], cf[:, 6:7], A.max, A.is_equal, ["B0", "cf5", "cf6"], ["oh0"])
+        cpy(T.oh[:, UP], T.oh[:, LO], ["oh0"], ["oh"])
+        for k in in_order("y", range(4)):
+            e, b, c = TILES[k], TILE_BANKS[k], slice(V * k, V * k + V)
+            step("t%d" % k)
+            mms(b, ALL, [(T.wi[:], T.xp[:, c])] + [(T.wi[:], T.xl[:, c])] * (k == APART), ["wi", "xp%d" % k, "xl%d" % k], True, False)
+            step("o%d" % k)
+            for h in (LO, UP):
+                mms(b, h, [(T.w16[:], T.ox[:])], ["w16", "ox"], False, h == UP)
+            step("y%d" % k)
+            relu(e, T.yy[:, c], ps[b][:], -16.0, ["B%d" % b], ["yy%d" % k])
+        for name, b, m in (("P", 3, 3), ("F", 4, 0)):
+            units = in_order(name, range(4))
+            for k in units:
+                step("%s%d" % (name, k))
+                mms(b, LO, [(into_row(m, a), T.yy[:, L * a:L * a + L]) for a in (2 * k, 2 * k + 1)], ["bm%d" % m, "yy%d" % k],
+                    k == units[0], b == 3 and k == units[-1])
+        step("hb")
+        act(T.hb[:], ps[3][:, LO], F.Identity, ["B3"], ["hb"], bias=129.0 - 63.5 / 128)
+        step("Fh")
+        mms(4, LO, [(T.wh[:], T.hb[:])], ["wh", "hb"], False, True)
+        step("uT")
+        mms(0, TINY, [(into_row(2, r), T.sb[:, r:L:16]) for r in range(16)], ["bm2", "sb"])
+        step("bit")
+        ts(T.ri[:], ps[0][:, TINY], 1.0 / 64, None, A.add, None, ["B0"], ["ri"])
+        tt(T.bt[:], ps[0][:, TINY], T.ri[:], A.is_lt, ["B0", "ri"], ["bt"])
+        tt(T.bd[:], T.bt[:], T.dh[:], A.mult, ["bt", "dh"], ["bd"])
+        step("Y0")
+        mms(0, TINY, [(T.wi[:], T.h0[:]), (T.wi[:], T.bd[:])], ["wi", "h0", "bd"], True, False)
+        step("n0")
+        mms(NB, TINY, [(into_row(0, r), T.hio[:, r:L:16]) for r in range(16)], ["bm0", "hio"], True, False)
+        step("hot")
+        act(T.hot[:], ps[4][:, LO], F.Sigmoid, ["B4", "ths"], ["hot"], bias=T.ths[:, t:t + 1], scale=65536.0)
+        step("top")
+        mms(5, LO, [(T.wtop[:], T.hot[:])], ["wtop", "hot"], False, True)
+        step("hi")
+        act(T.hi[:], ps[5][:, LO], F.Sign, ["B5"], ["hi"], bias=-HIGH)
+        step("lv")
+        move(WHO["lv"], lanes, ps[5][:, LO], ["B5"], [sk[q]])
+        step("sendb")
+        send(-shift, T.lb[:, 2 * V * t:2 * V * t + V], T.lv[:, ALL], "ab%d" % t, "sb_", sk, "lb%d" % t)
+        step("n1")
+        mms(NB, TINY, [(into_row(0, r), T.hi[:, r:L:16]) for r in range(16)], ["bm0", "hi"], False, True)
+        step("ind")
+        act(T.ind[:], ps[NB][:, TINY], F.Relu, ["B%d" % NB], ["ind", "acc"], bias=9.0 if WHO["hio"] == "v" else 1.0, scale=-1.0,
+            acc=None if last else T.acc[:, 0:1])
+        step("Y1")
+        mms(0, TINY, [(T.w512[:], T.ind[:])], ["w512", "ind"], False, True)
+        step("idx")
+        cpy(idx, ps[0][:, TINY], ["B0"], ["idx%d" % t])
+        step("sendi")
+        send(shift, got, idx, "ai%d" % t, "si", ["idx%d" % t], "li%d" % t)
+        if not last:
+            step("A")
+            mms(3, slice(0, 1), [(T.wa[:], T.acc[:, 0:1])], ["wa", "acc"])
+            step("f8")
+            act(T.f8[:, 0:1], ps[3][:, 0:1], F.Identity, ["B3"], ["f8"], bias=1288.0 - 3.5)
+            step("thr")
+            ts(T.thr[:, 0:1], ps[3][:, 0:1], T.capf[:, 0:1], T.f8[:, 0:1], A.add, A.subtract, ["B3", "capf", "f8"], ["thr"])
+        else:
+            step("wr0")
+            scaled([("wwrap", -W / 2.0), ("wif", 1.0), ("wlog", 1.0 / (16.0 * LN2))])
+            act(T.sg[:], T.pw[:, PAD:PAD + V], F.Sign, ["pw"], ["sg"], bias=0.5)
+            step("wr1")
+            mms(3, ALL, [(T.wif[:], T.pw[:, PAD:PAD + V])], ["wif", "pw"], True, False)
+            mms(3, ALL, [(T.wwrap[:], T.sg[:])], ["wwrap", "sg"], False, True)
+            step("wr2")
+            act(T.op[:, ALL], ps[3][:], F.Identity, ["B3"], ["op"], bias=W / 2.0)
+        steps = ["stp", "se"] if t else ["stp"]
+        for k, e in enumerate(STEPS):
+            c = slice(V * k, V * k + V)
+            win = T.sw[:, 0:wide].indirect(T.offa[:, 32 * k:32 * k + 32])
+            step("z%d" % k)
+            if e == "v":
+                tt(T.zg[:, c], win, T.oh[:], A.mult, steps + ["offa%d" % (k // 4), "oh"], ["zg%d" % k])
+            else:
+                b = 1 + k % 2
+                act(T.zu[:, c], win, F.Identity, steps + ["offa%d" % (k // 4)], ["zu%d" % k])
+                step("w%d" % k)
+                mms(b, ALL, [(T.w256[:], T.oh[:]), (T.wi[:], T.zu[:, c])], ["w256", "wi", "oh", "zu%d" % k])
+                step("r%d" % k)
+                relu("s" if e == "s" else "v", T.zg[:, c], ps[b][:], -256.0, ["B%d" % b], ["zg%d" % k])
+        halves = in_order("tt", range(2))
+        for h in halves:
+            picks = in_order("", ["k%d" % k for k in range(4 * h, 4 * h + 4)] + ["hx%d" % h])
+            c, b = (LO, UP)[h], PICK_BANKS[h]
+            for name in picks:
+                step(name)
+                k = int(name[-1])
+                if name[0] == "k":
+                    mms(b, LO, [(into_row((1, 4)[h], a), T.zg[:, L * a:L * a + L]) for a in (2 * k, 2 * k + 1)],
+                        ["bm1", "bm4", "zg%d" % k], name == picks[0], name == picks[-1])
+                else:
+                    mms(b, LO, [((T.wxa, T.wxb)[h][:], T.hi[:])], ["wxa", "wxb", "hi"], name == picks[0], name == picks[-1])
+            step("tt%d" % h)
+            relu(WHO["tt"][h], T.tt[:, c], ps[b][:, LO], -128.0, ["B%d" % b], ["tt%d" % h])
+            step("j%d" % h)
+            mms(7, LO, [((T.wja, T.wjb)[h][:], T.tt[:, c])], ["wja", "wjb", "tt%d" % h], h == halves[0], h == halves[1])
+        step("ch")
+        tt(T.ch[:], ps[7][:, LO], places, A.add, ["B7", "pw"], ["ch"])
+        child, ck = T.ch, "ch"
+        if last:
+            ts(T.ck[:], T.ch[:], 0.0, float(W), A.is_lt, A.mult, ["ch"], ["ck"])
+            tt(T.cw[:], T.ch[:], T.ck[:], A.add, ["ch", "ck"], ["cw"])
+            child, ck = T.cw, "cw"
+        step("sendm")
+        send(shift, T.lm[:, L * t:L * t + L], child[:], "am%d" % t, "sm", [ck], "lm%d" % t)
+        step("zero")
+        cpy(T.lv[:, 0:2 * V].indirect(got), zeros, ["li%d" % t, "lz0"], sk)
+        step("sel")
+        act(T.sel[:], T.lb[:, 2 * V * t:2 * V * (t + 1)].indirect(idx), F.Identity, ["lb%d" % t, "lz%d" % t, "idx%d" % t], ["sel"],
+            scale=DOWN)
+        step("max")
+        tt(lanes, lanes, T.sel[:], A.max, [sk[q], "sel"], [sk[q]])
+        if last:
+            decode(1 - q, 1)
+            decode(q, 2)
+        else:
+            climb(1 - q, CLIMB)
+        step("put")
+        if last:
+            cpy(T.op[:, 0:2 * V].indirect(got), T.lm[:, L * t:L * t + L], ["li%d" % t, "lm%d" % t], ["op"])
+        else:
+            cpy(T.pw[:, PAD:PAD + 2 * V].indirect(got), T.lm[:, L * t:L * t + L], ["li%d" % t, "lm%d" % t], ["pw", "padb"])
+
+    step("out")
+    dma("s", T.ymk[:], T.om[:, ALL], "o2", ["om0", "om1"], [])
+    dma("y", T.ypl[:], T.op[:, ALL], "o1", ["op"], [])
     emit()
-    for sem in ("sb_", "sn", "so", "sk", "cg", "cp_", "cs", "cv", "o1", "o2"):
+    for sem in ("sb_", "sm", "si", "cg", "cp_", "cs", "cv", "o1", "o2"):
         g.wait_ge(T.sem[sem], cnt[sem])

@@ -14,11 +14,11 @@ def _s(n, d):
 SCRATCH = {
     "xw": _s(WX, BF), "sw": _s(WX, BF), "pli": _s(V, I32), "sui": _s(V, I32), "mki": _s(V, BF),
     "hpi": _s(32, I32), "cpi": _s(8, I32), "thi": _s(8, I32),
-    "io1": _s(128, F32), "iob": _s(128, F32), "ioh": _s(128, F32), "iow": _s(128, F32), "pcol": _s(8, I32), "ci": _s(8, I32),
+    "io1": _s(16, F32), "iob": _s(128, F32), "w0": _s(128, BF), "pcol": _s(8, I32), "ci": _s(8, I32),
     "cf": _s(24, F32), "wi": _s(128, BF), "wif": _s(128, F32), "wim": _s(128, BF), "w128": _s(128, BF), "w256": _s(128, BF),
     "w512": _s(128, BF), "wneg": _s(128, BF), "w16": _s(128, BF), "w127": _s(128, BF), "wtop": _s(128, BF), "wwrap": _s(128, BF),
-    "wlog": _s(128, F16), "wu": _s(128, BF), "wa": _s(128, F32), "wh": _s(128, BF), "wh0": _s(128, BF), "wh1": _s(128, BF),
-    "wja": _s(128, BF), "wjb": _s(128, BF), "wxa": _s(128, BF), "wxb": _s(128, BF), "e8": _s(8, BF), "bm": _s(720, BF),
+    "wlog": _s(128, F16), "wu": _s(128, BF), "wa": _s(128, F32), "wh": _s(128, BF),
+    "wja": _s(128, BF), "wjb": _s(128, BF), "wxa": _s(128, BF), "wxb": _s(128, BF), "bm": _s(720, BF),
     "capf": _s(8, BF), "ths": _s(8, F32), "thr": _s(8, F32), "f8": _s(8, BF),
     "acc": _s(8, F32), "h0": _s(16, F16), "dh": _s(16, F32),
     "glist": _s(16, U16), "suu": _s(V, U16), "offa": _s(L, U16), "idx": _s(RO * 16, U16),
@@ -28,7 +28,7 @@ SCRATCH = {
     "hi": _s(L, BF), "hio": _s(L, BF), "ri": _s(16, I32), "bt": _s(16, BF), "bd": _s(16, F16), "ind": _s(16, BF),
     "tt": _s(V, F16), "ch": _s(L, F16), "ck": _s(L, F16), "cw": _s(L, F16), "sel": _s(L, BF),
     "lm": _s(RO * L, F16), "lb": _s(RO * 2 * V, BF), "li": _s(RO * 16, U16),
-    "da": _s(2 * V, BF), "la": _s(2 * V, F16), "om": _s(V, BF), "sg": _s(V, BF), "op": _s(2 * V, F32),
+    "da": _s(3 * V, BF), "la": _s(3 * V, F16), "om": _s(2 * V, BF), "sg": _s(V, BF), "op": _s(2 * V, F32),
 }
 for _k in range(8):
     SCRATCH["ps%d" % _k] = ("psum", [128, 512], F32)
@@ -42,15 +42,22 @@ DOWN = 2.0 ** -64
 HIGH = 4.0
 ROUND = 1.5 * 2.0 ** 23
 APART = 3
-CLIMB0, CLIMB = "svsvsvsv", "vsvsssss"
-TILES = "vvss"
-TILE_BANKS, PICK_BANKS, NB = [1, 2, 1, 6], [6, 4], 7
-STEPS = "vvvvvsss"
-WHO = {"sb": "v", "h16": "v", "lv": "s", "hio": "v", "tt": "sv"}
-ORDER = ("sa sc n0 tr q1< c4< al0 al1 hi3 lo0 q2< lo1 Sl0 hi0 Sh3 lo2 Sl1 hi1 Sh0 t0 lo3 hi2 Sh1 Sl2 va z5 Sl3 Sh2 t1 sb z6 t3 sd "
-         "ox u o0 h16 o3 y0 o1 y3 q3< y1 t2 o2 m16 y2 F0 oh P0 vc z7 P1 P3 z2 P2 F2 hb F3 vb z1 F1 Fh w5 hot z0 top r5 uT w6 hi bit "
-         "lv n1 z3 sendb w7 ind r6 hx1 k5 r7 Y0 Y1 A k0 idx z4 k3 sendi k6 hx0 k2 k7 k1 k4 tt0 wr0 tt1 f8 j0 j1 wr1 ch sel zero "
-         "sendm wr2 max old c0 c7 da1 db1 c2 c6 da2 c1 hio put c3 q0 thr c5 db2 out dc1 dc2").split()
+CLIMB0 = [("s", 32), ("v", 32), ("s", 32), ("v", 32), ("s", 48), ("v", 48), ("s", 32)]
+CLIMB = [("v", 16), ("s", 48), ("v", 64), ("s", 64), ("s", 64)]
+TILES = "mmss"
+TILE_BANKS, PICK_BANKS, NB = [1, 1, 2, 6], [6, 4], 7
+STEP_BANKS, AB = [1, 2, 1, 2, 1, 2, 1, 2], 3
+STEPS = "hvvvvsss"
+WHO = {"sb": "v", "h16": "v", "lv": "v", "hio": "s", "tt": "sv", "oh": "s"}
+ORDER = {
+    "v": "tr al0 al1 lo3 hi0 hi1 hi2 c0< vb va ox sb y0 h16 y1 oh z0 z3 b0 z2 b1 b2 z1 da1 idx ve z4 vc tt1 thr ch da2 dc1 zero "
+         "max dc2 mx vh su0 vd su1 a1 a3 pw a5 c2 put".split(),
+    "s": "lo0 lo1 lo2 hi3 sa z6 y2 y3 z7 hb oh2 hot z5 hi lv r5 ind r6 r7 tt0 f8 se db1 sel wr0 a6 hio db2 wr2 a4 a0 a2 c1 c4 c3 "
+         "out".split(),
+    "p": "n0 q1< q3< q2< Sl0 Sl3 Sh0 Sl1 Sh1 Sl2 Sh3 Sh2 t3 t2 o0 o2 o3 u q0< P0 F0 m16 P2 P3 P1 F2 F1 F3 Fh x6 uT w5 top w6 x5 k0 "
+         "n1 hx0 k2 Y0 Y1 x7 w7 k3 k1 k5 hx1 k6 k7 k4 j0 A wp j1 old db1 wr1 db2".split(),
+    "g": "gb sendb sendi sendm lz".split(),
+}
 
 
 def rank_program(g, core, T, topo):
@@ -64,13 +71,16 @@ def rank_program(g, core, T, topo):
     known = {q: {} for q in Q}
     writer, readers = {}, {}
     ops = []
-    now = [(-1, 0), -1]
+    now = [None, -1]
 
     def step(name):
-        now[0] = (now[1] + 1, ORDER.index(name + "<")) if name + "<" in ORDER else (now[1], ORDER.index(name))
+        now[0] = name
 
-    def in_order(name, ks):
-        return sorted(ks, key=lambda k: ORDER.index(name + str(k)))
+    def place(q):
+        order = ORDER.get("g" if q is None else q)
+        if now[0] is None or order is None:
+            return (now[1], -1)
+        return (now[1] + 1, order.index(now[0] + "<")) if now[0] + "<" in order else (now[1], order.index(now[0]))
 
     def wait(q, tok):
         sem, n, clock = tok
@@ -83,14 +93,16 @@ def rank_program(g, core, T, topo):
                 known[q][s2] = n2
 
     def record(q, kind, what, r, w):
-        w = w + [k for k in r if k[0] == "B"]
         deps = set(writer[k] for k in r if k in writer)
+        for k in r:
+            if k[0] == "B":
+                deps.update(i for i in readers.get(k, []) if ops[i][0] != q)
         for k in w:
             if k in writer:
                 deps.add(writer[k])
             deps.update(readers.get(k, []))
         me = len(ops)
-        ops.append((q, kind, what, now[0], sorted(deps)))
+        ops.append((q, kind, what, place(q), sorted(deps)))
         for k in r:
             readers.setdefault(k, []).append(me)
         for k in w:
@@ -102,16 +114,10 @@ def rank_program(g, core, T, topo):
         for i, o in enumerate(ops):
             for d in o[4]:
                 after[d].append(i)
-        left = [len(o[4]) for o in ops]
-        ready = [i for i in range(len(ops)) if left[i] == 0]
+        todo = {q: sorted((i for i, o in enumerate(ops) if o[0] == q), key=lambda i: (ops[i][3], i), reverse=True) for q in [None, *Q]}
         tok = {}
-        while ready:
-            i = min(ready, key=lambda k: (ops[k][3], k))
-            ready.remove(i)
-            for j in after[i]:
-                left[j] -= 1
-                if left[j] == 0:
-                    ready.append(j)
+        while any(todo.values()):
+            i = [l for l in todo.values() if l and all(d in tok for d in ops[l[-1]][4])][0].pop()
             q, kind, what, _, deps = ops[i]
             if kind == "arrival":
                 tok[i] = what + ({},)
@@ -178,12 +184,19 @@ def rank_program(g, core, T, topo):
     def iota(out, pattern, w):
         op("g", lambda: g.iota(out, pattern, 0, 0, allow_small_or_imprecise_dtypes=True), [], w)
 
-    def mms(bank, c, pairs, r, start=True, stop=True):
+    def mms(bank, c, pairs, r, start=True, stop=True, group=None):
         out = ps[bank][:, c]
 
         def call():
-            return [g.tensor.matmul(out, a, b, start and k == 0, stop and k == len(pairs) - 1) for k, (a, b) in enumerate(pairs)][-1]
-        op("p", call, r, ["B%d" % bank])
+            first, final = start, stop
+            if group:
+                first, final = not group[1], group[0] == 1
+                group[0], group[1] = group[0] - 1, True
+            return [g.tensor.matmul(out, a, b, first and k == 0, final and k == len(pairs) - 1) for k, (a, b) in enumerate(pairs)][-1]
+        if group:
+            op("p", call, r + ["B%d" % bank], [])
+        else:
+            op("p", call, r, ["B%d" % bank])
 
     def send(shift, out, in_, arr, loc, r, key):
         dst, src = T.cores[(rank + shift) % N], T.cores[(rank - shift) % N]
@@ -200,32 +213,24 @@ def rank_program(g, core, T, topo):
         return T.bm[:, 144 * m + 15 - a:144 * m + 143 - a]
 
     for qq, out, in_, name in (
-            ("y", T.mki[:], T.mk[:], "mk"), ("y", T.sui[:, LO], T.su[:, LO], "su0"), ("y", T.sui[:, UP], T.su[:, UP], "su1"),
-            ("y", T.pli[:], T.pl[:], "pl"), ("y", T.xw[:, 0:W], T.xf[:], "xf"), ("y", T.cpi[:, 0:1], T.cp[:], "cp"),
-            ("y", T.thi[:, 0:5], T.th[:], "th"), ("y", T.hpi[:], T.hp[:], "hp"), ("y", T.sw[:, 0:W], T.stp[:], "stp"),
+            ("y", T.hpi[:], T.hp[:], "hp"), ("y", T.mki[:], T.mk[:], "mk"), ("y", T.sui[:, LO], T.su[:, LO], "su0"),
+            ("y", T.sui[:, UP], T.su[:, UP], "su1"), ("y", T.pli[:], T.pl[:], "pl"), ("y", T.xw[:, 0:W], T.xf[:], "xf"),
+            ("y", T.cpi[:, 0:1], T.cp[:], "cp"), ("y", T.thi[:, 0:5], T.th[:], "th"), ("y", T.sw[:, 0:W], T.stp[:], "stp"),
             ("y", T.xw[:, W:WX], T.xf[:, 0:WX - W], "xe"), ("y", T.sw[:, W:WX], T.stp[:, 0:WX - W], "se")):
         dma(qq, out, in_, "l" + name, [], [name])
 
     op("g", lambda: g.iota(T.pcol[:, 0:1], [[0, 1]], 0, 1), [], ["pcol"])
-    iota(T.io1[:], [[1, 128]], ["io1"])
+    iota(T.io1[:], [[1, 16]], ["io1"])
     iota(T.iob[:], [[1, 8], [0, 16]], ["iob"])
-    iota(T.ioh[:], [[16, 8], [0, 2], [1, 8]], ["ioh"])
-    iota(T.iow[:], [[0, 8], [1, 2], [0, 8]], ["iow"])
-    for t in range(RO):
-        iota(T.lb[:, 2 * V * t + V:2 * V * (t + 1)], [[0, V]], ["lz%d" % t])
     zeros = T.lb[:, V:V + L]
-    fill(T.bm[:], 0.0, ["bm0", "bm1", "bm2", "bm3", "bm4"])
+    fill(T.w0[:], 0.0, ["w0"])
     fill(T.pw[:, 0:PAD], 0.0, ["pada"])
-    fill(T.pw[:, PAD + V:2 * PAD + V], 0.0, ["padb"])
-    g8 = T.io1[:, 0:8]
-    cpy(cf[:, 0:1], T.pcol[:, 0:1], ["pcol"], ["cf0"])
     ts(ci[:, 0:1], T.pcol[:, 0:1], 15, None, A.bitwise_and, None, ["pcol"], ["ci0"])
     ts(ci[:, 1:2], T.pcol[:, 0:1], 4, None, A.logical_shift_right, None, ["pcol"], ["ci1"])
-    ts(T.wi[:], T.io1[:], cf[:, 0:1], None, A.is_equal, None, ["io1", "cf0"], ["wi"])
-    ts(ci[:, 2:3], T.pcol[:, 0:1], 119, None, A.bitwise_and, None, ["pcol"], ["ci2"])
+    fill(T.pw[:, PAD + V:2 * PAD + V], 0.0, ["padb"])
+    cpy(cf[:, 1:3], ci[:, 0:2], ["ci0", "ci1"], ["cf1"])
     tt(ci[:, 3:4], ci[:, 0:1], ci[:, 1:2], A.add, ["ci0", "ci1"], ["ci3"])
     ts(ci[:, 5:6], ci[:, 0:1], 2.0, 9.0, A.mult, A.add, ["ci0"], ["ci5"])
-    cpy(cf[:, 1:4], ci[:, 0:3], ["ci0", "ci1", "ci2"], ["cf1"])
     ts(ci[:, 4:5], ci[:, 3:4], 1, None, A.bitwise_and, None, ["ci3"], ["ci4"])
     ts(ci[:, 6:7], ci[:, 5:6], 15, None, A.bitwise_and, None, ["ci5"], ["ci6"])
 
@@ -233,39 +238,59 @@ def rank_program(g, core, T, topo):
         for name, c in names:
             act(T[name][:], T.wi[:], F.Identity, ["wi"], [name], scale=c)
 
-    scaled([("wim", DOWN), ("w256", 256.0)])
     act(cf[:, 11:12], cf[:, 1:2], F.Sigmoid, ["cf1"], ["cf11"], bias=7.5 * 256, scale=-256.0)
-    ts(cf[:, 4:5], cf[:, 1:2], 0.0, None, A.is_equal, None, ["cf1"], ["cf4"])
+    ts(cf[:, 4:5], cf[:, 1:2], 0.0, 100.0, A.is_equal, A.mult, ["cf1"], ["cf4"])
     ts(cf[:, 9:10], ci[:, 4:5], 17.0, cf[:, 1:2], A.mult, A.add, ["ci4", "cf1"], ["cf9"])
     ts(cf[:, 13:14], ci[:, 6:7], -8.0, None, A.add, None, ["ci6"], ["cf13"])
-    ts(cf[:, 5:6], cf[:, 4:5], 99.0, 1.0 - 24576.0, A.mult, A.add, ["cf4"], ["cf5"])
+    ts(cf[:, 5:6], cf[:, 4:5], 1.0, -24576.0, A.max, A.add, ["cf4"], ["cf5"])
     ts(cf[:, 10:11], cf[:, 9:10], 16.0, None, A.mult, None, ["cf9"], ["cf10"])
     ts(cf[:, 7:8], cf[:, 1:2], 1.0 / 16, 1.0 / 32, A.mult, A.add, ["cf1"], ["cf7"])
-    ts(cf[:, 8:9], cf[:, 1:2], 1.0, None, A.min, None, ["cf1"], ["cf8"])
-    ts(cf[:, 12:13], cf[:, 1:2], 8.0, None, A.is_ge, None, ["cf1"], ["cf12"])
-    ts(T.glist[:], T.io1[:, 0:16], cf[:, 10:11], None, A.add, None, ["io1", "cf10"], ["glist"])
-    ts(cf[:, 6:7], cf[:, 1:2], -24576.0, cf[:, 5:6], A.add, A.max, ["cf1", "cf5"], ["cf6"])
-    ts(cf[:, 14:15], cf[:, 12:13], -65536.0 * 129 - 256.0 * 258, 65536.0 * 129 + 128, A.mult, A.add, ["cf12"], ["cf14"])
-    ts(T.e8[:], g8, cf[:, 2:3], None, A.is_equal, None, ["io1", "cf1"], ["e8"])
+    ts(cf[:, 6:7], cf[:, 4:5], cf[:, 1:2], -24576.0, A.add, A.add, ["cf1", "cf4"], ["cf6"])
+    ts(T.glist[:], T.io1[:], cf[:, 10:11], None, A.add, None, ["io1", "cf10"], ["glist"])
     ts(T.wu[:], T.iob[:], cf[:, 2:3], cf[:, 13:14], A.is_equal, A.mult, ["iob", "cf1", "cf13"], ["wu"])
-    ts(T.wh0[:], T.ioh[:], cf[:, 3:4], None, A.is_equal, None, ["ioh", "cf1"], ["wh0"])
-    ts(T.wh1[:], T.iow[:], 0.5 + 1.0 / 256, -0.5, A.mult, A.add, ["iow"], ["wh1"])
-    ts(T.wa[:], T.iob[:], cf[:, 2:3], -1.0, A.is_equal, A.mult, ["iob", "cf1"], ["wa"])
-    tt(T.wjb[:], T.wh0[:], T.iow[:], A.mult, ["wh0", "iow"], ["wjb"])
-    tt(T.wh[:], T.wh0[:], T.wh1[:], A.mult, ["wh0", "wh1"], ["wh"])
-    ts(T.wxa[:], T.wh0[:], 128.0, None, A.mult, None, ["wh0"], ["wxa"])
-    tt(T.wja[:], T.wh0[:], T.wjb[:], A.subtract, ["wh0", "wjb"], ["wja"])
-    tt(T.wh1[:], T.w256[:], T.wxa[:], A.subtract, ["w256", "wxa"], ["wh1", "wx"])
-    SPREAD = ((0, 15, 0.5, "cf1"), (2, 15, cf[:, 7:8], "cf7"), (3, 15, cf[:, 11:12], "cf11"), (3, 23, cf[:, 12:13], "cf12"),
-              (1, 15, cf[:, 8:9], "cf8"), (1, 23, cf[:, 4:5], "cf4"), (4, 15, cf[:, 8:9], "cf8"), (4, 7, cf[:, 4:5], "cf4"))
+
+    def select(out, in_, pattern, cmp, c, base, mult, r, w):
+        op("g", lambda: g.affine_select(out, in_, pattern, cmp, c, base, mult), r, w)
+
+    def matrix(name, entries):
+        for n, (c, k, m) in enumerate(entries):
+            pattern, base = ([[-1, 128]], 0) if k is None else ([[-16, 8], [1000, 2], [-1, 8]], -8 * k - 1000 * m)
+            select(T[name][:], T[name if n else "w0"][:], pattern, A.not_equal, c, base, 1, ["w0", name], [name])
+
+    def rows(m, entries):
+        cols = [T.bm[:, 144 * m + o:144 * m + o + 113:16] for o, c, lo, hi in entries]
+        for col, (o, c, lo, hi) in zip(cols, entries):
+            select(col, col, [[16, 8]], A.is_gt, c, lo, -1, ["bm"], ["bm%d_%d" % (m, o)])
+        for col, (o, c, lo, hi) in zip(cols, entries):
+            select(col, col, [[16, 8]], A.is_ge, 0.0, hi, -1, ["bm"], ["bm%d_%d" % (m, o)])
+
+    matrix("wi", [(1.0, None, None)])
+    matrix("wim", [(DOWN, None, None)])
+    iota(T.bm[:], [[0, 720]], ["bm"])
+    rows(0, [(15, 0.5, 0, 15)])
+    for name, c in (("w127", 127.0), ("w128", 128.0), ("w16", 16.0), ("wneg", -1.0)):
+        matrix(name, [(c, None, None)])
+    rows(3, [(15, 1.0, 0, 7), (23, 1.0, 8, 15)])
+    matrix("wh", [(-0.5, 0, 0), (-0.5, 1, 0), (1.0 / 256, 0, 1), (1.0 / 256, 1, 1)])
+
+    def late_matrices():
+        step("gb")
+        matrix("w256", [(256.0, None, None)])
+        rows(1, [(15, 1.0, 1, 15), (23, 1.0, 0, 0)])
+        rows(4, [(15, 1.0, 1, 15), (7, 1.0, 0, 0)])
+        matrix("w512", [(512.0, None, None)])
+        matrix("wxa", [(128.0, 0, 0), (-128.0, 0, 1)])
+        matrix("wxb", [(128.0, 1, 1), (-128.0, 1, 0)])
+        matrix("wja", [(1.0, 0, 0), (1.0, 1, 0)])
+        matrix("wjb", [(1.0, 0, 1), (1.0, 1, 1)])
 
     act(T.enc[:], T.mki[:], F.Sigmoid, ["mk"], ["enc"], bias=-125.0 * LN2, scale=8.0 * LN2)
     act(T.lv[:, ALL], T.enc[:], F.Square, ["enc"], ["lv0", "lv1"], scale=2.0 ** 63)
     for h in range(2):
+        step("su%d" % h)
         cpy(T.suu[:, 128 * h:128 * h + 128], T.sui[:, L * h:L * h + L:2], ["su%d" % h], ["suu0%d" % h])
 
-    def climb(q, engines):
-        n = L // len(engines)
+    def climb(q, calls, name="c"):
         lanes = T.lv[:, q:V:2]
         step("hio")
         if WHO["hio"] == "v":
@@ -274,32 +299,39 @@ def rank_program(g, core, T, topo):
             act(T.hio[:], lanes, F.Sign, ["lv%d" % q], ["hio"], bias=HIGH, scale=-1.0)
         step("old")
         mms(5, LO, [(T.wi[:], lanes)], ["wi", "lv%d" % q], True, False)
-        for k, e in enumerate(engines):
-            o = L * q + n * k
-            step("c%d" % k)
-            move(e, T.mg[:, 16 * n * k:16 * n * (k + 1)], T.lv[:, ALL].indirect(T.suu[:, o:o + n]),
-                 ["lv0", "lv1", "suu%d%d" % (q, n * k // 128)], ["mg%d" % k])
-        per = len(engines) // 4
+        o = 0
+        for k, (e, n) in enumerate(calls):
+            step("%s%d" % (name, k))
+            move(e, T.mg[:, 16 * o:16 * (o + n)], T.lv[:, ALL].indirect(T.suu[:, L * q + o:L * q + o + n]),
+                 ["lv0", "lv1", "suu%d%d" % (q, o // 128), "suu%d%d" % (q, (o + n - 1) // 128)],
+                 ["mg%d" % j for j in range(o // 16, (o + n) // 16)])
+            o += n
+        rise = [5, True]
         for k in range(4):
             step("q%d" % k)
             mms(5, slice(64 * k, 64 * k + 64), [(T.wim[:], T.mg[:, 1024 * k + a:1024 * k + 1024:16]) for a in range(16)],
-                ["wim"] + ["mg%d" % j for j in range(k * per, (k + 1) * per)], False, False)
+                ["wim"] + ["mg%d" % j for j in range(4 * k, 4 * k + 4)], group=rise)
+        return rise
 
-    def decode(k, bank):
-        a, b = slice(V * k, V * k + L), slice(V * k + L, V * k + V)
-        src, key = T.lv[:, k:V:2], "lv%d" % k
-        step("da%d" % bank)
-        ts(T.da[:, a], src, 2.0 ** -124, 2.0 ** -4, A.max, A.min, [key], ["da%d" % k])
-        ts(T.da[:, b], src, 2.0 ** -4, None, A.max, None, [key], ["db%d" % k])
-        step("db%d" % bank)
+    def decode(k, src, keys, out, n):
+        a, b = slice(2 * V * (k - 1), 2 * V * (k - 1) + n), slice(2 * V * (k - 1) + n, 2 * V * (k - 1) + 2 * n)
+        step("da%d" % k)
+        ts(T.da[:, a], src, 2.0 ** -124, 2.0 ** -4, A.max, A.min, keys, ["da%d" % k])
+        ts(T.da[:, b], src, 2.0 ** -4, None, A.max, None, keys, ["db%d" % k])
+        step("db%d" % k)
         act(T.la[:, a], T.da[:, a], F.Ln, ["da%d" % k], ["la%d" % k], scale=2.0 ** 64.25)
         act(T.la[:, b], T.da[:, b], F.Ln, ["db%d" % k], ["lc%d" % k], scale=2.0 ** -55.5)
-        mms(bank, LO, [(T.wlog[:], T.la[:, a]), (T.wlog[:], T.la[:, b])], ["wlog", "la%d" % k, "lc%d" % k])
-        step("dc%d" % bank)
-        ts(T.om[:, k:V:2], ps[bank][:, LO], ROUND + 7.0, -ROUND, A.add, A.add, ["B%d" % bank], ["om%d" % k])
+        mms(k, slice(0, n), [(T.wlog[:], T.la[:, a]), (T.wlog[:], T.la[:, b])], ["wlog", "la%d" % k, "lc%d" % k])
+        step("dc%d" % k)
+        ts(out, ps[k][:, 0:n], ROUND + 7.0, -ROUND, A.add, A.add, ["B%d" % k], ["om%d" % k])
 
-    climb(0, CLIMB0)
-    step("put")
+    step("vd")
+    ts(T.bm[:, 303:416:16], T.io1[:, 0:8], cf[:, 2:3], cf[:, 7:8], A.is_equal, A.mult, ["io1", "cf1", "cf7", "bm"], ["bm2_15"])
+    step("vh")
+    cpy(T.h0[:], T.hpi[:, 0:16], ["hp"], ["h0"])
+    tt(T.dh[:], T.hpi[:, 16:32], T.hpi[:, 0:16], A.subtract, ["hp"], ["dh"])
+    rise = climb(0, CLIMB0, "a")
+    step("pw")
     ts(T.pw[:, PAD:PAD + V], T.pli[:], -float(W), None, A.add, None, ["pl"], ["pw"])
     for t in range(RO):
         now[1] = t
@@ -322,48 +354,49 @@ def rank_program(g, core, T, topo):
         if t == 0:
             step("va")
             ts(T.thr[:, 0:1], T.cpi[:, 0:1], -1288.0, None, A.add, None, ["cp"], ["thr"])
+            step("sa")
+            act(cf[:, 14:15], cf[:, 11:12], F.Identity, ["cf11"], ["cf14"], bias=128.0 - 256 * 258, scale=65536.0 * 129 + 256 * 258)
+            act(T.wtop[:], T.wi[:], F.Square, ["wi"], ["wtop"], scale=2.0 ** 58)
+            step("se")
+            scaled([("wif", 1.0), ("wwrap", -W / 2.0), ("wlog", 1.0 / (16.0 * LN2))])
             step("vb")
             ts(T.ths[:, 0:5], T.thi[:, 0:5], -256.0, cf[:, 14:15], A.mult, A.add, ["th", "cf14"], ["ths"])
-            cpy(T.h0[:], T.hpi[:, 0:16], ["hp"], ["h0"])
-            tt(T.dh[:], T.hpi[:, 16:32], T.hpi[:, 0:16], A.subtract, ["hp"], ["dh"])
+            step("ve")
+            ts(T.wa[:], T.iob[:], cf[:, 2:3], -1.0, A.is_equal, A.mult, ["iob", "cf1"], ["wa"])
             step("vc")
             cpy(T.capf[:, 0:1], T.cpi[:, 0:1], ["cp"], ["capf"])
             cpy(T.suu[:, UP], T.sui[:, 1:V:2], ["su0", "su1"], ["suu10", "suu11"])
-            step("sa")
-            scaled([("w127", 127.0), ("w128", 128.0)])
-            step("sc")
-            scaled([("w16", 16.0), ("wneg", -1.0)])
-            for m, o, c, key in SPREAD[:4]:
-                act(T.bm[:, 144 * m + o:144 * m + o + 113:16], T.e8[:], F.Identity, ["e8", key], ["bm%d" % m], scale=c)
-            act(T.wtop[:], T.wi[:], F.Square, ["wi"], ["wtop"], scale=2.0 ** 58)
-            step("sd")
-            scaled([("w512", 512.0)])
-            for m, o, c, key in SPREAD[4:]:
-                act(T.bm[:, 144 * m + o:144 * m + o + 113:16], T.e8[:], F.Identity, ["e8", key], ["bm%d" % m], scale=c)
-            for w, c, key in ((T.wxa, cf[:, 11:12], "cf11"), (T.wxb, cf[:, 12:13], "cf12")):
-                act(w[:], T.wh1[:], F.Identity, ["wx", key], ["wxa", "wxb"], scale=c)
+        if t == 0:
+            late_matrices()
+            iota(T.lb[:, V:2 * V], [[0, V]], ["lz0"])
+        if not last:
+            step("lz")
+            iota(T.lb[:, 2 * V * (t + 1) + V:2 * V * (t + 2)], [[0, V]], ["lz%d" % (t + 1)])
         for k in range(4):
             c = slice(V * k, V * k + V)
+            low = T.xw[:, 0:wide].indirect(T.offa[:, 32 * k:32 * k + 32])
+            high = T.xw[:, 0:wide].indirect(T.offa[:, 128 + 32 * k:160 + 32 * k])
             step("lo%d" % k)
-            act(T.xl[:, c], T.xw[:, 0:wide].indirect(T.offa[:, 32 * k:32 * k + 32]), F.Identity, tables + ["offa0"], ["xl%d" % k],
-                scale=1.0 / 128)
-            step("hi%d" % k)
-            win = T.xw[:, 0:wide].indirect(T.offa[:, 128 + 32 * k:160 + 32 * k])
             if k == APART:
-                cpy(T.xp[:, c], win, tables + ["offa1"], ["xp%d" % k])
+                ts(T.xl[:, c], low, 1.0 / 128, None, A.mult, None, tables + ["offa0"], ["xl%d" % k])
             else:
-                tt(T.xp[:, c], win, T.xl[:, c], A.add, tables + ["offa1", "xl%d" % k], ["xp%d" % k])
-        parts = sorted([h + str(k) for h in ("Sl", "Sh") for k in range(4)], key=ORDER.index)
-        for name in parts:
+                act(T.xl[:, c], low, F.Identity, tables + ["offa0"], ["xl%d" % k], scale=1.0 / 128)
+            step("hi%d" % k)
+            if k == APART:
+                act(T.xp[:, c], high, F.Identity, tables + ["offa1"], ["xp%d" % k])
+            else:
+                tt(T.xp[:, c], high, T.xl[:, c], A.add, tables + ["offa1", "xl%d" % k], ["xp%d" % k])
+        loads = [8, False]
+        for name in [h + str(k) for h in ("Sl", "Sh") for k in range(4)]:
             step(name)
             k = int(name[2])
             w, x, key = (T.wi, T.xp, "xp") if name[1] == "h" else (T.w128 if k == APART else T.w127, T.xl, "xl")
             mms(0, LO, [(w[:], x[:, L * a:L * a + L]) for a in (2 * k, 2 * k + 1)], ["wi", "w127", "w128", key + str(k)],
-                name == parts[0], name == parts[-1])
+                group=loads)
+        step("ox")
+        ts(T.ox[:], ps[0][:, LO], -1288.0, T.thr[:, 0:1], A.add, A.is_gt, ["B0", "thr"], ["ox"])
         step("sb")
         move(WHO["sb"], T.sb[:], ps[0][:, LO], ["B0"], ["sb"])
-        step("ox")
-        ts(T.ox[:], T.sb[:], -1288.0, T.thr[:, 0:1], A.add, A.is_gt, ["sb", "thr"], ["ox"])
         step("u")
         mms(0, UP, [(T.wu[:], T.sb[:])], ["wu", "sb"])
         step("h16")
@@ -375,9 +408,18 @@ def rank_program(g, core, T, topo):
         mms(0, LO, [(T.wu[:], T.sb[:]), (T.wneg[:], T.h16[:])], ["wu", "sb", "wneg", "h16"])
         step("oh")
         ts(T.oh[:, LO], ps[0][:, LO], cf[:, 5:6], cf[:, 6:7], A.max, A.is_equal, ["B0", "cf5", "cf6"], ["oh0"])
-        cpy(T.oh[:, UP], T.oh[:, LO], ["oh0"], ["oh"])
-        for k in in_order("y", range(4)):
+        step("oh2")
+        move(WHO["oh"], T.oh[:, UP], T.oh[:, LO], ["oh0"], ["oh"])
+        for k in range(4):
             e, b, c = TILES[k], TILE_BANKS[k], slice(V * k, V * k + V)
+            if e == "m":
+                if k == 0:
+                    step("o%d" % k)
+                    for h in (LO, UP):
+                        mms(b, h, [(T.wi[:], T.ox[:])], ["wi", "ox"])
+                step("y%d" % k)
+                tt(T.yy[:, c], ps[b][:], T.xp[:, c], A.mult, ["B%d" % b, "xp%d" % k], ["yy%d" % k])
+                continue
             step("t%d" % k)
             mms(b, ALL, [(T.wi[:], T.xp[:, c])] + [(T.wi[:], T.xl[:, c])] * (k == APART), ["wi", "xp%d" % k, "xl%d" % k], True, False)
             step("o%d" % k)
@@ -385,38 +427,40 @@ def rank_program(g, core, T, topo):
                 mms(b, h, [(T.w16[:], T.ox[:])], ["w16", "ox"], False, h == UP)
             step("y%d" % k)
             relu(e, T.yy[:, c], ps[b][:], -16.0, ["B%d" % b], ["yy%d" % k])
-        for name, b, m in (("P", 3, 3), ("F", 4, 0)):
-            units = in_order(name, range(4))
-            for k in units:
+        burden = [5, False]
+        for name, b, m, sums in (("P", 3, 3, [4, False]), ("F", 4, 0, burden)):
+            for k in range(4):
                 step("%s%d" % (name, k))
-                mms(b, LO, [(into_row(m, a), T.yy[:, L * a:L * a + L]) for a in (2 * k, 2 * k + 1)], ["bm%d" % m, "yy%d" % k],
-                    k == units[0], b == 3 and k == units[-1])
+                mms(b, LO, [(into_row(m, a), T.yy[:, L * a:L * a + L]) for a in (2 * k, 2 * k + 1)],
+                    ["bm0_15", "bm3_15", "bm3_23", "yy%d" % k], group=sums)
         step("hb")
         act(T.hb[:], ps[3][:, LO], F.Identity, ["B3"], ["hb"], bias=129.0 - 63.5 / 128)
         step("Fh")
-        mms(4, LO, [(T.wh[:], T.hb[:])], ["wh", "hb"], False, True)
+        mms(4, LO, [(T.wh[:], T.hb[:])], ["wh", "hb"], group=burden)
         step("uT")
-        mms(0, TINY, [(into_row(2, r), T.sb[:, r:L:16]) for r in range(16)], ["bm2", "sb"])
-        step("bit")
+        mms(0, TINY, [(into_row(2, r), T.sb[:, r:L:16]) for r in range(16)], ["bm2_15", "sb"])
+        step("b0")
         ts(T.ri[:], ps[0][:, TINY], 1.0 / 64, None, A.add, None, ["B0"], ["ri"])
+        step("b1")
         tt(T.bt[:], ps[0][:, TINY], T.ri[:], A.is_lt, ["B0", "ri"], ["bt"])
+        step("b2")
         tt(T.bd[:], T.bt[:], T.dh[:], A.mult, ["bt", "dh"], ["bd"])
         step("Y0")
         mms(0, TINY, [(T.wi[:], T.h0[:]), (T.wi[:], T.bd[:])], ["wi", "h0", "bd"], True, False)
         step("n0")
-        mms(NB, TINY, [(into_row(0, r), T.hio[:, r:L:16]) for r in range(16)], ["bm0", "hio"], True, False)
+        mms(NB, TINY, [(into_row(0, r), T.hio[:, r:L:16]) for r in range(16)], ["bm0_15", "hio"], True, False)
         step("hot")
         act(T.hot[:], ps[4][:, LO], F.Sigmoid, ["B4", "ths"], ["hot"], bias=T.ths[:, t:t + 1], scale=65536.0)
         step("top")
-        mms(5, LO, [(T.wtop[:], T.hot[:])], ["wtop", "hot"], False, True)
+        mms(5, LO, [(T.wtop[:], T.hot[:])], ["wtop", "hot"], group=rise)
         step("hi")
         act(T.hi[:], ps[5][:, LO], F.Sign, ["B5"], ["hi"], bias=-HIGH)
         step("lv")
-        move(WHO["lv"], lanes, ps[5][:, LO], ["B5"], [sk[q]])
+        act(lanes, ps[5][:, LO], F.Identity, ["B5"], [sk[q]])
         step("sendb")
         send(-shift, T.lb[:, 2 * V * t:2 * V * t + V], T.lv[:, ALL], "ab%d" % t, "sb_", sk, "lb%d" % t)
         step("n1")
-        mms(NB, TINY, [(into_row(0, r), T.hi[:, r:L:16]) for r in range(16)], ["bm0", "hi"], False, True)
+        mms(NB, TINY, [(into_row(0, r), T.hi[:, r:L:16]) for r in range(16)], ["bm0_15", "hi"], False, True)
         step("ind")
         act(T.ind[:], ps[NB][:, TINY], F.Relu, ["B%d" % NB], ["ind", "acc"], bias=9.0 if WHO["hio"] == "v" else 1.0, scale=-1.0,
             acc=None if last else T.acc[:, 0:1])
@@ -428,71 +472,78 @@ def rank_program(g, core, T, topo):
         send(shift, got, idx, "ai%d" % t, "si", ["idx%d" % t], "li%d" % t)
         if not last:
             step("A")
-            mms(3, slice(0, 1), [(T.wa[:], T.acc[:, 0:1])], ["wa", "acc"])
+            mms(AB, slice(0, 1), [(T.wa[:], T.acc[:, 0:1])], ["wa", "acc"])
             step("f8")
-            act(T.f8[:, 0:1], ps[3][:, 0:1], F.Identity, ["B3"], ["f8"], bias=1288.0 - 3.5)
+            act(T.f8[:, 0:1], ps[AB][:, 0:1], F.Identity, ["B%d" % AB], ["f8"], bias=1288.0 - 3.5)
             step("thr")
-            ts(T.thr[:, 0:1], ps[3][:, 0:1], T.capf[:, 0:1], T.f8[:, 0:1], A.add, A.subtract, ["B3", "capf", "f8"], ["thr"])
+            ts(T.thr[:, 0:1], ps[AB][:, 0:1], T.capf[:, 0:1], T.f8[:, 0:1], A.add, A.subtract, ["B%d" % AB, "capf", "f8"], ["thr"])
         else:
             step("wr0")
-            scaled([("wwrap", -W / 2.0), ("wif", 1.0), ("wlog", 1.0 / (16.0 * LN2))])
             act(T.sg[:], T.pw[:, PAD:PAD + V], F.Sign, ["pw"], ["sg"], bias=0.5)
             step("wr1")
-            mms(3, ALL, [(T.wif[:], T.pw[:, PAD:PAD + V])], ["wif", "pw"], True, False)
-            mms(3, ALL, [(T.wwrap[:], T.sg[:])], ["wwrap", "sg"], False, True)
+            mms(AB, ALL, [(T.wif[:], T.pw[:, PAD:PAD + V])], ["wif", "pw"], True, False)
+            mms(AB, ALL, [(T.wwrap[:], T.sg[:])], ["wwrap", "sg"], False, True)
             step("wr2")
-            act(T.op[:, ALL], ps[3][:], F.Identity, ["B3"], ["op"], bias=W / 2.0)
+            act(T.op[:, ALL], ps[AB][:], F.Identity, ["B%d" % AB], ["op"], bias=W / 2.0)
         steps = ["stp", "se"] if t else ["stp"]
         for k, e in enumerate(STEPS):
             c = slice(V * k, V * k + V)
             win = T.sw[:, 0:wide].indirect(T.offa[:, 32 * k:32 * k + 32])
             step("z%d" % k)
-            if e == "v":
+            if e == "h":
+                for a in (2 * k, 2 * k + 1):
+                    tt(T.zg[:, L * a:L * a + L], T.sw[:, 0:wide].indirect(T.offa[:, 16 * a:16 * a + 16]), T.oh[:, LO], A.mult,
+                       steps + ["offa%d" % (k // 4), "oh0"], ["z%s%d" % ("hg"[a % 2], k)])
+            elif e == "v":
                 tt(T.zg[:, c], win, T.oh[:], A.mult, steps + ["offa%d" % (k // 4), "oh"], ["zg%d" % k])
             else:
-                b = 1 + k % 2
-                act(T.zu[:, c], win, F.Identity, steps + ["offa%d" % (k // 4)], ["zu%d" % k])
+                b, both = STEP_BANKS[k], [2, False]
+                move("v" if e == "u" else "s", T.zu[:, c], win, steps + ["offa%d" % (k // 4)], ["zu%d" % k])
+                step("x%d" % k)
+                mms(b, ALL, [(T.wi[:], T.zu[:, c])], ["wi", "zu%d" % k], group=both)
                 step("w%d" % k)
-                mms(b, ALL, [(T.w256[:], T.oh[:]), (T.wi[:], T.zu[:, c])], ["w256", "wi", "oh", "zu%d" % k])
+                mms(b, ALL, [(T.w256[:], T.oh[:])], ["w256", "oh"], group=both)
                 step("r%d" % k)
-                relu("s" if e == "s" else "v", T.zg[:, c], ps[b][:], -256.0, ["B%d" % b], ["zg%d" % k])
-        halves = in_order("tt", range(2))
-        for h in halves:
-            picks = in_order("", ["k%d" % k for k in range(4 * h, 4 * h + 4)] + ["hx%d" % h])
-            c, b = (LO, UP)[h], PICK_BANKS[h]
-            for name in picks:
-                step(name)
-                k = int(name[-1])
-                if name[0] == "k":
-                    mms(b, LO, [(into_row((1, 4)[h], a), T.zg[:, L * a:L * a + L]) for a in (2 * k, 2 * k + 1)],
-                        ["bm1", "bm4", "zg%d" % k], name == picks[0], name == picks[-1])
-                else:
-                    mms(b, LO, [((T.wxa, T.wxb)[h][:], T.hi[:])], ["wxa", "wxb", "hi"], name == picks[0], name == picks[-1])
+                relu("v" if e == "r" else "s", T.zg[:, c], ps[b][:], -256.0, ["B%d" % b], ["zg%d" % k])
+        join = [2 + last, False]
+        if last:
+            step("wp")
+            mms(7, LO, [(T.wif[:], places)], ["wif", "pw"], group=join)
+        for h in range(2):
+            c, b, picks = (LO, UP)[h], PICK_BANKS[h], [5, False]
+            for k in range(4 * h, 4 * h + 4):
+                step("k%d" % k)
+                mms(b, LO, [(into_row((1, 4)[h], a), T.zg[:, L * a:L * a + L]) for a in (2 * k, 2 * k + 1)],
+                    [("bm1_15", "bm4_15")[h], ("bm1_23", "bm4_7")[h], "zg%d" % k, "zh%d" % k], group=picks)
+            step("hx%d" % h)
+            mms(b, LO, [((T.wxa, T.wxb)[h][:], T.hi[:])], ["wxa", "wxb", "hi"], group=picks)
             step("tt%d" % h)
             relu(WHO["tt"][h], T.tt[:, c], ps[b][:, LO], -128.0, ["B%d" % b], ["tt%d" % h])
             step("j%d" % h)
-            mms(7, LO, [((T.wja, T.wjb)[h][:], T.tt[:, c])], ["wja", "wjb", "tt%d" % h], h == halves[0], h == halves[1])
+            mms(7, LO, [((T.wja, T.wjb)[h][:], T.tt[:, c])], ["wja", "wjb", "tt%d" % h], group=join)
         step("ch")
-        tt(T.ch[:], ps[7][:, LO], places, A.add, ["B7", "pw"], ["ch"])
-        child, ck = T.ch, "ch"
         if last:
-            ts(T.ck[:], T.ch[:], 0.0, float(W), A.is_lt, A.mult, ["ch"], ["ck"])
-            tt(T.cw[:], T.ch[:], T.ck[:], A.add, ["ch", "ck"], ["cw"])
-            child, ck = T.cw, "cw"
+            ts(T.ck[:], ps[7][:, LO], 0.0, float(W), A.is_lt, A.mult, ["B7"], ["ck"])
+            tt(T.ch[:], ps[7][:, LO], T.ck[:], A.add, ["B7", "ck"], ["ch"])
+        else:
+            tt(T.ch[:], ps[7][:, LO], places, A.add, ["B7", "pw"], ["ch"])
         step("sendm")
-        send(shift, T.lm[:, L * t:L * t + L], child[:], "am%d" % t, "sm", [ck], "lm%d" % t)
+        send(shift, T.lm[:, L * t:L * t + L], T.ch[:], "am%d" % t, "sm", ["ch"], "lm%d" % t)
+        if last:
+            decode(1, T.lv[:, ALL], sk, T.om[:, ALL], V)
         step("zero")
-        cpy(T.lv[:, 0:2 * V].indirect(got), zeros, ["li%d" % t, "lz0"], sk)
+        cpy((T.om if last else T.lv)[:, 0:2 * V].indirect(got), zeros, ["li%d" % t, "lz0"], ["om1"] if last else sk)
         step("sel")
         act(T.sel[:], T.lb[:, 2 * V * t:2 * V * (t + 1)].indirect(idx), F.Identity, ["lb%d" % t, "lz%d" % t, "idx%d" % t], ["sel"],
             scale=DOWN)
-        step("max")
-        tt(lanes, lanes, T.sel[:], A.max, [sk[q], "sel"], [sk[q]])
         if last:
-            decode(1 - q, 1)
-            decode(q, 2)
+            decode(2, T.sel[:], ["sel"], T.hb[:], L)
+            step("mx")
+            tt(T.om[:, q:V:2], T.om[:, q:V:2], T.hb[:], A.max, ["om1", "om2"], ["om1"])
         else:
-            climb(1 - q, CLIMB)
+            step("max")
+            tt(lanes, lanes, T.sel[:], A.max, [sk[q], "sel"], [sk[q]])
+            rise = climb(1 - q, CLIMB)
         step("put")
         if last:
             cpy(T.op[:, 0:2 * V].indirect(got), T.lm[:, L * t:L * t + L], ["li%d" % t, "lm%d" % t], ["op"])
@@ -500,7 +551,7 @@ def rank_program(g, core, T, topo):
             cpy(T.pw[:, PAD:PAD + 2 * V].indirect(got), T.lm[:, L * t:L * t + L], ["li%d" % t, "lm%d" % t], ["pw", "padb"])
 
     step("out")
-    dma("s", T.ymk[:], T.om[:, ALL], "o2", ["om0", "om1"], [])
+    dma("s", T.ymk[:], T.om[:, ALL], "o2", ["om1"], [])
     dma("y", T.ypl[:], T.op[:, ALL], "o1", ["op"], [])
     emit()
     for sem in ("sb_", "sm", "si", "cg", "cp_", "cs", "cv", "o1", "o2"):

import math
from concourse.mybir import AluOpType as A, ActivationFunctionType as F

W, V, L, RO = 1920, 512, 256, 5
WX = W + 255 * (RO - 1)
PAD = 32
F32, BF, F16, I32, U16 = "float32", "bfloat16", "float16", "int32", "uint16"


def _s(n, d):
    return ("sbuf", [128, n], d)


SCRATCH = {
    "xw": _s(WX, BF), "sw": _s(WX, BF), "pli": _s(V, I32), "sui": _s(V, I32), "mki": _s(V, BF),
    "hpi": _s(32, I32), "cpi": _s(8, I32), "thi": _s(8, I32),
    "io1": _s(16, F32), "iob": _s(128, F32), "w0": _s(128, BF), "pcol": _s(8, I32), "ci": _s(8, I32),
    "cf": _s(24, F32), "wi": _s(128, BF), "wif": _s(128, F32), "wim": _s(128, BF), "w128": _s(128, BF), "w256": _s(128, BF),
    "w512": _s(128, BF), "wneg": _s(128, BF), "w16": _s(128, BF), "w127": _s(128, BF), "wtop": _s(128, BF), "wwrap": _s(128, BF),
    "wlog": _s(128, F16), "wu": _s(128, BF), "wa": _s(128, F32), "wh": _s(128, BF),
    "wja": _s(128, BF), "wjb": _s(128, BF), "wxa": _s(128, BF), "wxb": _s(128, BF), "bm": _s(720, BF),
    "capf": _s(8, BF), "ths": _s(8, F32), "thr": _s(8, F32), "f8": _s(8, BF),
    "acc": _s(8, F32), "h0": _s(16, F16), "dh": _s(16, F32),
    "glist": _s(16, U16), "suu": _s(V, U16), "offa": _s(L, U16), "idx": _s(RO * 16, U16),
    "pw": _s(PAD + 2 * V, F32), "lv": _s(2 * V, BF), "enc": _s(V, F32),
    "tw": _s(544, F32), "xl": _s(2048, BF), "xp": _s(2048, F16), "mg": _s(4096, BF), "zg": _s(4096, BF), "zu": _s(4096, BF),
    "yy": _s(2048, F16), "sb": _s(L, BF), "ox": _s(L, BF), "h16": _s(L, F16), "oh": _s(V, BF), "hb": _s(L, BF), "hot": _s(L, BF),
    "hi": _s(L, BF), "hio": _s(L, BF), "ri": _s(16, I32), "bt": _s(16, BF), "bd": _s(16, F16), "ind": _s(16, BF),
    "tt": _s(V, F16), "ch": _s(L, F16), "ck": _s(L, F16), "cw": _s(L, F16), "sel": _s(L, BF),
    "lm": _s(RO * L, F16), "lb": _s(RO * 2 * V, BF), "li": _s(RO * 16, U16),
    "da": _s(3 * V, BF), "la": _s(3 * V, F16), "om": _s(2 * V, BF), "sg": _s(V, BF), "op": _s(2 * V, F32),
}
for _k in range(8):
    SCRATCH["ps%d" % _k] = ("psum", [128, 512], F32)

LOADS = ["hp", "pl", "xf", "mk", "su0", "su1", "cp", "th", "stp", "xe", "se"]
SEMAPHORES = (["cv", "cs", "cp_", "cg", "sb_", "sm", "si", "o1", "o2"] + ["l" + n for n in LOADS]
              + ["a%s%d" % (k, t) for k in "bim" for t in range(RO)])

LN2 = math.log(2.0)
DOWN = 2.0 ** -64
HIGH = 4.0
ROUND = 1.5 * 2.0 ** 23
APART = 3
CLIMB0 = [("s", 32), ("v", 32), ("s", 32), ("v", 32), ("s", 48), ("v", 48), ("s", 32)]
CLIMB = [("v", 16), ("s", 48), ("v", 64), ("s", 64), ("s", 64)]
TILES = "mmss"
TILE_BANKS, PICK_BANKS, NB = [1, 1, 2, 6], [6, 4], 7
STEP_BANKS, AB = [1, 2, 1, 2, 1, 2, 1, 2], 3
STEPS = "hvvvvsss"
WHO = {"sb": "v", "h16": "v", "lv": "v", "hio": "s", "tt": "sv", "oh": "s"}
ORDER = {
    "v": "tr al0 al1 lo3 hi0 hi1 hi2 c0< vb va ox sb y0 h16 y1 oh z0 z3 b0 z2 b1 b2 z1 da1 idx ve z4 vc tt1 thr ch da2 dc1 zero "
         "max dc2 mx vh su0 vd su1 a1 a3 pw a5 c2 put".split(),
    "s": "lo0 lo1 lo2 hi3 sa z6 y2 y3 z7 hb oh2 hot z5 hi lv r5 ind r6 r7 tt0 f8 se db1 sel wr0 a6 hio db2 wr2 a4 a0 a2 c1 c4 c3 "
         "out".split(),
    "p": "n0 q1< q3< q2< Sl0 Sl3 Sh0 Sl1 Sh1 Sl2 Sh3 Sh2 t3 t2 o0 o2 o3 u q0< P0 F0 m16 P2 P3 P1 F2 F1 F3 Fh x6 uT w5 top w6 x5 k0 "
         "n1 hx0 k2 Y0 Y1 x7 w7 k3 k1 k5 hx1 k6 k7 k4 j0 A wp j1 old db1 wr1 db2".split(),
    "g": "gb sendb sendi sendm lz".split(),
}


def rank_program(g, core, T, topo):
    rank = T.rank_of(core)
    if rank is None:
        return
    N = len(T.cores)
    Q = {"v": g.vector, "s": g.scalar, "p": g.tensor, "g": g, "y": g.sync}
    SEM = {"v": "cv", "s": "cs", "p": "cp_", "g": "cg"}
    cnt = {}
    known = {q: {} for q in Q}
    writer, readers = {}, {}
    ops = []
    now = [None, -1]

    def step(name):
        now[0] = name

    def place(q):
        order = ORDER.get("g" if q is None else q)
        if now[0] is None or order is None:
            return (now[1], -1)
        return (now[1] + 1, order.index(now[0] + "<")) if now[0] + "<" in order else (now[1], order.index(now[0]))

    def wait(q, tok):
        sem, n, clock = tok
        if (q == "p" and sem == "cp_") or known[q].get(sem, 0) >= n:
            return
        Q[q].wait_ge(T.sem[sem], n)
        known[q][sem] = n
        for s2, n2 in clock.items():
            if known[q].get(s2, 0) < n2:
                known[q][s2] = n2

    def record(q, kind, what, r, w):
        deps = set(writer[k] for k in r if k in writer)
        for k in r:
            if k[0] == "B":
                deps.update(i for i in readers.get(k, []) if ops[i][0] != q)
        for k in w:
            if k in writer:
                deps.add(writer[k])
            deps.update(readers.get(k, []))
        me = len(ops)
        ops.append((q, kind, what, place(q), sorted(deps)))
        for k in r:
            readers.setdefault(k, []).append(me)
        for k in w:
            writer[k] = me
            readers[k] = []

    def emit():
        after = [[] for _ in ops]
        for i, o in enumerate(ops):
            for d in o[4]:
                after[d].append(i)
        todo = {q: sorted((i for i, o in enumerate(ops) if o[0] == q), key=lambda i: (ops[i][3], i), reverse=True) for q in [None, *Q]}
        tok = {}
        while any(todo.values()):
            i = [l for l in todo.values() if l and all(d in tok for d in ops[l[-1]][4])][0].pop()
            q, kind, what, _, deps = ops[i]
            if kind == "arrival":
                tok[i] = what + ({},)
                continue
            best = {}
            for d in deps:
                tk = tok[d]
                if tk is not None and (tk[0] not in best or best[tk[0]][1] < tk[1]):
                    best[tk[0]] = tk
            for tk in best.values():
                wait(q, tk)
            if kind == "op":
                ins = what()
                if q == "p" and all(ops[j][0] == "p" for j in after[i]):
                    tok[i] = None
                    continue
                sem, n = SEM[q], 1
                ins.then_inc(T.sem[sem], 1)
            elif kind == "dma":
                sem, n = what[2], 16
                Q[q].dma_start(what[0], what[1]).then_inc(T.sem[sem], 16)
            else:
                sem, n = what[1], what[2]
                what[0]()
            cnt[sem] = cnt.get(sem, 0) + n
            tok[i] = (sem, cnt[sem], dict(known[q]))

    def op(q, call, r, w):
        record(q, "op", call, r, w)

    def dma(q, out, in_, sem, r, w):
        record(q, "dma", (out, in_, sem), r, w)

    def ts(out, in0, s1, s2, o0, o1, r, w):
        if o1 is None:
            op("v", lambda: g.vector.tensor_scalar(out, in0, s1, None, o0), r, w)
        else:
            op("v", lambda: g.vector.tensor_scalar(out, in0, s1, s2, o0, o1), r, w)

    def tt(out, in0, in1, o, r, w):
        op("v", lambda: g.vector.tensor_tensor(out, in0, in1, o), r, w)

    def cpy(out, in_, r, w):
        op("v", lambda: g.vector.tensor_copy(out, in_), r, w)

    def fill(ap, c, w):
        op("v", lambda: g.vector.memset(ap, c), [], w)

    def act(out, in_, f, r, w, bias=0.0, scale=1.0, acc=None):
        op("s", lambda: g.scalar.activation(out, in_, f, bias=bias, scale=scale, accum_out=acc), r, w)

    def move(e, out, in_, r, w):
        if e == "s":
            act(out, in_, F.Identity, r, w)
        else:
            cpy(out, in_, r, w)

    def relu(e, out, in_, bias, r, w):
        if e == "s":
            act(out, in_, F.Relu, r, w, bias=bias)
        else:
            ts(out, in_, bias, 0.0, A.add, A.max, r, w)

    def iota(out, pattern, w):
        op("g", lambda: g.iota(out, pattern, 0, 0, allow_small_or_imprecise_dtypes=True), [], w)

    def mms(bank, c, pairs, r, start=True, stop=True, group=None):
        out = ps[bank][:, c]

        def call():
            first, final = start, stop
            if group:
                first, final = not group[1], group[0] == 1
                group[0], group[1] = group[0] - 1, True
            return [g.tensor.matmul(out, a, b, first and k == 0, final and k == len(pairs) - 1) for k, (a, b) in enumerate(pairs)][-1]
        if group:
            op("p", call, r + ["B%d" % bank], [])
        else:
            op("p", call, r, ["B%d" % bank])

    def send(shift, out, in_, arr, loc, r, key):
        dst, src = T.cores[(rank + shift) % N], T.cores[(rank - shift) % N]
        rid, pid = topo.addr(dst, core)
        record("g", "send", (lambda: g.remote_dma(out, in_, T.sem[arr], T.sem[loc], pid, rid, topo.mask(core, dst)), loc,
                             len(topo.engines(core, dst))), r, ["sent" + key])
        record(None, "arrival", (arr, len(topo.engines(src, core))), ["sent" + key], [key])

    ps = [T["ps%d" % k] for k in range(8)]
    cf, ci = T.cf, T.ci
    LO, UP, ALL, TINY = slice(0, L), slice(L, V), slice(0, V), slice(0, 16)

    def into_row(m, a):
        return T.bm[:, 144 * m + 15 - a:144 * m + 143 - a]

    for qq, out, in_, name in (
            ("y", T.hpi[:], T.hp[:], "hp"), ("y", T.mki[:], T.mk[:], "mk"), ("y", T.sui[:, LO], T.su[:, LO], "su0"),
            ("y", T.sui[:, UP], T.su[:, UP], "su1"), ("y", T.pli[:], T.pl[:], "pl"), ("y", T.xw[:, 0:W], T.xf[:], "xf"),
            ("y", T.cpi[:, 0:1], T.cp[:], "cp"), ("y", T.thi[:, 0:5], T.th[:], "th"), ("y", T.sw[:, 0:W], T.stp[:], "stp"),
            ("y", T.xw[:, W:WX], T.xf[:, 0:WX - W], "xe"), ("y", T.sw[:, W:WX], T.stp[:, 0:WX - W], "se")):
        dma(qq, out, in_, "l" + name, [], [name])

    op("g", lambda: g.iota(T.pcol[:, 0:1], [[0, 1]], 0, 1), [], ["pcol"])
    iota(T.io1[:], [[1, 16]], ["io1"])
    iota(T.iob[:], [[1, 8], [0, 16]], ["iob"])
    zeros = T.lb[:, V:V + L]
    fill(T.w0[:], 0.0, ["w0"])
    fill(T.pw[:, 0:PAD], 0.0, ["pada"])
    ts(ci[:, 0:1], T.pcol[:, 0:1], 15, None, A.bitwise_and, None, ["pcol"], ["ci0"])
    ts(ci[:, 1:2], T.pcol[:, 0:1], 4, None, A.logical_shift_right, None, ["pcol"], ["ci1"])
    fill(T.pw[:, PAD + V:2 * PAD + V], 0.0, ["padb"])
    cpy(cf[:, 1:3], ci[:, 0:2], ["ci0", "ci1"], ["cf1"])
    tt(ci[:, 3:4], ci[:, 0:1], ci[:, 1:2], A.add, ["ci0", "ci1"], ["ci3"])
    ts(ci[:, 5:6], ci[:, 0:1], 2.0, 9.0, A.mult, A.add, ["ci0"], ["ci5"])
    ts(ci[:, 4:5], ci[:, 3:4], 1, None, A.bitwise_and, None, ["ci3"], ["ci4"])
    ts(ci[:, 6:7], ci[:, 5:6], 15, None, A.bitwise_and, None, ["ci5"], ["ci6"])

    def scaled(names):
        for name, c in names:
            act(T[name][:], T.wi[:], F.Identity, ["wi"], [name], scale=c)

    act(cf[:, 11:12], cf[:, 1:2], F.Sigmoid, ["cf1"], ["cf11"], bias=7.5 * 256, scale=-256.0)
    ts(cf[:, 4:5], cf[:, 1:2], 0.0, 100.0, A.is_equal, A.mult, ["cf1"], ["cf4"])
    ts(cf[:, 9:10], ci[:, 4:5], 17.0, cf[:, 1:2], A.mult, A.add, ["ci4", "cf1"], ["cf9"])
    ts(cf[:, 13:14], ci[:, 6:7], -8.0, None, A.add, None, ["ci6"], ["cf13"])
    ts(cf[:, 5:6], cf[:, 4:5], 1.0, -24576.0, A.max, A.add, ["cf4"], ["cf5"])
    ts(cf[:, 10:11], cf[:, 9:10], 16.0, None, A.mult, None, ["cf9"], ["cf10"])
    ts(cf[:, 7:8], cf[:, 1:2], 1.0 / 16, 1.0 / 32, A.mult, A.add, ["cf1"], ["cf7"])
    ts(cf[:, 6:7], cf[:, 4:5], cf[:, 1:2], -24576.0, A.add, A.add, ["cf1", "cf4"], ["cf6"])
    ts(T.glist[:], T.io1[:], cf[:, 10:11], None, A.add, None, ["io1", "cf10"], ["glist"])
    ts(T.wu[:], T.iob[:], cf[:, 2:3], cf[:, 13:14], A.is_equal, A.mult, ["iob", "cf1", "cf13"], ["wu"])

    def select(out, in_, pattern, cmp, c, base, mult, r, w):
        op("g", lambda: g.affine_select(out, in_, pattern, cmp, c, base, mult), r, w)

    def matrix(name, entries):
        for n, (c, k, m) in enumerate(entries):
            pattern, base = ([[-1, 128]], 0) if k is None else ([[-16, 8], [1000, 2], [-1, 8]], -8 * k - 1000 * m)
            select(T[name][:], T[name if n else "w0"][:], pattern, A.not_equal, c, base, 1, ["w0", name], [name])

    def rows(m, entries):
        cols = [T.bm[:, 144 * m + o:144 * m + o + 113:16] for o, c, lo, hi in entries]
        for col, (o, c, lo, hi) in zip(cols, entries):
            select(col, col, [[16, 8]], A.is_gt, c, lo, -1, ["bm"], ["bm%d_%d" % (m, o)])
        for col, (o, c, lo, hi) in zip(cols, entries):
            select(col, col, [[16, 8]], A.is_ge, 0.0, hi, -1, ["bm"], ["bm%d_%d" % (m, o)])

    matrix("wi", [(1.0, None, None)])
    matrix("wim", [(DOWN, None, None)])
    iota(T.bm[:], [[0, 720]], ["bm"])
    rows(0, [(15, 0.5, 0, 15)])
    for name, c in (("w127", 127.0), ("w128", 128.0), ("w16", 16.0), ("wneg", -1.0)):
        matrix(name, [(c, None, None)])
    rows(3, [(15, 1.0, 0, 7), (23, 1.0, 8, 15)])
    matrix("wh", [(-0.5, 0, 0), (-0.5, 1, 0), (1.0 / 256, 0, 1), (1.0 / 256, 1, 1)])

    def late_matrices():
        step("gb")
        matrix("w256", [(256.0, None, None)])
        rows(1, [(15, 1.0, 1, 15), (23, 1.0, 0, 0)])
        rows(4, [(15, 1.0, 1, 15), (7, 1.0, 0, 0)])
        matrix("w512", [(512.0, None, None)])
        matrix("wxa", [(128.0, 0, 0), (-128.0, 0, 1)])
        matrix("wxb", [(128.0, 1, 1), (-128.0, 1, 0)])
        matrix("wja", [(1.0, 0, 0), (1.0, 1, 0)])
        matrix("wjb", [(1.0, 0, 1), (1.0, 1, 1)])

    act(T.enc[:], T.mki[:], F.Sigmoid, ["mk"], ["enc"], bias=-125.0 * LN2, scale=8.0 * LN2)
    act(T.lv[:, ALL], T.enc[:], F.Square, ["enc"], ["lv0", "lv1"], scale=2.0 ** 63)
    for h in range(2):
        step("su%d" % h)
        cpy(T.suu[:, 128 * h:128 * h + 128], T.sui[:, L * h:L * h + L:2], ["su%d" % h], ["suu0%d" % h])

    def climb(q, calls, name="c"):
        lanes = T.lv[:, q:V:2]
        step("hio")
        if WHO["hio"] == "v":
            ts(T.hio[:], lanes, HIGH, 2.0, A.is_lt, A.mult, ["lv%d" % q], ["hio"])
        else:
            act(T.hio[:], lanes, F.Sign, ["lv%d" % q], ["hio"], bias=HIGH, scale=-1.0)
        step("old")
        mms(5, LO, [(T.wi[:], lanes)], ["wi", "lv%d" % q], True, False)
        o = 0
        for k, (e, n) in enumerate(calls):
            step("%s%d" % (name, k))
            move(e, T.mg[:, 16 * o:16 * (o + n)], T.lv[:, ALL].indirect(T.suu[:, L * q + o:L * q + o + n]),
                 ["lv0", "lv1", "suu%d%d" % (q, o // 128), "suu%d%d" % (q, (o + n - 1) // 128)],
                 ["mg%d" % j for j in range(o // 16, (o + n) // 16)])
            o += n
        rise = [5, True]
        for k in range(4):
            step("q%d" % k)
            mms(5, slice(64 * k, 64 * k + 64), [(T.wim[:], T.mg[:, 1024 * k + a:1024 * k + 1024:16]) for a in range(16)],
                ["wim"] + ["mg%d" % j for j in range(4 * k, 4 * k + 4)], group=rise)
        return rise

    def decode(k, src, keys, out, n):
        a, b = slice(2 * V * (k - 1), 2 * V * (k - 1) + n), slice(2 * V * (k - 1) + n, 2 * V * (k - 1) + 2 * n)
        step("da%d" % k)
        ts(T.da[:, a], src, 2.0 ** -124, 2.0 ** -4, A.max, A.min, keys, ["da%d" % k])
        ts(T.da[:, b], src, 2.0 ** -4, None, A.max, None, keys, ["db%d" % k])
        step("db%d" % k)
        act(T.la[:, a], T.da[:, a], F.Ln, ["da%d" % k], ["la%d" % k], scale=2.0 ** 64.25)
        act(T.la[:, b], T.da[:, b], F.Ln, ["db%d" % k], ["lc%d" % k], scale=2.0 ** -55.5)
        mms(k, slice(0, n), [(T.wlog[:], T.la[:, a]), (T.wlog[:], T.la[:, b])], ["wlog", "la%d" % k, "lc%d" % k])
        step("dc%d" % k)
        ts(out, ps[k][:, 0:n], ROUND + 7.0, -ROUND, A.add, A.add, ["B%d" % k], ["om%d" % k])

    step("vd")
    ts(T.bm[:, 303:416:16], T.io1[:, 0:8], cf[:, 2:3], cf[:, 7:8], A.is_equal, A.mult, ["io1", "cf1", "cf7", "bm"], ["bm2_15"])
    step("vh")
    cpy(T.h0[:], T.hpi[:, 0:16], ["hp"], ["h0"])
    tt(T.dh[:], T.hpi[:, 16:32], T.hpi[:, 0:16], A.subtract, ["hp"], ["dh"])
    rise = climb(0, CLIMB0, "a")
    step("pw")
    ts(T.pw[:, PAD:PAD + V], T.pli[:], -float(W), None, A.add, None, ["pl"], ["pw"])
    for t in range(RO):
        now[1] = t
        q, last = t % 2, t == RO - 1
        shift = 1 + t % (N - 1)
        wide = W + 255 * t
        tables = ["xf", "xe"] if t else ["xf"]
        places = T.pw[:, PAD + q:PAD + V:2]
        sk = ["lv0", "lv1"]
        lanes = T.lv[:, q:V:2]
        idx, got = T.idx[:, 16 * t:16 * t + 16], T.li[:, 16 * t:16 * t + 16]

        step("tr")
        op("v", lambda p=places: g.vector.transpose(T.tw[:, 0:256], p), ["pw"], ["tw1"])
        op("v", lambda p=T.pw[:, q:q + 576:2]: g.vector.transpose(T.tw[:, 256:544], p), ["pw", "pada", "padb"], ["tw2"])
        for h in range(2):
            step("al%d" % h)
            ts(T.offa[:, 128 * h:128 * h + 128], T.tw[:, 0:544].indirect(T.glist[:, 8 * h:8 * h + 8]), float(W), None, A.add, None,
               ["tw1", "tw2", "glist"], ["offa%d" % h])
        if t == 0:
            step("va")
            ts(T.thr[:, 0:1], T.cpi[:, 0:1], -1288.0, None, A.add, None, ["cp"], ["thr"])
            step("sa")
            act(cf[:, 14:15], cf[:, 11:12], F.Identity, ["cf11"], ["cf14"], bias=128.0 - 256 * 258, scale=65536.0 * 129 + 256 * 258)
            act(T.wtop[:], T.wi[:], F.Square, ["wi"], ["wtop"], scale=2.0 ** 58)
            step("se")
            scaled([("wif", 1.0), ("wwrap", -W / 2.0), ("wlog", 1.0 / (16.0 * LN2))])
            step("vb")
            ts(T.ths[:, 0:5], T.thi[:, 0:5], -256.0, cf[:, 14:15], A.mult, A.add, ["th", "cf14"], ["ths"])
            step("ve")
            ts(T.wa[:], T.iob[:], cf[:, 2:3], -1.0, A.is_equal, A.mult, ["iob", "cf1"], ["wa"])
            step("vc")
            cpy(T.capf[:, 0:1], T.cpi[:, 0:1], ["cp"], ["capf"])
            cpy(T.suu[:, UP], T.sui[:, 1:V:2], ["su0", "su1"], ["suu10", "suu11"])
        if t == 0:
            late_matrices()
            iota(T.lb[:, V:2 * V], [[0, V]], ["lz0"])
        if not last:
            step("lz")
            iota(T.lb[:, 2 * V * (t + 1) + V:2 * V * (t + 2)], [[0, V]], ["lz%d" % (t + 1)])
        for k in range(4):
            c = slice(V * k, V * k + V)
            low = T.xw[:, 0:wide].indirect(T.offa[:, 32 * k:32 * k + 32])
            high = T.xw[:, 0:wide].indirect(T.offa[:, 128 + 32 * k:160 + 32 * k])
            step("lo%d" % k)
            if k == APART:
                ts(T.xl[:, c], low, 1.0 / 128, None, A.mult, None, tables + ["offa0"], ["xl%d" % k])
            else:
                act(T.xl[:, c], low, F.Identity, tables + ["offa0"], ["xl%d" % k], scale=1.0 / 128)
            step("hi%d" % k)
            if k == APART:
                act(T.xp[:, c], high, F.Identity, tables + ["offa1"], ["xp%d" % k])
            else:
                tt(T.xp[:, c], high, T.xl[:, c], A.add, tables + ["offa1", "xl%d" % k], ["xp%d" % k])
        loads = [8, False]
        for name in [h + str(k) for h in ("Sl", "Sh") for k in range(4)]:
            step(name)
            k = int(name[2])
            w, x, key = (T.wi, T.xp, "xp") if name[1] == "h" else (T.w128 if k == APART else T.w127, T.xl, "xl")
            mms(0, LO, [(w[:], x[:, L * a:L * a + L]) for a in (2 * k, 2 * k + 1)], ["wi", "w127", "w128", key + str(k)],
                group=loads)
        step("ox")
        ts(T.ox[:], ps[0][:, LO], -1288.0, T.thr[:, 0:1], A.add, A.is_gt, ["B0", "thr"], ["ox"])
        step("sb")
        move(WHO["sb"], T.sb[:], ps[0][:, LO], ["B0"], ["sb"])
        step("u")
        mms(0, UP, [(T.wu[:], T.sb[:])], ["wu", "sb"])
        step("h16")
        if WHO["h16"] == "s":
            act(T.h16[:], ps[0][:, UP], F.Identity, ["B0"], ["h16"], bias=24576.0 - 7.5)
        else:
            ts(T.h16[:], ps[0][:, UP], 24576.0 - 7.5, None, A.add, None, ["B0"], ["h16"])
        step("m16")
        mms(0, LO, [(T.wu[:], T.sb[:]), (T.wneg[:], T.h16[:])], ["wu", "sb", "wneg", "h16"])
        step("oh")
        ts(T.oh[:, LO], ps[0][:, LO], cf[:, 5:6], cf[:, 6:7], A.max, A.is_equal, ["B0", "cf5", "cf6"], ["oh0"])
        step("oh2")
        move(WHO["oh"], T.oh[:, UP], T.oh[:, LO], ["oh0"], ["oh"])
        for k in range(4):
            e, b, c = TILES[k], TILE_BANKS[k], slice(V * k, V * k + V)
            if e == "m":
                if k == 0:
                    step("o%d" % k)
                    for h in (LO, UP):
                        mms(b, h, [(T.wi[:], T.ox[:])], ["wi", "ox"])
                step("y%d" % k)
                tt(T.yy[:, c], ps[b][:], T.xp[:, c], A.mult, ["B%d" % b, "xp%d" % k], ["yy%d" % k])
                continue
            step("t%d" % k)
            mms(b, ALL, [(T.wi[:], T.xp[:, c])] + [(T.wi[:], T.xl[:, c])] * (k == APART), ["wi", "xp%d" % k, "xl%d" % k], True, False)
            step("o%d" % k)
            for h in (LO, UP):
                mms(b, h, [(T.w16[:], T.ox[:])], ["w16", "ox"], False, h == UP)
            step("y%d" % k)
            relu(e, T.yy[:, c], ps[b][:], -16.0, ["B%d" % b], ["yy%d" % k])
        burden = [5, False]
        for name, b, m, sums in (("P", 3, 3, [4, False]), ("F", 4, 0, burden)):
            for k in range(4):
                step("%s%d" % (name, k))
                mms(b, LO, [(into_row(m, a), T.yy[:, L * a:L * a + L]) for a in (2 * k, 2 * k + 1)],
                    ["bm0_15", "bm3_15", "bm3_23", "yy%d" % k], group=sums)
        step("hb")
        act(T.hb[:], ps[3][:, LO], F.Identity, ["B3"], ["hb"], bias=129.0 - 63.5 / 128)
        step("Fh")
        mms(4, LO, [(T.wh[:], T.hb[:])], ["wh", "hb"], group=burden)
        step("uT")
        mms(0, TINY, [(into_row(2, r), T.sb[:, r:L:16]) for r in range(16)], ["bm2_15", "sb"])
        step("b0")
        ts(T.ri[:], ps[0][:, TINY], 1.0 / 64, None, A.add, None, ["B0"], ["ri"])
        step("b1")
        tt(T.bt[:], ps[0][:, TINY], T.ri[:], A.is_lt, ["B0", "ri"], ["bt"])
        step("b2")
        tt(T.bd[:], T.bt[:], T.dh[:], A.mult, ["bt", "dh"], ["bd"])
        step("Y0")
        mms(0, TINY, [(T.wi[:], T.h0[:]), (T.wi[:], T.bd[:])], ["wi", "h0", "bd"], True, False)
        step("n0")
        mms(NB, TINY, [(into_row(0, r), T.hio[:, r:L:16]) for r in range(16)], ["bm0_15", "hio"], True, False)
        step("hot")
        act(T.hot[:], ps[4][:, LO], F.Sigmoid, ["B4", "ths"], ["hot"], bias=T.ths[:, t:t + 1], scale=65536.0)
        step("top")
        mms(5, LO, [(T.wtop[:], T.hot[:])], ["wtop", "hot"], group=rise)
        step("hi")
        act(T.hi[:], ps[5][:, LO], F.Sign, ["B5"], ["hi"], bias=-HIGH)
        step("lv")
        act(lanes, ps[5][:, LO], F.Identity, ["B5"], [sk[q]])
        step("sendb")
        send(-shift, T.lb[:, 2 * V * t:2 * V * t + V], T.lv[:, ALL], "ab%d" % t, "sb_", sk, "lb%d" % t)
        step("n1")
        mms(NB, TINY, [(into_row(0, r), T.hi[:, r:L:16]) for r in range(16)], ["bm0_15", "hi"], False, True)
        step("ind")
        act(T.ind[:], ps[NB][:, TINY], F.Relu, ["B%d" % NB], ["ind", "acc"], bias=9.0 if WHO["hio"] == "v" else 1.0, scale=-1.0,
            acc=None if last else T.acc[:, 0:1])
        step("Y1")
        mms(0, TINY, [(T.w512[:], T.ind[:])], ["w512", "ind"], False, True)
        step("idx")
        cpy(idx, ps[0][:, TINY], ["B0"], ["idx%d" % t])
        step("sendi")
        send(shift, got, idx, "ai%d" % t, "si", ["idx%d" % t], "li%d" % t)
        if not last:
            step("A")
            mms(AB, slice(0, 1), [(T.wa[:], T.acc[:, 0:1])], ["wa", "acc"])
            step("f8")
            act(T.f8[:, 0:1], ps[AB][:, 0:1], F.Identity, ["B%d" % AB], ["f8"], bias=1288.0 - 3.5)
            step("thr")
            ts(T.thr[:, 0:1], ps[AB][:, 0:1], T.capf[:, 0:1], T.f8[:, 0:1], A.add, A.subtract, ["B%d" % AB, "capf", "f8"], ["thr"])
        else:
            step("wr0")
            act(T.sg[:], T.pw[:, PAD:PAD + V], F.Sign, ["pw"], ["sg"], bias=0.5)
            step("wr1")
            mms(AB, ALL, [(T.wif[:], T.pw[:, PAD:PAD + V])], ["wif", "pw"], True, False)
            mms(AB, ALL, [(T.wwrap[:], T.sg[:])], ["wwrap", "sg"], False, True)
            step("wr2")
            act(T.op[:, ALL], ps[AB][:], F.Identity, ["B%d" % AB], ["op"], bias=W / 2.0)
        steps = ["stp", "se"] if t else ["stp"]
        for k, e in enumerate(STEPS):
            c = slice(V * k, V * k + V)
            win = T.sw[:, 0:wide].indirect(T.offa[:, 32 * k:32 * k + 32])
            step("z%d" % k)
            if e == "h":
                for a in (2 * k, 2 * k + 1):
                    tt(T.zg[:, L * a:L * a + L], T.sw[:, 0:wide].indirect(T.offa[:, 16 * a:16 * a + 16]), T.oh[:, LO], A.mult,
                       steps + ["offa%d" % (k // 4), "oh0"], ["z%s%d" % ("hg"[a % 2], k)])
            elif e == "v":
                tt(T.zg[:, c], win, T.oh[:], A.mult, steps + ["offa%d" % (k // 4), "oh"], ["zg%d" % k])
            else:
                b, both = STEP_BANKS[k], [2, False]
                move("v" if e == "u" else "s", T.zu[:, c], win, steps + ["offa%d" % (k // 4)], ["zu%d" % k])
                step("x%d" % k)
                mms(b, ALL, [(T.wi[:], T.zu[:, c])], ["wi", "zu%d" % k], group=both)
                step("w%d" % k)
                mms(b, ALL, [(T.w256[:], T.oh[:])], ["w256", "oh"], group=both)
                step("r%d" % k)
                relu("v" if e == "r" else "s", T.zg[:, c], ps[b][:], -256.0, ["B%d" % b], ["zg%d" % k])
        join = [2 + last, False]
        if last:
            step("wp")
            mms(7, LO, [(T.wif[:], places)], ["wif", "pw"], group=join)
        for h in range(2):
            c, b, picks = (LO, UP)[h], PICK_BANKS[h], [5, False]
            for k in range(4 * h, 4 * h + 4):
                step("k%d" % k)
                mms(b, LO, [(into_row((1, 4)[h], a), T.zg[:, L * a:L * a + L]) for a in (2 * k, 2 * k + 1)],
                    [("bm1_15", "bm4_15")[h], ("bm1_23", "bm4_7")[h], "zg%d" % k, "zh%d" % k], group=picks)
            step("hx%d" % h)
            mms(b, LO, [((T.wxa, T.wxb)[h][:], T.hi[:])], ["wxa", "wxb", "hi"], group=picks)
            step("tt%d" % h)
            relu(WHO["tt"][h], T.tt[:, c], ps[b][:, LO], -128.0, ["B%d" % b], ["tt%d" % h])
            step("j%d" % h)
            mms(7, LO, [((T.wja, T.wjb)[h][:], T.tt[:, c])], ["wja", "wjb", "tt%d" % h], group=join)
        step("ch")
        if last:
            ts(T.ck[:], ps[7][:, LO], 0.0, float(W), A.is_lt, A.mult, ["B7"], ["ck"])
            tt(T.ch[:], ps[7][:, LO], T.ck[:], A.add, ["B7", "ck"], ["ch"])
        else:
            tt(T.ch[:], ps[7][:, LO], places, A.add, ["B7", "pw"], ["ch"])
        step("sendm")
        send(shift, T.lm[:, L * t:L * t + L], T.ch[:], "am%d" % t, "sm", ["ch"], "lm%d" % t)
        if last:
            decode(1, T.lv[:, ALL], sk, T.om[:, ALL], V)
        step("zero")
        cpy((T.om if last else T.lv)[:, 0:2 * V].indirect(got), zeros, ["li%d" % t, "lz0"], ["om1"] if last else sk)
        step("sel")
        act(T.sel[:], T.lb[:, 2 * V * t:2 * V * (t + 1)].indirect(idx), F.Identity, ["lb%d" % t, "lz%d" % t, "idx%d" % t], ["sel"],
            scale=DOWN)
        if last:
            decode(2, T.sel[:], ["sel"], T.hb[:], L)
            step("mx")
            tt(T.om[:, q:V:2], T.om[:, q:V:2], T.hb[:], A.max, ["om1", "om2"], ["om1"])
        else:
            step("max")
            tt(lanes, lanes, T.sel[:], A.max, [sk[q], "sel"], [sk[q]])
            rise = climb(1 - q, CLIMB)
        step("put")
        if last:
            cpy(T.op[:, 0:2 * V].indirect(got), T.lm[:, L * t:L * t + L], ["li%d" % t, "lm%d" % t], ["op"])
        else:
            cpy(T.pw[:, PAD:PAD + 2 * V].indirect(got), T.lm[:, L * t:L * t + L], ["li%d" % t, "lm%d" % t], ["pw", "padb"])

    step("out")
    dma("s", T.ymk[:], T.om[:, ALL], "o2", ["om1"], [])
    dma("y", T.ypl[:], T.op[:, ALL], "o1", ["op"], [])
    emit()
    for sem in ("sb_", "sm", "si", "cg", "cp_", "cs", "cv", "o1", "o2"):
        g.wait_ge(T.sem[sem], cnt[sem])
